import numpy as np, ml_dtypes
CORES = [6,15,38,47]
N = 4
import mx_ref
BF = ml_dtypes.bfloat16
def gentries(a):
    return np.ascontiguousarray(a.reshape(8, 16, -1).transpose(0, 2, 1)).reshape(8, -1)
def gtable(e):
    e = np.asarray(e); return np.ascontiguousarray(e.reshape(8, -1, 16).transpose(0, 2, 1)).reshape(128, -1).astype(np.int32)
def gcols(t, e):
    v = np.concatenate([t.reshape(8, 16, -1, 4), np.zeros((8, 16, 1, 4), BF)], axis=2)
    return np.ascontiguousarray(np.stack([v[g][:, e[g]] for g in range(8)])).reshape(128, -1)
def tile(rs):
    return np.stack(rs, axis=2).reshape(128, -1).astype(BF)
def cut(t, i, w=512):
    return t[:, w * i:w * i + w]
def pick(q, e):
    c = np.concatenate([q[0].reshape(128, -1, 4), np.zeros((128, 1, 4), np.uint8)], axis=1); s = np.concatenate([q[1], np.ones((16, 1), np.uint8)], axis=1)
    return (np.ascontiguousarray(c[:, e].reshape(128, -1)), np.ascontiguousarray(s[:, e]))
def join(*qs):
    return (np.concatenate([q[0] for q in qs], axis=1), np.concatenate([q[1] for q in qs], axis=1))
def put(q, e, v):
    c, s = q[0].reshape(128, -1, 4).copy(), q[1].copy(); c[:, e] = v[0].reshape(128, -1, 4); s[:, e] = v[1]
    return (c.reshape(128, -1), s)
def pk(c, s):
    return (np.ascontiguousarray(c), mx_ref.live(s))
def emit(q):
    return q[0], q[1]
def packed(v, rng):
    q = [mx_ref.quantize(np.ascontiguousarray(v[r])) for r in range(N)]
    return np.stack([a for a, b in q]), np.stack([mx_ref.plane(b, rng) for a, b in q])
def values_of_codes():
    e, c = np.zeros((128, 128, 4), np.float32), np.zeros((128, 2, 4), np.uint8)
    e[np.arange(128), np.arange(128), 0] = 1
    c[:127, :, 0] = np.arange(256).reshape(2, 128).T[:127]
    return mx_ref.matmul(mx_ref.quantize(e.reshape(128, 512).astype(BF)), (c.reshape(128, 8), np.full((16, 2), 127, np.uint8))).T.reshape(-1).astype(np.float64)
CODE_VALUE, SCALE_VALUE = values_of_codes(), 2.0 ** (np.arange(256) - 127.0)
def decode(q):
    return (CODE_VALUE[q[0]].reshape(16, 8, -1, 4) * SCALE_VALUE[q[1]][:, None, :, None] + 0.0).reshape(128, -1).astype(np.float32)
def f(rng, *shape):
    return mx_ref.flush((rng.standard_normal(shape, dtype=np.float32) * np.exp2(rng.integers(-2, 3, shape[:-1] + (1,)))).astype(BF))
def wide(rng, *shape, cols=0):
    v = rng.standard_normal(shape, dtype=np.float32) * np.exp2(rng.integers(-12, 13, shape)).astype(np.float32)
    if cols: v *= np.repeat(np.exp2(rng.integers(-cols, cols + 1, shape[:-2] + (1, shape[-1] // 4))) * (rng.random(shape[:-2] + (1, shape[-1] // 4)) > 0.0625), 4, axis=-1).astype(np.float32)
    return mx_ref.flush(v.astype(BF))
M, P, K, L, A, R = 352, 320, 64, 160, 128, 3
def order(p):
    return np.argsort(-(p + np.float32(0.0)), axis=1, kind="stable")
def counts(e):
    return np.stack([np.bincount(e[g], minlength=M) for g in range(8)])
def gput(t, e, v):
    a, b = t.reshape(8, 16, -1, 4).copy(), v.reshape(8, 16, -1, 4)
    for g in range(8): a[g][:, e[g]] = b[g]
    return a.reshape(128, -1)
def big(v):
    v = v.astype(np.float32)
    v[np.abs(v) < np.float32(2.0 ** -16)] = 0
    return v.astype(BF)
def stored(l):
    return np.stack([gtable(e) for e in l])
def numbers_of(rng):
    return {"m": big(f(rng, N, 128, 4 * M)), "u": np.array(f(rng, N, 128, 512)), "v": np.array(f(rng, N, 128, 512)), "pt": stored(rng.integers(0, M, (N, 8, P)))}
def weights(rng, on=range(16), w=None):
    w = big(f(rng, N, 128, 2048)) if w is None else w
    w = w.reshape(N, 8, 16, 4, 8, 16, 4)
    for i in range(16):
        if i not in on:
            w[:, :, i] = 0
            w[:, :, :, :, :, i] = 0
    c, p = packed(w.reshape(N, 128, 2048), rng)
    return {"wc": c, "ws": p}
def signs(rng):
    return np.stack([rng.permutation(8) % 2 * 2.0 - 1.0 for r in range(N)])
def digits(rng, a, k, e):
    d = numbers_of(rng)
    x = d["m"].astype(np.float32).reshape(N, 8, 16, M, 4)
    s = np.arange(M) // 2
    b = ((s[:, None] >> np.arange(8)) & 1) * 2.0 ** (np.arange(8) - 23.0)
    x[:, :, 0] = 0
    x[:, :, 0, :, 0] = a[:, :, None]
    x[:, :, 8] = b[:, :4]
    x[:, :, 9] = b[:, 4:]
    x[:, :, 10:] = rng.integers(4, 8, (N, 8, 6, M, 4)) * rng.choice([-1.0, 1.0], (N, 8, 6, M, 4)) * 2.0 ** -20
    u = d["u"].reshape(N, 128, 128, 4)
    for g in range(8):
        u[:, :, 16 * g:16 * g + 2] = 0
        for j in range(2):
            u[:, 16 * g, 16 * g + j, 0] = k.astype(np.float32).astype(BF)
            u[:, 16 * g + 8:16 * g + 10, 16 * g + j] = (k * e[:, g] ** j).astype(np.float32).astype(BF)[:, None, None]
    d["m"] = x.reshape(N, 128, 4 * M).astype(BF)
    return d
def setup_inputs(rng):
    return {**numbers_of(rng), **weights(rng)}
def setup_inputs_ties(rng):
    d = numbers_of(rng)
    o = rng.permutation(N)
    x = d["m"].reshape(N, 8, 16, M, 4)
    u = d["u"].reshape(N, 8, 16, 128, 4)
    def small(*s):
        return (rng.integers(4, 8, s) * rng.choice([-1.0, 1.0], s) * 2.0 ** -30).astype(np.float32).astype(BF)
    for r in range(N):
        k = rng.permutation(M) % 3
        if o[r] == 0: k = np.zeros(M, int)
        if o[r] == 1: k = np.full(M, 2)
        a = x[r][:, :8, :3].copy()
        if o[r] % 2 == 0:
            a = small(8, 8, 3, 4)
            for j in range(2): u[r][:, :8, j::16] = small(8, 8, 8, 4)
            for g in rng.permutation(8)[:4]:
                a[g] = 0
                a[g, 0, :2, 0] = (np.array([1.0, -1.0]) * 2.0 ** -30).astype(np.float32).astype(BF)
                u[r, g, :8, 16 * g:16 * g + 2] = 0
                u[r, g, 0, 16 * g:16 * g + 2, 0] = (rng.choice([-1.0, 1.0], 2) * 2.0 ** -30).astype(np.float32).astype(BF)
        a[:, :, 2] = 0
        x[r][:, :8] = a[:, :, k]
    for g in range(8):
        e = u[:, g, :8, 16 * g:16 * g + 2].copy()
        u[:, :, :, 16 * g:16 * g + 2] = 0
        u[:, g, :8, 16 * g:16 * g + 2] = e
    return {**d, **weights(rng, range(8, 16))}
def setup_inputs_near(rng):
    l = np.sort(rng.integers(0, M, (N, 8, P)), axis=2)
    k = np.where(rng.permutation(N) < N // 2, 2.0 ** -30, 1.0)
    d = digits(rng, signs(rng), k, signs(rng))
    x = d["m"].reshape(N, 8, 16, M, 4)
    for r in range(N):
        for g in rng.permutation(8)[:4]: x[r, g, 0, l[r, g, rng.integers(P)], 0] = 2.0 ** 30
    return {**d, "pt": stored(l), **weights(rng, range(1, 8))}
def setup_inputs_shares(rng):
    o = rng.permutation(N)
    l = np.argsort(rng.random((N, 8, M)), axis=2)[:, :, :P]
    e = np.ones((N, 8))
    for r in range(N):
        if o[r] % 4 == 0: e[r] = -1
        if o[r] % 4 == 1: l[r] = l[r][:, :1].copy()
        if o[r] % 4 == 3: l[r] = l[r][:, rng.permutation(P) // 2]
    return {**digits(rng, np.ones((N, 8)), np.ones(N), e), "pt": stored(l), **weights(rng, range(1, 8))}
def setup_inputs_huge(rng):
    d = numbers_of(rng)
    o = rng.permutation(N)
    l = rng.integers(0, M, (N, 8, P))
    x = 2.0 ** 30 * (0.9 + 0.1 * rng.random((N, 8, 16, M, 4)))
    x[:, :, 15] = 2.0 ** 26 * rng.uniform(-1, 1, (N, 8, M, 4))
    for r in range(N):
        if o[r] % 2:
            c, s = rng.permutation(M) % 2, rng.permutation(P) % 2
            x[r][:, :15] *= (2.0 * c - 1.0)[:, None]
            e = np.stack([np.flatnonzero(c == i) for i in range(2)])
            l[r] = e[s[None, :], rng.integers(0, M // 2, (8, P))]
    u = d["u"].reshape(N, 128, 128, 4)
    for j in range(2):
        u[:, :, j::16] = (2.0 ** 30 * (0.9 + 0.1 * rng.random((N, 128, 8, 4))) * signs(rng)[:, None, :, None]).astype(np.float32).astype(BF)
        u[:, 15::16, j::16] = 0
    d["m"] = big(x.reshape(N, 128, 4 * M))
    return {**d, "pt": stored(l), **weights(rng, [15], rng.choice([-1.0, 1.0], (N, 128, 2048)).astype(np.float32).astype(BF))}
def setup_inputs_spread(rng):
    d = setup_inputs(rng)
    d["m"] = big(wide(rng, N, 128, 4 * M, cols=6))
    return d
def check_inputs(d):
    b = []
    for k in ("m", "u", "v"):
        a = np.abs(d[k].astype(np.float32))
        if not (np.isfinite(a).all() and ((a == 0) | (a >= 2.0 ** -30) & (a <= 2.0 ** 30)).all()): b.append("a value of " + k)
    if ((d["pt"] < 0) | (d["pt"] >= M)).any(): b.append("an entry of pt")
    if (d["wc"] % 128 == 127).any(): b.append("a code of wc that is no number")
    return b
def reference(m, u, v, pt, wc, ws):
    qu = [mx_ref.quantize(u[r]) for r in range(N)]
    lay = [pk(wc[r], ws[r]) for r in range(N)]
    pages = [m[r] for r in range(N)]
    now = [gentries(pt[r]).astype(np.int64) for r in range(N)]
    for t in range(R):
        o, wr, sent = [], [], []
        for r in range(N):
            one = gcols(pages[r], now[r])
            s = mx_ref.matmul(qu[r], mx_ref.quantize(one))
            o.append(order(s[::16]))
            wr.append(order(s[1::16])[:, :A])
            sent.append(mx_ref.quantize(gcols(one, o[r][:, :K])))
        came = decode(join(*sent)).astype(BF)
        for r in range(N):
            h = now[r].copy()
            free = np.argsort(counts(np.take_along_axis(h, o[r][:, :P - L], axis=1)) > 0, axis=1, kind="stable")
            p = gput(pages[r], free[:, :K], cut(came, (r - 1) % N, 4 * K))
            np.put_along_axis(h, o[r][:, P - L:], free[:, np.arange(L) % K], axis=1)
            at = np.take_along_axis(h, wr[r], axis=1)
            more = np.take_along_axis(counts(h), at, axis=1) > 1
            z = gcols(p, at)
            q = mx_ref.quantize(z)
            made = tile([np.maximum(mx_ref.matmul(pick(lay[r], np.arange(128 * b, 128 * b + 128)), q), np.float32(0.0)) * np.float32(0.03125) + z[:, b::4].astype(np.float32) for b in range(4)])
            i = np.argsort(np.argsort(~more, axis=1, kind="stable"), axis=1)
            to = np.where(more, np.take_along_axis(free, K + i, axis=1), at)
            np.put_along_axis(h, wr[r], to, axis=1)
            pages[r] = gput(p, to, made)
            now[r] = h
    y, om = np.zeros((N, 128, P), np.float32), np.zeros((N, 8, P), np.float32)
    oc, osc = np.zeros((N, 128, 4 * P), np.uint8), np.zeros((N, 16, P), np.uint8)
    for r in range(N):
        q = mx_ref.quantize(gcols(pages[r], now[r]))
        y[r] = mx_ref.matmul(mx_ref.quantize(v[r]), q)
        om[r] = now[r]
        oc[r], osc[r] = emit(q)
    return {"y": y, "om": om, "oc": oc, "osc": osc}

@@ -1,0 +1,549 @@
+import numpy as np
+from concourse.mybir import dt, AluOpType, AxisListType, ActivationFunctionType
+
+A = AluOpType
+AF = ActivationFunctionType
+M, P, K, L, NA, R = 352, 320, 64, 160, 128, 3
+NV, MID = 9, 12
+ZV = [0, 0, 1]
+LAT, PASSES, SEED, NOISE = 100, 400, 1, 4000
+BIG = float(2 ** 20)
+HUGE = float(2 ** 25)
+FAR = 1e29
+F32, BF, I32, U16, X4, U8 = "float32", "bfloat16", "int32", "uint16", "float8_e4m3fn_x4", "uint8"
+
+
+def _sb(n, d):
+    return ("sbuf", [128, n], d)
+
+
+SCRATCH = {
+    "mt": _sb(4 * M, BF), "ut": _sb(512, BF), "vt": _sb(512, BF), "pti": _sb(20, I32),
+    "qw": _sb(512, X4), "sw": _sb(512, U8), "qu": _sb(128, X4), "su": _sb(128, U8),
+    "qu2": _sb(256, X4), "su2": _sb(256, U8), "qv": _sb(128, X4), "sv": _sb(128, U8),
+    "qf": _sb(P, X4), "sf": _sb(P, U8), "qz": _sb(128, X4), "sz": _sb(128, U8),
+    "qb": _sb(384, X4), "sb": _sb(384, U8), "qland": _sb(320, X4), "sland": _sb(320, U8),
+    "qe": _sb(512, X4), "se": _sb(512, U8), "et": _sb(2048, BF), "e1": _sb(2048, BF),
+    "pool0": _sb(2048, BF), "pool1": _sb(2048, BF), "pool2": _sb(2048, BF), "pool3": _sb(1280, BF),
+    "bt": _sb(512, BF), "zt": _sb(512, BF), "rel": _sb(4 * P, F32), "fk": _sb(2 * P, BF),
+    "uli": _sb(16, I32), "ul": _sb(16, U16), "yi": _sb(P, I32), "zi": _sb(P, I32), "nz": _sb(P, F32),
+    "ma": _sb(P, F32), "d0": _sb(P, F32), "d16": _sb(P, F32), "d4": _sb(128, F32), "x4": _sb(128, F32),
+    "nz4": _sb(128, F32), "ci": _sb(8, I32), "cf": _sb(8, F32), "x16": _sb(16, F32), "lt": _sb(16, F32),
+    "on16": _sb(192, BF), "rs16": _sb(P, BF), "ones": _sb(128, F32),
+    "j4": _sb(P + K, F32), "jw": _sb(22, F32), "jo": _sb(20, F32), "du": _sb(22, F32),
+    "tc": _sb(M, F32), "pg": _sb(M, F32), "i1": _sb(M, F32), "ht": _sb(464, F32), "cc": _sb(20, F32),
+    "hm": _sb(2 * P, F32), "hh": _sb(2 * P, F32), "fl": _sb(24 * 192, BF), "sc": _sb(24 * 192, BF),
+    "st0": _sb(14 * P, BF), "st1": _sb(14 * P, BF), "cs2": _sb(14 * 336, BF), "mk": _sb(65 * 14, BF),
+    "tr": _sb(2 * P, BF), "trs": _sb(2 * P, BF), "half": _sb(576, BF), "y2": _sb(576, I32), "up": _sb(20, F32),
+    "tt": _sb(28 * P, BF), "junk": _sb(8 * L, BF), "eq": _sb(2 * P, BF), "eqs": _sb(2 * P, BF),
+    "acc": _sb(80, F32), "ce": _sb(40, F32), "rk": _sb(40, F32), "ro": _sb(20, F32), "ra": _sb(20, F32),
+    "rou": _sb(20, U16), "rau": _sb(20, U16), "vz": _sb(P, F32),
+    "so": _sb(P, F32), "sa": _sb(P, F32), "sn": _sb(128, F32), "sn2": _sb(P, F32), "sn3": _sb(P, F32), "sn4": _sb(L, F32),
+    "bl": _sb(16, U16), "zl": _sb(32, U16), "fu": _sb(80, U16), "ou": _sb(10, U16), "au": _sb(8, U16),
+    "ptu": _sb(20, U16), "sm": _sb(160, F32), "smi": _sb(80, I32), "blu": _sb(20, U16), "to": _sb(L, F32),
+    "tou": _sb(10, U16), "cnt": _sb(8, F32), "cni": _sb(8, I32), "cn": _sb(24, I32), "twu": _sb(20, U16),
+    "fr": _sb(144, F32), "shu": _sb(22, U16), "totu": _sb(2, U16), "bs": _sb(24, F32), "posu": _sb(22, U16),
+    "sh": _sb(M, F32), "shj": _sb(P + K, F32), "tw": _sb(4 * 1024, F32), "more": _sb(128, F32),
+    "cs": _sb(128, F32), "ix": _sb(P, F32), "ixj": _sb(P, F32), "tl": _sb(20, U16), "yt": _sb(2 * P, F32),
+}
+for _b in range(8):
+    SCRATCH["ps%d" % _b] = ("psum", [128, 512], F32)
+NDMA = 16
+SEMAPHORES = ["sV", "sS", "sP", "sG", "sent", "arr0", "arr1", "arr2"] + ["d%d" % i for i in range(NDMA)]
+
+
+def v(name, a=0, b=None, s=1):
+    return ("view", name, a, SCRATCH[name][1][1] if b is None else b, s, None, None)
+
+
+def by(w, off):
+    return w[:5] + (off, w[6])
+
+
+def cast(w, d):
+    return w[:6] + (d,)
+
+
+def is_view(x):
+    return isinstance(x, tuple) and len(x) == 7 and x[0] == "view"
+
+
+def ap(T, x):
+    if not is_view(x):
+        return x
+    r = T[x[1]][:, x[2]:x[3]] if x[4] == 1 else T[x[1]][:, x[2]:x[3]:x[4]]
+    if x[6] is not None:
+        r = r.bitcast(x[6])
+    if x[5] is not None:
+        r = r.indirect(ap(T, x[5]))
+    return r
+
+
+def span(x):
+    if x[1].startswith("ps"):
+        return 1
+    return sum(1 << c for c in range(x[2], x[3], x[4]))
+
+
+def width(x):
+    return 16 * len(range(x[5][2], x[5][3])) if x[5] is not None else len(range(x[2], x[3], x[4]))
+
+
+def busy(o):
+    if o["dma"]:
+        return 100, 2500
+    vs = [x for x in o["a"] if is_view(x)]
+    n, k = width(vs[0]), o["k"]
+    if k == "remote":
+        return 700, 3500
+    if o["q"] == "G":
+        return 150 + 1.7 * n, LAT
+    if o["q"] == "P":
+        return 0.6 * (n + 16), LAT
+    if k == "quant":
+        return 12 + 0.88 * n, LAT
+    extra = 20 if "accum_out" in o["kw"] else 0
+    if vs[0][5] is not None:
+        return 50 + 3.15 * n, LAT
+    if any(x[5] is not None for x in vs):
+        return 60 + 1.25 * n + extra, LAT
+    if k == "tt" and not any(x[1].startswith("ps") for x in vs):
+        n = 2 * n
+    elif k != "tt" and o["q"] == "V" and all(SCRATCH[x[1]][2] in (BF, U16) for x in vs[:3]):
+        n = n / 2
+    return 20 + 0.83 * max(64, n) + extra, LAT
+
+
+def needs(ops):
+    seen, pre = {}, []
+    for i, o in enumerate(ops):
+        mine = [(x[1], span(x), False) for x in o["r"]] + [(x[1], span(x), True) for x in o["w"]]
+        s = set()
+        for name, m, wr in mine:
+            for j, m2, wr2 in seen.get(name, []):
+                if m & m2 and (wr or wr2 or (name.startswith("ps") and ops[j]["q"] != o["q"])):
+                    s.add(j)
+        pre.append(s)
+        for name, m, wr in mine:
+            seen.setdefault(name, []).append((i, m, wr))
+    return pre
+
+
+def order(ops):
+    n, pre = len(ops), needs(ops)
+    reach = [0] * n
+    for i in range(n):
+        if ops[i]["ext"]:
+            pre[i] |= set([j for j in range(i) if ops[j]["k"] == "remote"][-2:])
+        far = 0
+        for j in pre[i]:
+            far |= reach[j]
+        reach[i] = far | sum(1 << j for j in pre[i])
+        pre[i] = [j for j in sorted(pre[i]) if not far >> j & 1]
+    cost = [busy(o) for o in ops]
+    post = [[] for _ in ops]
+    for i in range(n):
+        for j in pre[i]:
+            post[j].append(i)
+    way = [0.0] * n
+    for i in range(n - 1, -1, -1):
+        way[i] = cost[i][0] + cost[i][1] + max([way[j] for j in post[i]] + [0.0])
+
+    def place(seq, before, back):
+        start, held = [0.0] * n, {}
+        for i in seq:
+            t, d = 0.0, cost[i][0]
+            for j in before[i]:
+                t = max(t, start[j] + cost[j][0] + cost[i if back else j][1])
+            row = held.setdefault(ops[i]["q"], [])
+            k = len(row)
+            while k > 0 and row[k - 1][1] > t:
+                k -= 1
+            while k < len(row) and row[k][0] < t + d:
+                if row[k][1] > t:
+                    t = row[k][1]
+                k += 1
+            row.insert(k, (t, t + d))
+            start[i] = t
+        return start
+
+    def legal(key):
+        top = list(key)
+        for i in range(n - 1, -1, -1):
+            for j in post[i]:
+                top[i] = max(top[i], top[j] + 1e-3)
+        return sorted(range(n), key=lambda i: (-top[i], i))
+
+    rnd = np.random.default_rng(SEED)
+    key, best = way, None
+    for p in range(PASSES):
+        fw = place(legal(key), pre, False)
+        end = max(fw[i] + cost[i][0] + cost[i][1] for i in range(n))
+        if best is None or end <= best[0]:
+            best = (end, fw)
+        if p % 2 == 1 and p > 6:
+            grp = {ops[int(i)]["run"]: NOISE * float(rnd.random()) for i in rnd.integers(0, n, 6)}
+            key = [-best[1][i] + grp.get(ops[i]["run"], 0.0) for i in range(n)]
+        else:
+            bw = place(legal([fw[i] + cost[i][0] + cost[i][1] for i in range(n)]), post, True)
+            key = [bw[i] + cost[i][0] for i in range(n)]
+    EST[0] = best[0]
+    return sorted(range(n), key=lambda i: (best[1][i], i))
+
+
+PLAN, EST = {}, [0.0]
+
+
+def emit(g, T, ops):
+    if "order" not in PLAN:
+        PLAN["order"] = order(ops)
+        PLAN["needs"] = needs([ops[i] for i in PLAN["order"]])
+    ops = [ops[i] for i in PLAN["order"]]
+    qs = {"V": g.vector, "S": g.scalar, "P": g.tensor, "G": g, "Y": g.sync}
+    need = set()
+    for o, pre in zip(ops, PLAN["needs"]):
+        deps = {}
+        for j in pre:
+            key = ("dma", j) if ops[j]["dma"] else ops[j]["q"]
+            deps[key] = max(deps.get(key, j), j)
+        o["deps"] = list(deps.values())
+        need |= set(o["deps"])
+    count = {q: 0 for q in qs}
+    known = {q: {} for q in qs}
+    nd = 0
+    last = {}
+    for i, o in enumerate(ops):
+        q, kn = o["q"], known[o["q"]]
+        for j in sorted(o["deps"], reverse=True):
+            s, n = ops[j]["sig"]
+            if kn.get(s, 0) < n:
+                qs[q].wait_ge(T.sem[s], n)
+                kn[s] = n
+                for s2, n2 in ops[j]["kn"].items():
+                    if kn.get(s2, 0) < n2:
+                        kn[s2] = n2
+        for s, n in o["ext"]:
+            if kn.get(s, 0) < n:
+                qs[q].wait_ge(T.sem[s], n)
+                kn[s] = n
+        o["kn"] = dict(kn)
+        ins = o["f"](qs[q])(*[ap(T, x) for x in o["a"]], **{k: ap(T, x) for k, x in o["kw"].items()})
+        if o["dma"]:
+            o["sig"] = ("d%d" % nd, 16)
+            nd += 1
+            ins.then_inc(T.sem[o["sig"][0]], 16)
+            last[o["sig"][0]] = 16
+        elif i in need:
+            count[q] += 1
+            o["sig"] = ("s" + q, count[q])
+            ins.then_inc(T.sem["s" + q], 1)
+            last["s" + q] = count[q]
+    return last
+
+
+def rank_program(g, core, T, topo):
+    rank = T.rank_of(core)
+    if rank is None:
+        return
+    nxt = T.cores[(rank + 1) % len(T.cores)]
+    ops = []
+    run = ["", 0]
+
+    def op(q, f, a, nout=1, kw=None, dma=False, ext=(), after=(), k=None):
+        kw = kw or {}
+        w = [x for x in a[:nout] if is_view(x)] + [x for n, x in kw.items() if n == "accum_out"]
+        r = [x for x in a[nout:] if is_view(x)] + [x for n, x in kw.items() if n != "accum_out" and is_view(x)] + list(after)
+        r += [x[5] for x in r + w if x[5] is not None]
+        name = w[0][1] if w else ""
+        if name != run[0]:
+            run[0], run[1] = name, len(ops)
+        ops.append({"q": q, "f": f, "a": a, "kw": kw, "r": r, "w": w, "dma": dma, "ext": ext, "k": k, "run": run[1]})
+
+    def ts(o, i, s1, op0, s2=None, op1=None):
+        op("V", lambda e: e.tensor_scalar, [o, i, s1, s2, op0] + ([] if op1 is None else [op1]))
+
+    def tt(o, a, b, f):
+        op("V", lambda e: e.tensor_tensor, [o, a, b, f], k="tt")
+
+    def cp(o, i, after=()):
+        op("V", lambda e: e.tensor_copy, [o, i], after=after)
+
+    def scan(o, a, b, init, op0, op1):
+        op("V", lambda e: e.tensor_tensor_scan, [o, a, b, init, op0, op1])
+
+    def ms(o, c):
+        op("V", lambda e: e.memset, [o, c])
+
+    def act(o, i, f=AF.Copy, **kw):
+        op("S", lambda e: e.activation, [o, i, f], kw=kw)
+
+    def quant(c, s, i):
+        op("V", lambda e: e.quantize_mx, [c, s, i], nout=2, k="quant")
+
+    def mm(b, n, wq, wsc, wa, xq, xs, xa, ext=()):
+        op("P", lambda e: e.matmul_mx, [v("ps%d" % b, 0, n), v(wq, wa, wa + 128), v(wsc, wa, wa + 128), v(xq, xa, xa + n), v(xs, xa, xa + n), True, True], ext=ext)
+
+    def iota(o, pat, base=0, cm=0):
+        kw = {} if SCRATCH[o[1]][2] == I32 else {"allow_small_or_imprecise_dtypes": True}
+        op("G", lambda e: e.iota, [o, pat, base, cm], kw=kw)
+
+    def dma(q, o, i, after=()):
+        op(q, lambda e: e.dma_start, [o, i], dma=True, after=after)
+
+    dma("Y", v("mt"), T.m[:])
+    dma("S", v("pti"), T.pt[:])
+    dma("S", v("ut"), T.u[:])
+    dma("Y", cast(v("qw"), dt.uint8), T.wc[:], after=[v("mt")])
+    dma("Y", v("sw"), T.ws[:], after=[v("mt")])
+    dma("Y", v("vt"), T.v[:], after=[v("mt")])
+
+    ns, hw = 20 - NV, 32 * MID + 32
+    iota(v("uli"), [[1, 2], [16, 8]])
+    iota(v("yi"), [[0, 20], [1, 16]], 128, -1)
+    iota(v("ci", 0, 1), [[0, 1]], 0, 1)
+    iota(v("x4"), [[0, 32], [1, 4]])
+    iota(v("x16"), [[1, 16]])
+    iota(v("jw"), [[16, 22]])
+    iota(v("cc"), [[16, 20]], 16)
+    iota(v("y2", 0, hw), [[0, MID + 1], [16, 2], [0, 16]], 0, 1)
+    iota(v("i1"), [[1, M]])
+    iota(v("pg"), [[1, 22], [22, 16]])
+    for k in (0, 1, 3):
+        iota(v("tw", 1024 * k + P, 1024 * k + 1024), [[0, 1024 - P]])
+    for r in range(R):
+        iota(v("pool%d" % r, 1536, 2048), [[0, 512]])
+    iota(v("j4"), [[4, P + K]])
+    iota(v("bt"), [[0, 512]])
+    iota(v("tc"), [[1, 16], [16, 22]])
+    iota(v("e1"), [[0, 2048]], 1)
+    op("G", lambda e: e.affine_select, [v("et"), v("e1"), [[-1, 4], [1, 512]], A.is_equal, 0.0, 0, -4])
+    for x in range(2):
+        ms(v("st%d" % x, 16 * (NV + 1) * ns, 16 * MID * ns), 0.0)
+        ms(v("rel", P * x + 128, P * x + P), 0.0)
+    ms(v("mk", 0, 65 * ns), 1.0)
+    ms(v("mk", 0, 65 * ns, ns), 0.0)
+    ms(v("cs2", 0, 16 * ns), 0.0)
+    ms(v("cs2", 16 * (MID + 1) * ns, 16 * (MID + 2) * ns), 0.0)
+    ms(v("acc"), 0.0)
+    ts(v("y2", 0, hw), v("y2", 0, hw), 16, A.bitwise_and)
+    ts(v("half", 0, hw), v("y2", 0, hw), 0.0, A.is_equal)
+    ms(v("d0"), FAR)
+    ms(v("on16"), 1.0)
+    ms(v("rs16"), 1.0)
+    ms(v("ones"), 1.0)
+    ms(v("shj", P, P + K), 1.0)
+    ms(v("ix", NA, P), 0.0)
+    ms(v("ht"), 0.0)
+    ms(v("d0", 0, P, 16), -2 * FAR)
+    ms(v("rs16", 0, P, 16), 0.0)
+    cp(v("ul"), v("uli"))
+    ts(v("zi"), v("yi"), 15, A.bitwise_and)
+    ts(v("nz"), v("zi"), 0.0, A.not_equal)
+    act(v("ma"), v("nz"), AF.Identity, scale=-FAR)
+    act(v("d16"), v("nz"), AF.Identity, scale=HUGE + BIG, bias=-HUGE)
+    ts(v("ci", 1, 2), v("ci", 0, 1), 15, A.bitwise_and)
+    ts(v("ci", 2, 3), v("ci", 0, 1), 2, A.logical_shift_right, 3, A.bitwise_and)
+    ts(v("ci", 3, 4), v("ci", 0, 1), 3, A.bitwise_and)
+    cp(v("cf", 0, 2), v("ci", 1, 3))
+    cp(v("cf", 4, 5), v("ci", 3, 4))
+    ts(v("cf", 2, 3), v("ci", 1, 2), -BIG, A.mult, 15 * BIG, A.add)
+    ts(v("cf", 5, 6), v("ci", 2, 3), -BIG, A.mult, 3 * BIG, A.add)
+    tt(v("cf", 3, 4), v("cf", 5, 6), v("cf", 4, 5), A.subtract)
+    ts(v("nz4"), v("x4"), v("cf", 1, 2), A.subtract, 0.0, A.not_equal)
+    ts(v("d4"), v("nz4"), HUGE + BIG, A.mult, -HUGE, A.add)
+    ts(v("lt"), v("x16"), v("cf", 0, 1), A.is_lt)
+    ts(v("du"), v("jw"), v("cf", 0, 1), A.add, float(M), A.add)
+    ts(v("jo"), v("jw", 0, 20), v("cf", 0, 1), A.add, float(3 * K), A.add)
+    for f in range(3):
+        ts(v("ht", 128 * f + 112, 128 * f + 128), v("zi", 0, 16), 0.0, A.is_equal, float(256 ** f), A.mult)
+    for t in range(4):
+        ts(v("fu", 20 * t, 20 * t + 20), v("pti"), 4.0, A.mult, float(t), A.add)
+    cp(v("ptu"), v("pti"))
+    quant(v("qu"), v("su"), v("ut"))
+    cp(cast(v("qu2"), dt.uint32), by(cast(v("qu"), dt.uint32), v("ul")))
+    act(v("su2"), by(v("su"), v("ul")))
+
+    def gather_f(r):
+        src = v("mt") if r == 0 else v("pool%d" % (r - 1))
+        for t in range(4):
+            if t < 2 and r > 0:
+                tt(v("pool%d" % r, t, 4 * P, 4), by(v("rel", P * t, P * t + P), v("rau")), v("fk", P * t, P * t + P), A.add)
+            else:
+                (cp if t < 2 else act)(v("pool%d" % r, t, 4 * P, 4), by(src, v("fu", 20 * t, 20 * t + 20)))
+        quant(v("qf"), v("sf"), v("pool%d" % r, 0, 4 * P))
+
+    def own(x, b):
+        for lo, hi in (((L, P), (0, L)) if x == 0 else ((0, P),)):
+            tt(v("hm", P * x + lo, P * x + hi), v("ps%d" % b, lo, hi), v("ma", lo, hi), A.add)
+            scan(v("hh", P * x + lo, P * x + hi), v("d0", lo, hi), v("hm", P * x + lo, P * x + hi), 0.0, A.min, A.max)
+
+    def col(x, c):
+        return v("hh", P * x + 16 * c + 15, P * x + 16 * c + 16)
+
+    def rank_v(x, b):
+        w = 16 * NV
+        for c in range(NV):
+            e, z = 16 * c + 16, w * (12 * x + c)
+            ts(v("fl", z, z + e), v("ps%d" % b, 0, e), col(x, c), A.is_ge)
+            if e < w:
+                ts(v("fl", z + e, z + w), v("ps%d" % b, e, w), col(x, c), A.is_gt)
+            scan(v("sc", z, z + w), v("on16", 0, w), v("fl", z, z + w), 0.0, A.mult, A.add)
+        tt(v("eq", P * x, P * x + P), v("ps%d" % b, 0, P), v("hh", P * x, P * x + P), A.is_equal)
+        scan(v("eqs", P * x, P * x + P), v("rs16"), v("eq", P * x, P * x + P), 0.0, A.mult, A.add)
+        z = 12 * w * x
+        tt(v("rk", 20 * x, 20 * x + NV), v("sc", z + w - 1, z + w * NV, w), v("eqs", P * x + 15, P * x + w, 16), A.subtract)
+        tt(v("ce", 20 * x + NV, 20 * x + 20), v("cc", NV, 20), v("eqs", P * x + w + 15, P * x + P, 16), A.subtract)
+
+    def rank_s(x, b):
+        for c in range(19, NV - 1, -1):
+            e, z = 16 * c + 16, P * (14 * x + c - NV)
+            w = P if c >= MID else e
+            act(v("tt", z, z + w), v("ps%d" % b, 0, w), AF.Sign, bias=col(x, c), scale=-1.0)
+            act(v("st%d" % x, c - NV, e * ns, ns), v("tt", z, z + e), AF.Relu, accum_out=v("acc", 40 * x + c, 40 * x + c + 1))
+            if e < w:
+                act(v("tt", z + e, z + w), v("tt", z + e, z + w), AF.Relu, scale=-1.0, accum_out=v("acc", 40 * x + 20 + c, 40 * x + 21 + c))
+
+    def rank_end(x):
+        st, w = "st%d" % x, 16 * MID
+        rf, ru = ("ro", "rou") if x == 0 else ("ra", "rau")
+        tt(v("rk", 20 * x + NV, 20 * x + 20), v("ce", 20 * x + NV, 20 * x + 20), v("acc", 40 * x + NV, 40 * x + 20), A.subtract)
+        tt(v(rf, MID, 20), v("rk", 20 * x + MID, 20 * x + 20), v("acc", 40 * x + 20 + MID, 40 * x + 40), A.add)
+        for k in range(MID - 1, NV - 1, -1):
+            s = ns - (k + 1 - NV)
+            scan(v("cs2", 16 * (k + 1) * ns, 16 * (k + 2) * ns), v("mk", s, s + 16 * ns), v(st, 16 * k * ns, 16 * (k + 1) * ns), 0.0, A.mult, A.add)
+        for k in range(0, NV, 4):
+            n = 16 * min(4, NV - k) * ns
+            scan(v("cs2", 16 * (k + 1) * ns, 16 * (k + 1) * ns + n), v("mk", 0, n), v(st, 16 * k * ns, 16 * k * ns + n), 0.0, A.mult, A.add)
+        op("V", lambda e: e.transpose, [v("tr", 0, w), v("cs2", 17 * ns - 1, (w + 16) * ns, ns)])
+        op("V", lambda e: e.transpose, [v("tr", w, 2 * w + 32), v("cs2", ns - 1, (w + 32) * ns, ns)])
+        scan(v("trs", 0, hw), v("tr", 0, hw), v("half", 0, hw), 0.0, A.add, A.mult)
+        tt(v("up", 0, MID, 2), v("trs", 15, w, 32), v("trs", w + 31, 2 * w, 32), A.add)
+        tt(v("up", 1, MID, 2), v("trs", w + 47, 2 * w + 32, 32), v("trs", 31, w, 32), A.add)
+        tt(v(rf, 0, MID), v("rk", 20 * x, 20 * x + MID), v("up", 0, MID), A.add)
+        cp(v(ru), v(rf))
+
+    def list4(row, n, out):
+        scan(v("sn", 0, n), v("d4", 0, n), v(row, 0, n), 0.0, A.add, A.max)
+        ts(v(out), v("sn", 3, n, 4), v("cf", 3, 4), A.subtract)
+
+    def list16(row, n, out, k, tmp):
+        scan(v(tmp, 0, n), v("d16", 0, n), row, 0.0, A.add, A.max)
+        ts(out, v(tmp, 15, n, 16), v("cf", 2, 3), A.subtract, k, A.mult)
+
+    def sources(r):
+        ts(v("smi", 0, 20), v("ro"), float(512 - L), A.add)
+        ts(v("smi", 20, 40), v("smi", 0, 20), 512 + K - 1, A.bitwise_and)
+        tt(v("sm", 20 * r, 20 * r + 20), v("smi", 20, 40), v("jo"), A.max)
+        ts(v("blu"), v("sm", 20 * r, 20 * r + 20), float(-3 * K), A.add)
+        ts(v("sm", 60, 80), v("sm", 20 * r, 20 * r + 20), float(P), A.add)
+
+    def next_lists():
+        ts(v("smi", 40, 60), v("ra"), float(1024 - NA), A.add)
+        ts(v("smi", 60, 80), v("smi", 40, 60), 1023, A.bitwise_and)
+        tt(v("sm", 80, 100), v("smi", 60, 80), v("sm", 60, 80), A.max)
+        for t in range(2, 4):
+            ts(v("fu", 20 * t, 20 * t + 20), v("sm", 80, 100), 4.0, A.mult, float(t - 2048), A.add)
+
+    def tables(r):
+        end = r == R - 1
+        k = 3 if end else r
+        list16(v("tw", 1024 * r, 1024 * r + P), P, v("twu"), 1.0, "sn3")
+        for i in range(8):
+            act(v("junk", L * i, L * i + L), by(v("ht", 16 * (7 - i), 16 * (7 - i) + M), v("tou")), accum_out=v("cnt", i, i + 1))
+        cp(v("cni"), v("cnt"))
+        ts(v("cn", 0, 8), v("cni"), 255, A.bitwise_and)
+        ts(v("cn", 8, 16), v("cni"), 8, A.logical_shift_right, 255, A.bitwise_and)
+        ts(v("cn", 16, 24), v("cni"), 16, A.logical_shift_right)
+        ts(v("shu"), v("cn", 0, 22), 1.0, A.is_gt)
+        act(v("sh"), by(v("i1"), v("shu")))
+        act(v("shj", 0, P), by(v("sh"), v("twu")))
+        ts(v("fr", 0, 22), v("cn", 0, 22), 0.0, A.is_equal)
+        ts(v("fr", 24, 46), v("cn", 0, 22), 1000.0, A.mult)
+        scan(v("fr", 48, 70), v("ones", 0, 22), v("fr", 0, 22), 0.0, A.mult, A.add)
+        tt(v("fr", 72, 94), v("fr", 24, 46), v("du"), A.min)
+        cp(v("totu", 0, 1), v("fr", 69, 70))
+        tt(v("bs", 0, 16), by(v("i1"), v("totu", 0, 1)), v("lt"), A.mult)
+        op("V", lambda e: e.tensor_reduce, [v("bs", 16, 17), v("bs", 0, 16), AxisListType.X, A.add])
+        ts(v("fr", 96, 118), v("fr", 48, 70), v("bs", 16, 17), A.add, -1.0, A.add)
+        tt(v("fr", 120, 142), v("fr", 96, 118), v("fr", 72, 94), A.max)
+        cp(v("posu"), v("fr", 120, 142))
+        if end:
+            act(v("tw", 3072, 3072 + P), by(v("pg"), v("twu")))
+        cp(by(v("tw", 1024 * k + P, 1024 * k + 1024), v("posu")), v("pg" if end else "i1"))
+        list16(v("sa", 0, NA), NA, v("au"), 0.25, "sn4")
+        act(v("more"), by(v("shj"), v("au")))
+        scan(v("cs"), v("ones"), v("more"), float(P + 4 * K - 1), A.mult, A.add)
+        tt(v("ix", 0, NA), v("cs"), v("more"), A.mult)
+        act(v("ixj"), by(v("ix"), v("rau")))
+        list16(v("ixj"), P, v("sm", 100, 120), 1.0, "sn2")
+        tt(v("sm", 120, 140), v("sm", 100, 120), v("sm", 20 * r, 20 * r + 20), A.max)
+        ts(v("tl"), v("sm", 120, 140), float(-3 * K), A.add)
+        act(v("yt", P, 2 * P) if end else v("tw", 1024 * (r + 1), 1024 * (r + 1) + P), by(v("tw", 1024 * k, 1024 * k + 1024), v("tl")))
+
+    rid, pid, _ = topo.addr(nxt)
+    mask = topo.mask(core, nxt)
+    neng = len(topo.engines(core, nxt))
+
+    gather_f(0)
+    act(v("tw", 0, P), by(v("tc"), v("ptu")))
+    quant(v("qland", 0, 128), v("sland", 0, 128), v("bt"))
+    quant(v("qe"), v("se"), v("et"))
+    quant(v("qv"), v("sv"), v("vt"))
+    for r in range(R):
+        pool = "pool%d" % r
+        for b in range(4):
+            mm(b, P, "qu2", "su2", 128 * (b // 2), "qf", "sf", 0)
+        own(0, 0)
+        own(1, 2)
+        rank_v(0, 0)
+        rank_s(0, 1)
+        rank_end(0)
+        cp(by(v("so"), v("rou")), v("j4", 0, P))
+        list4("so", K, "bl")
+        act(v("bt", 0, 256), by(v(pool, 0, 4 * P), v("bl")))
+        quant(v("qb", 128 * r, 128 * r + 128), v("sb", 128 * r, 128 * r + 128), v("bt"))
+        a, arr = 128 + K * r, T.sem["arr%d" % r]
+        op("G", lambda e: e.remote_dma, [ap(T, cast(v("qland", a, a + K), dt.uint8)), cast(v("qb", 128 * r, 128 * r + K), dt.uint8), arr, T.sem.sent, pid, rid, mask], k="remote")
+        op("G", lambda e: e.remote_dma, [ap(T, v("sland", a, a + K)), v("sb", 128 * r, 128 * r + K), arr, T.sem.sent, pid, rid, mask], k="remote")
+        sources(r)
+        act(v("vz"), by(v("j4"), v("blu")))
+        for b in range(4):
+            mm(4 + b, 128, "qe", "se", 128 * b, "qland", "sland", a - K, ext=[("arr%d" % r, 2 * neng)])
+            act(v(pool, 4 * P + b, 4 * P + 4 * K, 4), v("ps%d" % (4 + b), K, 128))
+        rank_v(1, 2)
+        rank_s(1, 3)
+        rank_end(1)
+        list16(v("so", 0, L), L, v("ou"), 0.25, "sn4")
+        act(v("to"), by(v("tw", 1024 * r, 1024 * r + P), v("ou")))
+        list16(v("to"), L, v("tou"), 1.0, "sn4")
+        cp(by(v("sa"), v("rau")), v("vz"), after=[v("tou")])
+        list4("sa", NA, "zl")
+        (cp if ZV[r] else act)(v("zt", 0, 256), by(v(pool, 0, 1536), v("zl", 0, 16)))
+        act(v("zt", 256, 512), by(v(pool, 0, 1536), v("zl", 16, 32)))
+        quant(v("qz"), v("sz"), v("zt"))
+        for t in range(2):
+            ts(v("fu", 20 * t, 20 * t + 20), v("sm", 20 * r, 20 * r + 20), 4.0, A.mult, float(t - 12 * K), A.add)
+            act(v("fk", P * t, P * t + P), by(v(pool, 0, 1536), v("fu", 20 * t, 20 * t + 20)))
+        for b in (2, 3, 0, 1):
+            mm(4 + b, 128, "qw", "sw", 128 * b, "qz", "sz", 0)
+            act(v("rel", P * b, P * b + 128), v("ps%d" % (4 + b), 0, 128), AF.Relu, scale=0.03125)
+            if b >= 2:
+                tt(v(pool, 1536 + b, 2048, 4), v("rel", P * b, P * b + 128), v("zt", b, 512, 4), A.add)
+        next_lists()
+        gather_f(r + 1)
+        tables(r)
+
+    for h in range(2):
+        mm(h, L, "qv", "sv", 0, "qf", "sf", L * h)
+    dma("Y", T.oc[:], cast(v("qf"), dt.uint8))
+    for k in range(4):
+        dma("Y", T.osc[4 * k:4 * k + 4, :], T.sf[32 * k:32 * k + 4, :], after=[v("sf")])
+    act(v("yt", L, P), v("ps1", 0, L))
+    cp(v("yt", 0, L), v("ps0", 0, L))
+    dma("S", T.y[:], v("yt", 0, P))
+    dma("S", T.om[:], T.yt[0:128:16, P:2 * P], after=[v("yt", P, 2 * P)])
+
+    last = emit(g, T, ops)
+    for s in sorted(last):
+        g.wait_ge(T.sem[s], last[s])
+    g.wait_ge(T.sem.sent, 2 * neng * R)

@@ -5,8 +5,9 @@ A = AluOpType
 AF = ActivationFunctionType
 M, P, K, L, NA, R = 352, 320, 64, 160, 128, 3
 NV, MID = 9, 12
-ZV = [0, 0, 1]
-LAT, PASSES, SEED, NOISE = 100, 400, 1, 4000
+CASES = [(120, (800, 3800), 1.0, 2.0), (150, (1200, 5000), 1.25, 3.15), (130, (1000, 4500), 1.6, 4.6)]
+WEIGHT = [0.3, 0.4, 0.3]
+PASSES, SEED, NOISE = 1600, 2, 1500
 BIG = float(2 ** 20)
 HUGE = float(2 ** 25)
 FAR = 1e29
@@ -29,12 +30,12 @@ SCRATCH = {
     "uli": _sb(16, I32), "ul": _sb(16, U16), "yi": _sb(P, I32), "zi": _sb(P, I32), "nz": _sb(P, F32),
     "ma": _sb(P, F32), "d0": _sb(P, F32), "d16": _sb(P, F32), "d4": _sb(128, F32), "x4": _sb(128, F32),
     "nz4": _sb(128, F32), "ci": _sb(8, I32), "cf": _sb(8, F32), "x16": _sb(16, F32), "lt": _sb(16, F32),
-    "on16": _sb(192, BF), "rs16": _sb(P, BF), "ones": _sb(128, F32),
+    "on16": _sb(576, BF), "rs16": _sb(P, BF), "ones": _sb(128, F32),
     "j4": _sb(P + K, F32), "jw": _sb(22, F32), "jo": _sb(20, F32), "du": _sb(22, F32),
     "tc": _sb(M, F32), "pg": _sb(M, F32), "i1": _sb(M, F32), "ht": _sb(464, F32), "cc": _sb(20, F32),
     "hm": _sb(2 * P, F32), "hh": _sb(2 * P, F32), "fl": _sb(24 * 192, BF), "sc": _sb(24 * 192, BF),
     "st0": _sb(14 * P, BF), "st1": _sb(14 * P, BF), "cs2": _sb(14 * 336, BF), "mk": _sb(65 * 14, BF),
-    "tr": _sb(2 * P, BF), "trs": _sb(2 * P, BF), "half": _sb(576, BF), "y2": _sb(576, I32), "up": _sb(20, F32),
+    "tr": _sb(2 * P, BF), "trs": _sb(2 * P, BF), "half": _sb(576, BF), "y2": _sb(576, I32), "up": _sb(40, F32),
     "tt": _sb(28 * P, BF), "junk": _sb(8 * L, BF), "eq": _sb(2 * P, BF), "eqs": _sb(2 * P, BF),
     "acc": _sb(80, F32), "ce": _sb(40, F32), "rk": _sb(40, F32), "ro": _sb(20, F32), "ra": _sb(20, F32),
     "rou": _sb(20, U16), "rau": _sb(20, U16), "vz": _sb(P, F32),
@@ -89,29 +90,29 @@ def width(x):
     return 16 * len(range(x[5][2], x[5][3])) if x[5] is not None else len(range(x[2], x[3], x[4]))
 
 
-def busy(o):
+def busy(o, lat, far, pick, put):
     if o["dma"]:
         return 100, 2500
     vs = [x for x in o["a"] if is_view(x)]
     n, k = width(vs[0]), o["k"]
     if k == "remote":
-        return 700, 3500
+        return far
     if o["q"] == "G":
-        return 150 + 1.7 * n, LAT
+        return 150 + 1.7 * n, lat
     if o["q"] == "P":
-        return 0.6 * (n + 16), LAT
+        return 0.6 * (n + 16), lat
     if k == "quant":
-        return 12 + 0.88 * n, LAT
+        return 12 + 0.88 * n, lat
     extra = 20 if "accum_out" in o["kw"] else 0
     if vs[0][5] is not None:
-        return 50 + 3.15 * n, LAT
+        return 50 + put * n, lat
     if any(x[5] is not None for x in vs):
-        return 60 + 1.25 * n + extra, LAT
+        return 60 + pick * n + extra, lat
     if k == "tt" and not any(x[1].startswith("ps") for x in vs):
         n = 2 * n
     elif k != "tt" and o["q"] == "V" and all(SCRATCH[x[1]][2] in (BF, U16) for x in vs[:3]):
         n = n / 2
-    return 20 + 0.83 * max(64, n) + extra, LAT
+    return 20 + 0.83 * max(64, n) + extra, lat
 
 
 def needs(ops):
@@ -140,7 +141,8 @@ def order(ops):
             far |= reach[j]
         reach[i] = far | sum(1 << j for j in pre[i])
         pre[i] = [j for j in sorted(pre[i]) if not far >> j & 1]
-    cost = [busy(o) for o in ops]
+    cases = [[busy(o, *c) for o in ops] for c in CASES]
+    cost = cases[1]
     post = [[] for _ in ops]
     for i in range(n):
         for j in pre[i]:
@@ -174,24 +176,35 @@ def order(ops):
                 top[i] = max(top[i], top[j] + 1e-3)
         return sorted(range(n), key=lambda i: (-top[i], i))
 
+    def length(seq, c):
+        done, free = [0.0] * n, {}
+        for i in seq:
+            t = free.get(ops[i]["q"], 0.0)
+            for j in pre[i]:
+                if done[j] > t:
+                    t = done[j]
+            free[ops[i]["q"]] = t + c[i][0]
+            done[i] = t + c[i][0] + c[i][1]
+        return max(done)
+
     rnd = np.random.default_rng(SEED)
     key, best = way, None
     for p in range(PASSES):
         fw = place(legal(key), pre, False)
-        end = max(fw[i] + cost[i][0] + cost[i][1] for i in range(n))
+        seq = sorted(range(n), key=lambda i: (fw[i], i))
+        end = sum(length(seq, c) * w for c, w in zip(cases, WEIGHT))
         if best is None or end <= best[0]:
-            best = (end, fw)
+            best = (end, fw, seq)
         if p % 2 == 1 and p > 6:
             grp = {ops[int(i)]["run"]: NOISE * float(rnd.random()) for i in rnd.integers(0, n, 6)}
             key = [-best[1][i] + grp.get(ops[i]["run"], 0.0) for i in range(n)]
         else:
             bw = place(legal([fw[i] + cost[i][0] + cost[i][1] for i in range(n)]), post, True)
             key = [bw[i] + cost[i][0] for i in range(n)]
-    EST[0] = best[0]
-    return sorted(range(n), key=lambda i: (best[1][i], i))
+    return best[2]
 
 
-PLAN, EST = {}, [0.0]
+PLAN = {}
 
 
 def emit(g, T, ops):
@@ -290,6 +303,11 @@ def rank_program(g, core, T, topo):
     def dma(q, o, i, after=()):
         op(q, lambda e: e.dma_start, [o, i], dma=True, after=after)
 
+    def fill(name, a, b, c):
+        for lo in range(a, b, 512):
+            hi = min(b, lo + 512)
+            act(v(name, lo, hi), v("bt", 0, hi - lo), AF.Identity, bias=c)
+
     dma("Y", v("mt"), T.m[:])
     dma("S", v("pti"), T.pt[:])
     dma("S", v("ut"), T.u[:])
@@ -298,6 +316,7 @@ def rank_program(g, core, T, topo):
     dma("Y", v("vt"), T.v[:], after=[v("mt")])
 
     ns, hw = 20 - NV, 32 * MID + 32
+    ms(v("bt"), 0.0)
     iota(v("uli"), [[1, 2], [16, 8]])
     iota(v("yi"), [[0, 20], [1, 16]], 128, -1)
     iota(v("ci", 0, 1), [[0, 1]], 0, 1)
@@ -313,27 +332,27 @@ def rank_program(g, core, T, topo):
     for r in range(R):
         iota(v("pool%d" % r, 1536, 2048), [[0, 512]])
     iota(v("j4"), [[4, P + K]])
-    iota(v("bt"), [[0, 512]])
     iota(v("tc"), [[1, 16], [16, 22]])
     iota(v("e1"), [[0, 2048]], 1)
     op("G", lambda e: e.affine_select, [v("et"), v("e1"), [[-1, 4], [1, 512]], A.is_equal, 0.0, 0, -4])
     for x in range(2):
-        ms(v("st%d" % x, 16 * (NV + 1) * ns, 16 * MID * ns), 0.0)
-        ms(v("rel", P * x + 128, P * x + P), 0.0)
-    ms(v("mk", 0, 65 * ns), 1.0)
+        fill("st%d" % x, 16 * (NV + 1) * ns, 16 * MID * ns, 0.0)
+        fill("rel", P * x + 128, P * x + P, 0.0)
+    fill("mk", 0, 65 * ns, 1.0)
     ms(v("mk", 0, 65 * ns, ns), 0.0)
-    ms(v("cs2", 0, 16 * ns), 0.0)
-    ms(v("cs2", 16 * (MID + 1) * ns, 16 * (MID + 2) * ns), 0.0)
-    ms(v("acc"), 0.0)
+    fill("cs2", 0, 16 * ns, 0.0)
+    fill("cs2", 16 * (MID + 1) * ns, 16 * (MID + 2) * ns, 0.0)
+    fill("up", 0, 40, 0.0)
     ts(v("y2", 0, hw), v("y2", 0, hw), 16, A.bitwise_and)
     ts(v("half", 0, hw), v("y2", 0, hw), 0.0, A.is_equal)
-    ms(v("d0"), FAR)
-    ms(v("on16"), 1.0)
-    ms(v("rs16"), 1.0)
-    ms(v("ones"), 1.0)
-    ms(v("shj", P, P + K), 1.0)
-    ms(v("ix", NA, P), 0.0)
-    ms(v("ht"), 0.0)
+    fill("on16", 0, 48 * NV, 1.0)
+    ms(v("on16", 0, 48 * NV, 16 * NV), 0.0)
+    fill("rs16", 0, P, 1.0)
+    fill("ones", 0, 128, 1.0)
+    fill("shj", P, P + K, 1.0)
+    fill("ix", NA, P, 0.0)
+    fill("ht", 0, 464, 0.0)
+    fill("d0", 0, P, FAR)
     ms(v("d0", 0, P, 16), -2 * FAR)
     ms(v("rs16", 0, P, 16), 0.0)
     cp(v("ul"), v("uli"))
@@ -350,7 +369,7 @@ def rank_program(g, core, T, topo):
     ts(v("cf", 5, 6), v("ci", 2, 3), -BIG, A.mult, 3 * BIG, A.add)
     tt(v("cf", 3, 4), v("cf", 5, 6), v("cf", 4, 5), A.subtract)
     ts(v("nz4"), v("x4"), v("cf", 1, 2), A.subtract, 0.0, A.not_equal)
-    ts(v("d4"), v("nz4"), HUGE + BIG, A.mult, -HUGE, A.add)
+    act(v("d4"), v("nz4"), AF.Identity, scale=HUGE + BIG, bias=-HUGE)
     ts(v("lt"), v("x16"), v("cf", 0, 1), A.is_lt)
     ts(v("du"), v("jw"), v("cf", 0, 1), A.add, float(M), A.add)
     ts(v("jo"), v("jw", 0, 20), v("cf", 0, 1), A.add, float(3 * K), A.add)
@@ -387,7 +406,9 @@ def rank_program(g, core, T, topo):
             ts(v("fl", z, z + e), v("ps%d" % b, 0, e), col(x, c), A.is_ge)
             if e < w:
                 ts(v("fl", z + e, z + w), v("ps%d" % b, e, w), col(x, c), A.is_gt)
-            scan(v("sc", z, z + w), v("on16", 0, w), v("fl", z, z + w), 0.0, A.mult, A.add)
+            if c % 3 == 2 or c == NV - 1:
+                n = w * (c % 3 + 1)
+                scan(v("sc", z + w - n, z + w), v("on16", 0, n), v("fl", z + w - n, z + w), 0.0, A.mult, A.add)
         tt(v("eq", P * x, P * x + P), v("ps%d" % b, 0, P), v("hh", P * x, P * x + P), A.is_equal)
         scan(v("eqs", P * x, P * x + P), v("rs16"), v("eq", P * x, P * x + P), 0.0, A.mult, A.add)
         z = 12 * w * x
@@ -401,13 +422,12 @@ def rank_program(g, core, T, topo):
             act(v("tt", z, z + w), v("ps%d" % b, 0, w), AF.Sign, bias=col(x, c), scale=-1.0)
             act(v("st%d" % x, c - NV, e * ns, ns), v("tt", z, z + e), AF.Relu, accum_out=v("acc", 40 * x + c, 40 * x + c + 1))
             if e < w:
-                act(v("tt", z + e, z + w), v("tt", z + e, z + w), AF.Relu, scale=-1.0, accum_out=v("acc", 40 * x + 20 + c, 40 * x + 21 + c))
+                act(v("tt", z + e, z + w), v("tt", z + e, z + w), AF.Relu, scale=-1.0, accum_out=v("up", 20 * x + c, 20 * x + c + 1))
 
     def rank_end(x):
         st, w = "st%d" % x, 16 * MID
         rf, ru = ("ro", "rou") if x == 0 else ("ra", "rau")
         tt(v("rk", 20 * x + NV, 20 * x + 20), v("ce", 20 * x + NV, 20 * x + 20), v("acc", 40 * x + NV, 40 * x + 20), A.subtract)
-        tt(v(rf, MID, 20), v("rk", 20 * x + MID, 20 * x + 20), v("acc", 40 * x + 20 + MID, 40 * x + 40), A.add)
         for k in range(MID - 1, NV - 1, -1):
             s = ns - (k + 1 - NV)
             scan(v("cs2", 16 * (k + 1) * ns, 16 * (k + 2) * ns), v("mk", s, s + 16 * ns), v(st, 16 * k * ns, 16 * (k + 1) * ns), 0.0, A.mult, A.add)
@@ -417,9 +437,9 @@ def rank_program(g, core, T, topo):
         op("V", lambda e: e.transpose, [v("tr", 0, w), v("cs2", 17 * ns - 1, (w + 16) * ns, ns)])
         op("V", lambda e: e.transpose, [v("tr", w, 2 * w + 32), v("cs2", ns - 1, (w + 32) * ns, ns)])
         scan(v("trs", 0, hw), v("tr", 0, hw), v("half", 0, hw), 0.0, A.add, A.mult)
-        tt(v("up", 0, MID, 2), v("trs", 15, w, 32), v("trs", w + 31, 2 * w, 32), A.add)
-        tt(v("up", 1, MID, 2), v("trs", w + 47, 2 * w + 32, 32), v("trs", 31, w, 32), A.add)
-        tt(v(rf, 0, MID), v("rk", 20 * x, 20 * x + MID), v("up", 0, MID), A.add)
+        tt(v("up", 20 * x, 20 * x + MID, 2), v("trs", 15, w, 32), v("trs", w + 31, 2 * w, 32), A.add)
+        tt(v("up", 20 * x + 1, 20 * x + MID, 2), v("trs", w + 47, 2 * w + 32, 32), v("trs", 31, w, 32), A.add)
+        tt(v(rf), v("rk", 20 * x, 20 * x + 20), v("up", 20 * x, 20 * x + 20), A.add)
         cp(v(ru), v(rf))
 
     def list4(row, n, out):
@@ -518,7 +538,7 @@ def rank_program(g, core, T, topo):
         list16(v("to"), L, v("tou"), 1.0, "sn4")
         cp(by(v("sa"), v("rau")), v("vz"), after=[v("tou")])
         list4("sa", NA, "zl")
-        (cp if ZV[r] else act)(v("zt", 0, 256), by(v(pool, 0, 1536), v("zl", 0, 16)))
+        cp(v("zt", 0, 256), by(v(pool, 0, 1536), v("zl", 0, 16)))
         act(v("zt", 256, 512), by(v(pool, 0, 1536), v("zl", 16, 32)))
         quant(v("qz"), v("sz"), v("zt"))
         for t in range(2):

@@ -4,10 +4,20 @@ from concourse.mybir import dt, AluOpType, AxisListType, ActivationFunctionType
 A = AluOpType
 AF = ActivationFunctionType
 M, P, K, L, NA, R = 352, 320, 64, 160, 128, 3
-NV, MID = 9, 12
-CASES = [(120, (800, 3800), 1.0, 2.0), (150, (1200, 5000), 1.25, 3.15), (130, (1000, 4500), 1.6, 4.6)]
+HC = 704
+PW = HC + NA
+FW, CW = 920, 1008
+TW = 1600
+V_LO = [(7, 8, 9), ()]
+V_UP = [(6, 7, 8), (7, 8)]
+CHUNKS = [0, 252, 504, 756, FW]
+PIECES = [0, 504, 756, FW]
+F_V = [(0, 1), (3,), (3,), (2, 3)]
+Z_V = 1
+NFL = 1
+CASES = [(120, (500, 2000), 1.0, 2.0), (150, (800, 3000), 1.25, 3.15), (130, (1000, 4500), 1.6, 4.6)]
 WEIGHT = [0.3, 0.4, 0.3]
-PASSES, SEED, NOISE = 1600, 2, 1500
+PASSES, SEED, NOISE = 3000, 2, 800
 BIG = float(2 ** 20)
 HUGE = float(2 ** 25)
 FAR = 1e29
@@ -19,33 +29,31 @@ def _sb(n, d):
 
 
 SCRATCH = {
-    "mt": _sb(4 * M, BF), "ut": _sb(512, BF), "vt": _sb(512, BF), "pti": _sb(20, I32),
+    "pool": _sb(4 * (R * (P + K) + PW), BF), "ut": _sb(512, BF), "vt": _sb(512, BF), "pti": _sb(20, I32),
     "qw": _sb(512, X4), "sw": _sb(512, U8), "qu": _sb(128, X4), "su": _sb(128, U8),
     "qu2": _sb(256, X4), "su2": _sb(256, U8), "qv": _sb(128, X4), "sv": _sb(128, U8),
     "qf": _sb(P, X4), "sf": _sb(P, U8), "qz": _sb(128, X4), "sz": _sb(128, U8),
     "qb": _sb(384, X4), "sb": _sb(384, U8), "qland": _sb(320, X4), "sland": _sb(320, U8),
-    "qe": _sb(512, X4), "se": _sb(512, U8), "et": _sb(2048, BF), "e1": _sb(2048, BF),
-    "pool0": _sb(2048, BF), "pool1": _sb(2048, BF), "pool2": _sb(2048, BF), "pool3": _sb(1280, BF),
-    "bt": _sb(512, BF), "zt": _sb(512, BF), "rel": _sb(4 * P, F32), "fk": _sb(2 * P, BF),
+    "qe": _sb(512, X4), "se": _sb(512, U8), "et": _sb(516, BF), "e1": _sb(516, BF), "zero": _sb(512, BF),
+    "qk": _sb(256, X4), "sk": _sb(256, U8), "kt": _sb(1024, BF), "k1": _sb(256, BF),
+    "fl0": _sb(4 * FW, BF), "fl1": _sb(4 * FW, BF), "qfl0": _sb(CW, X4), "sfl0": _sb(CW, U8),
+    "qfl1": _sb(CW, X4), "sfl1": _sb(CW, U8), "db": _sb(FW, F32), "bsc": _sb(2 * FW, F32), "sel": _sb(160, F32),
+    "bt": _sb(512, BF), "zt": _sb(512, BF), "rel": _sb(512, F32),
     "uli": _sb(16, I32), "ul": _sb(16, U16), "yi": _sb(P, I32), "zi": _sb(P, I32), "nz": _sb(P, F32),
     "ma": _sb(P, F32), "d0": _sb(P, F32), "d16": _sb(P, F32), "d4": _sb(128, F32), "x4": _sb(128, F32),
     "nz4": _sb(128, F32), "ci": _sb(8, I32), "cf": _sb(8, F32), "x16": _sb(16, F32), "lt": _sb(16, F32),
-    "on16": _sb(576, BF), "rs16": _sb(P, BF), "ones": _sb(128, F32),
-    "j4": _sb(P + K, F32), "jw": _sb(22, F32), "jo": _sb(20, F32), "du": _sb(22, F32),
-    "tc": _sb(M, F32), "pg": _sb(M, F32), "i1": _sb(M, F32), "ht": _sb(464, F32), "cc": _sb(20, F32),
-    "hm": _sb(2 * P, F32), "hh": _sb(2 * P, F32), "fl": _sb(24 * 192, BF), "sc": _sb(24 * 192, BF),
-    "st0": _sb(14 * P, BF), "st1": _sb(14 * P, BF), "cs2": _sb(14 * 336, BF), "mk": _sb(65 * 14, BF),
-    "tr": _sb(2 * P, BF), "trs": _sb(2 * P, BF), "half": _sb(576, BF), "y2": _sb(576, I32), "up": _sb(40, F32),
-    "tt": _sb(28 * P, BF), "junk": _sb(8 * L, BF), "eq": _sb(2 * P, BF), "eqs": _sb(2 * P, BF),
-    "acc": _sb(80, F32), "ce": _sb(40, F32), "rk": _sb(40, F32), "ro": _sb(20, F32), "ra": _sb(20, F32),
-    "rou": _sb(20, U16), "rau": _sb(20, U16), "vz": _sb(P, F32),
-    "so": _sb(P, F32), "sa": _sb(P, F32), "sn": _sb(128, F32), "sn2": _sb(P, F32), "sn3": _sb(P, F32), "sn4": _sb(L, F32),
-    "bl": _sb(16, U16), "zl": _sb(32, U16), "fu": _sb(80, U16), "ou": _sb(10, U16), "au": _sb(8, U16),
-    "ptu": _sb(20, U16), "sm": _sb(160, F32), "smi": _sb(80, I32), "blu": _sb(20, U16), "to": _sb(L, F32),
+    "ones": _sb(128, F32), "j4": _sb(3 * K + P + K, F32), "jw": _sb(22, F32), "jo": _sb(20, F32), "du": _sb(22, F32),
+    "tc": _sb(M, F32), "pg": _sb(M, F32), "i1": _sb(M, F32), "ht": _sb(464, F32),
+    "hm": _sb(2 * P, F32), "hh": _sb(2 * P, F32), "junk": _sb(8 * L, BF), "tsum": _sb(40, F32), "rk": _sb(40, F32),
+    "rou": _sb(20, U16), "rau": _sb(20, U16), "vz": _sb(P, F32), "so": _sb(P, F32), "sa": _sb(P, F32),
+    "sn": _sb(192, F32), "sn2": _sb(P, F32), "sno": _sb(L, F32), "snt": _sb(L, F32), "sna": _sb(NA, F32),
+    "snp": _sb(NA, F32), "snx": _sb(NA, F32), "bl": _sb(16, U16), "zl": _sb(32, U16), "fu": _sb(80, U16),
+    "ou": _sb(10, U16), "au": _sb(8, U16), "pal": _sb(8, U16), "wl": _sb(8, U16), "wx": _sb(8, F32),
+    "ptu": _sb(20, U16), "sm": _sb(40, F32), "smi": _sb(80, I32), "blu": _sb(20, U16), "to": _sb(L, F32),
     "tou": _sb(10, U16), "cnt": _sb(8, F32), "cni": _sb(8, I32), "cn": _sb(24, I32), "twu": _sb(20, U16),
-    "fr": _sb(144, F32), "shu": _sb(22, U16), "totu": _sb(2, U16), "bs": _sb(24, F32), "posu": _sb(22, U16),
-    "sh": _sb(M, F32), "shj": _sb(P + K, F32), "tw": _sb(4 * 1024, F32), "more": _sb(128, F32),
-    "cs": _sb(128, F32), "ix": _sb(P, F32), "ixj": _sb(P, F32), "tl": _sb(20, U16), "yt": _sb(2 * P, F32),
+    "fr": _sb(96, F32), "shu": _sb(22, U16), "totu": _sb(2, U16), "bs": _sb(24, F32), "posu": _sb(22, U16),
+    "sh": _sb(M + 16, F32), "tw": _sb(4 * TW, F32), "pa": _sb(NA, F32), "more": _sb(NA, F32),
+    "cs": _sb(NA, F32), "ix": _sb(NA, F32), "tl": _sb(20, U16), "yt": _sb(2 * P, F32),
 }
 for _b in range(8):
     SCRATCH["ps%d" % _b] = ("psum", [128, 512], F32)
@@ -83,6 +91,8 @@ def ap(T, x):
 def span(x):
     if x[1].startswith("ps"):
         return 1
+    if x[4] == 1:
+        return ((1 << (x[3] - x[2])) - 1) << x[2]
     return sum(1 << c for c in range(x[2], x[3], x[4]))
 
 
@@ -130,12 +140,16 @@ def needs(ops):
     return pre
 
 
+def adds_to(o, p):
+    return o["grp"] is not None and o["grp"] == p["grp"]
+
+
 def order(ops):
     n, pre = len(ops), needs(ops)
     reach = [0] * n
     for i in range(n):
         if ops[i]["ext"]:
-            pre[i] |= set([j for j in range(i) if ops[j]["k"] == "remote"][-2:])
+            pre[i] |= set(j for j in range(i) if ops[j]["k"] == "remote" and ops[j]["arr"] == ops[i]["ext"][0][0])
         far = 0
         for j in pre[i]:
             far |= reach[j]
@@ -143,65 +157,64 @@ def order(ops):
         pre[i] = [j for j in sorted(pre[i]) if not far >> j & 1]
     cases = [[busy(o, *c) for o in ops] for c in CASES]
     cost = cases[1]
+    pre = [[(j, 0.0 if adds_to(ops[i], ops[j]) else 1.0) for j in pre[i]] for i in range(n)]
     post = [[] for _ in ops]
     for i in range(n):
-        for j in pre[i]:
-            post[j].append(i)
+        for j, f in pre[i]:
+            post[j].append((i, f))
     way = [0.0] * n
     for i in range(n - 1, -1, -1):
-        way[i] = cost[i][0] + cost[i][1] + max([way[j] for j in post[i]] + [0.0])
+        way[i] = cost[i][0] + max([way[j] + f * cost[i][1] for j, f in post[i]] + [cost[i][1]])
 
-    def place(seq, before, back):
-        start, held = [0.0] * n, {}
-        for i in seq:
-            t, d = 0.0, cost[i][0]
-            for j in before[i]:
-                t = max(t, start[j] + cost[j][0] + cost[i if back else j][1])
-            row = held.setdefault(ops[i]["q"], [])
-            k = len(row)
-            while k > 0 and row[k - 1][1] > t:
-                k -= 1
-            while k < len(row) and row[k][0] < t + d:
-                if row[k][1] > t:
-                    t = row[k][1]
-                k += 1
-            row.insert(k, (t, t + d))
-            start[i] = t
-        return start
+    qi = ["VSPGY".index(o["q"]) for o in ops]
+    ahead = [[(j, f * cost[i][1]) for j, f in post[i]] for i in range(n)]
+    behind = [[(j, f * cost[j][1]) for j, f in pre[i]] for i in range(n)]
 
-    def legal(key):
-        top = list(key)
-        for i in range(n - 1, -1, -1):
-            for j in post[i]:
-                top[i] = max(top[i], top[j] + 1e-3)
-        return sorted(range(n), key=lambda i: (-top[i], i))
+    def place(key, before, after):
+        left, ready, free = [len(p) for p in before], [0.0] * n, [0.0] * 5
+        wait = [[i for i in range(n) if not left[i] and qi[i] == q] for q in range(5)]
+        seq, end = [], [0.0] * n
+        for _ in range(n):
+            t, q = min((max(free[q], min([ready[i] for i in wait[q]])), q) for q in range(5) if wait[q])
+            i = max([(key[i], i) for i in wait[q] if ready[i] <= t])[1]
+            wait[q].remove(i)
+            end[i] = free[q] = t + cost[i][0]
+            seq.append(i)
+            for j, w in after[i]:
+                if end[i] + w > ready[j]:
+                    ready[j] = end[i] + w
+                left[j] -= 1
+                if not left[j]:
+                    wait[qi[j]].append(j)
+        return seq, end
 
     def length(seq, c):
-        done, free = [0.0] * n, {}
+        done, free, end = [0.0] * n, [0.0] * 5, 0.0
         for i in seq:
-            t = free.get(ops[i]["q"], 0.0)
-            for j in pre[i]:
-                if done[j] > t:
-                    t = done[j]
-            free[ops[i]["q"]] = t + c[i][0]
-            done[i] = t + c[i][0] + c[i][1]
-        return max(done)
+            t = free[qi[i]]
+            for j, f in pre[i]:
+                if done[j] + f * c[j][1] > t:
+                    t = done[j] + f * c[j][1]
+            done[i] = free[qi[i]] = t + c[i][0]
+            end = max(end, done[i] + c[i][1])
+        return end
 
     rnd = np.random.default_rng(SEED)
-    key, best = way, None
+    key, best, now = way, None, None
     for p in range(PASSES):
-        fw = place(legal(key), pre, False)
-        seq = sorted(range(n), key=lambda i: (fw[i], i))
+        seq, fw = place(key, pre, ahead)
         end = sum(length(seq, c) * w for c, w in zip(cases, WEIGHT))
-        if best is None or end <= best[0]:
-            best = (end, fw, seq)
-        if p % 2 == 1 and p > 6:
-            grp = {ops[int(i)]["run"]: NOISE * float(rnd.random()) for i in rnd.integers(0, n, 6)}
-            key = [-best[1][i] + grp.get(ops[i]["run"], 0.0) for i in range(n)]
+        if best is None or end < best[0]:
+            best = (end, seq)
+        if now is None or end <= now[0] + 150 * float(rnd.random()) ** 3:
+            now = (end, fw, key)
+        if p < 8 or p % 10 == 0:
+            key = place(now[1], post, behind)[1]
         else:
-            bw = place(legal([fw[i] + cost[i][0] + cost[i][1] for i in range(n)]), post, True)
-            key = [bw[i] + cost[i][0] for i in range(n)]
-    return best[2]
+            grp = {ops[int(i)]["run"]: NOISE * float(rnd.standard_normal()) for i in rnd.integers(0, n, 4)}
+            key = [now[2][i] + grp.get(ops[i]["run"], 0.0) for i in range(n)]
+    PLAN["end"] = best[0]
+    return best[1]
 
 
 PLAN = {}
@@ -217,6 +230,8 @@ def emit(g, T, ops):
     for o, pre in zip(ops, PLAN["needs"]):
         deps = {}
         for j in pre:
+            if adds_to(o, ops[j]):
+                continue
             key = ("dma", j) if ops[j]["dma"] else ops[j]["q"]
             deps[key] = max(deps.get(key, j), j)
         o["deps"] = list(deps.values())
@@ -262,7 +277,7 @@ def rank_program(g, core, T, topo):
     ops = []
     run = ["", 0]
 
-    def op(q, f, a, nout=1, kw=None, dma=False, ext=(), after=(), k=None):
+    def op(q, f, a, nout=1, kw=None, dma=False, ext=(), after=(), k=None, grp=None, arr=None):
         kw = kw or {}
         w = [x for x in a[:nout] if is_view(x)] + [x for n, x in kw.items() if n == "accum_out"]
         r = [x for x in a[nout:] if is_view(x)] + [x for n, x in kw.items() if n != "accum_out" and is_view(x)] + list(after)
@@ -270,7 +285,7 @@ def rank_program(g, core, T, topo):
         name = w[0][1] if w else ""
         if name != run[0]:
             run[0], run[1] = name, len(ops)
-        ops.append({"q": q, "f": f, "a": a, "kw": kw, "r": r, "w": w, "dma": dma, "ext": ext, "k": k, "run": run[1]})
+        ops.append({"q": q, "f": f, "a": a, "kw": kw, "r": r, "w": w, "dma": dma, "ext": ext, "k": k, "run": run[1], "grp": grp, "arr": arr})
 
     def ts(o, i, s1, op0, s2=None, op1=None):
         op("V", lambda e: e.tensor_scalar, [o, i, s1, s2, op0] + ([] if op1 is None else [op1]))
@@ -293,12 +308,15 @@ def rank_program(g, core, T, topo):
     def quant(c, s, i):
         op("V", lambda e: e.quantize_mx, [c, s, i], nout=2, k="quant")
 
-    def mm(b, n, wq, wsc, wa, xq, xs, xa, ext=()):
-        op("P", lambda e: e.matmul_mx, [v("ps%d" % b, 0, n), v(wq, wa, wa + 128), v(wsc, wa, wa + 128), v(xq, xa, xa + n), v(xs, xa, xa + n), True, True], ext=ext)
+    def mm(b, n, wq, wsc, wa, xq, xs, xa, ext=(), start=True, stop=True, grp=None):
+        op("P", lambda e: e.matmul_mx, [v("ps%d" % b, 0, n), v(wq, wa, wa + 128), v(wsc, wa, wa + 128), v(xq, xa, xa + n), v(xs, xa, xa + n), start, stop], ext=ext, grp=grp)
 
     def iota(o, pat, base=0, cm=0):
         kw = {} if SCRATCH[o[1]][2] == I32 else {"allow_small_or_imprecise_dtypes": True}
         op("G", lambda e: e.iota, [o, pat, base, cm], kw=kw)
+
+    def keep(o, i, pat, f, base, cm):
+        op("G", lambda e: e.affine_select, [o, i, pat, f, 0.0, base, cm])
 
     def dma(q, o, i, after=()):
         op(q, lambda e: e.dma_start, [o, i], dma=True, after=after)
@@ -306,59 +324,60 @@ def rank_program(g, core, T, topo):
     def fill(name, a, b, c):
         for lo in range(a, b, 512):
             hi = min(b, lo + 512)
-            act(v(name, lo, hi), v("bt", 0, hi - lo), AF.Identity, bias=c)
+            act(v(name, lo, hi), v("zero", 0, hi - lo), AF.Identity, bias=c)
 
-    dma("Y", v("mt"), T.m[:])
+    def pool(r, a, b, s=1):
+        z = 4 * (P + K) * (R - r)
+        return v("pool", z + a, z + b, s)
+
+    mt = pool(-1, 0, 4 * M)
+    dma("Y", mt, T.m[:])
     dma("S", v("pti"), T.pt[:])
     dma("S", v("ut"), T.u[:])
-    dma("Y", cast(v("qw"), dt.uint8), T.wc[:], after=[v("mt")])
-    dma("Y", v("sw"), T.ws[:], after=[v("mt")])
-    dma("Y", v("vt"), T.v[:], after=[v("mt")])
+    dma("Y", cast(v("qw"), dt.uint8), T.wc[:], after=[mt])
+    dma("Y", v("sw"), T.ws[:], after=[mt])
+    dma("Y", v("vt"), T.v[:], after=[mt])
 
-    ns, hw = 20 - NV, 32 * MID + 32
-    ms(v("bt"), 0.0)
+    ms(v("zero"), 0.0)
+    ms(v("bt", 256, 512), 0.0)
+    ms(v("e1"), 1.0)
+    ms(v("fl0"), 0.0)
+    if NFL > 1:
+        fill("fl1", 0, 4 * FW, 0.0)
     iota(v("uli"), [[1, 2], [16, 8]])
     iota(v("yi"), [[0, 20], [1, 16]], 128, -1)
     iota(v("ci", 0, 1), [[0, 1]], 0, 1)
     iota(v("x4"), [[0, 32], [1, 4]])
     iota(v("x16"), [[1, 16]])
     iota(v("jw"), [[16, 22]])
-    iota(v("cc"), [[16, 20]], 16)
-    iota(v("y2", 0, hw), [[0, MID + 1], [16, 2], [0, 16]], 0, 1)
+    keep(v("kt", 0, 512), v("e1", 0, 512), [[-1, 128], [0, 4]], A.is_equal, 0, 1)
+    keep(v("k1", 0, 128), v("e1", 0, 128), [[-16, 8], [0, 16]], A.is_ge, 0, 1)
+    keep(v("k1", 128, 256), v("k1", 0, 128), [[16, 8], [0, 16]], A.is_ge, 15, -1)
+    fill("kt", 512, 1024, 0.0)
+    for b in range(4):
+        act(v("kt", 512 + 5 * b, 1024, 16), v("k1", 128 + b, 256, 4))
     iota(v("i1"), [[1, M]])
     iota(v("pg"), [[1, 22], [22, 16]])
-    for k in (0, 1, 3):
-        iota(v("tw", 1024 * k + P, 1024 * k + 1024), [[0, 1024 - P]])
-    for r in range(R):
-        iota(v("pool%d" % r, 1536, 2048), [[0, 512]])
-    iota(v("j4"), [[4, P + K]])
+    iota(v("j4"), [[4, 3 * K + P + K]], -12 * K)
     iota(v("tc"), [[1, 16], [16, 22]])
-    iota(v("e1"), [[0, 2048]], 1)
-    op("G", lambda e: e.affine_select, [v("et"), v("e1"), [[-1, 4], [1, 512]], A.is_equal, 0.0, 0, -4])
-    for x in range(2):
-        fill("st%d" % x, 16 * (NV + 1) * ns, 16 * MID * ns, 0.0)
-        fill("rel", P * x + 128, P * x + P, 0.0)
-    fill("mk", 0, 65 * ns, 1.0)
-    ms(v("mk", 0, 65 * ns, ns), 0.0)
-    fill("cs2", 0, 16 * ns, 0.0)
-    fill("cs2", 16 * (MID + 1) * ns, 16 * (MID + 2) * ns, 0.0)
-    fill("up", 0, 40, 0.0)
-    ts(v("y2", 0, hw), v("y2", 0, hw), 16, A.bitwise_and)
-    ts(v("half", 0, hw), v("y2", 0, hw), 0.0, A.is_equal)
-    fill("on16", 0, 48 * NV, 1.0)
-    ms(v("on16", 0, 48 * NV, 16 * NV), 0.0)
-    fill("rs16", 0, P, 1.0)
+    keep(v("et"), v("e1"), [[-1, 516]], A.is_equal, 3, 4)
+    for k in (0, 1, 3):
+        iota(v("tw", TW * k + P, TW * k + HC), [[0, HC - P]])
+    iota(v("tw", 2 * TW + P, 2 * TW + P + K), [[0, K]], M)
     fill("ones", 0, 128, 1.0)
-    fill("shj", P, P + K, 1.0)
-    fill("ix", NA, P, 0.0)
+    fill("sh", M, M + 16, 1.0)
     fill("ht", 0, 464, 0.0)
-    fill("d0", 0, P, FAR)
-    ms(v("d0", 0, P, 16), -2 * FAR)
-    ms(v("rs16", 0, P, 16), 0.0)
+    fill("d0", 0, P, -FAR)
+    ms(v("d0", 0, P, 16), 2 * FAR)
+    fill("db", 0, FW, BIG)
+    ms(v("db", 0, 40, 4), 0.0)
+    ms(v("db", 40, 80, 4), -16.0)
+    ms(v("db", 84, FW, 84), -16.0)
+    ms(v("db", 124, FW, 84), -16.0)
     cp(v("ul"), v("uli"))
     ts(v("zi"), v("yi"), 15, A.bitwise_and)
     ts(v("nz"), v("zi"), 0.0, A.not_equal)
-    act(v("ma"), v("nz"), AF.Identity, scale=-FAR)
+    act(v("ma"), v("nz"), AF.Identity, scale=FAR)
     act(v("d16"), v("nz"), AF.Identity, scale=HUGE + BIG, bias=-HUGE)
     ts(v("ci", 1, 2), v("ci", 0, 1), 15, A.bitwise_and)
     ts(v("ci", 2, 3), v("ci", 0, 1), 2, A.logical_shift_right, 3, A.bitwise_and)
@@ -368,10 +387,12 @@ def rank_program(g, core, T, topo):
     ts(v("cf", 2, 3), v("ci", 1, 2), -BIG, A.mult, 15 * BIG, A.add)
     ts(v("cf", 5, 6), v("ci", 2, 3), -BIG, A.mult, 3 * BIG, A.add)
     tt(v("cf", 3, 4), v("cf", 5, 6), v("cf", 4, 5), A.subtract)
+    ts(v("cf", 6, 7), v("cf", 5, 6), v("cf", 0, 1), A.add, 176.0, A.add)
     ts(v("nz4"), v("x4"), v("cf", 1, 2), A.subtract, 0.0, A.not_equal)
     act(v("d4"), v("nz4"), AF.Identity, scale=HUGE + BIG, bias=-HUGE)
     ts(v("lt"), v("x16"), v("cf", 0, 1), A.is_lt)
-    ts(v("du"), v("jw"), v("cf", 0, 1), A.add, float(M), A.add)
+    ts(v("cf", 7, 8), v("ci", 1, 2), 22.0, A.mult, float(PW - P + 1), A.add)
+    ts(v("du"), v("i1", 0, 22), v("cf", 7, 8), A.add)
     ts(v("jo"), v("jw", 0, 20), v("cf", 0, 1), A.add, float(3 * K), A.add)
     for f in range(3):
         ts(v("ht", 128 * f + 112, 128 * f + 128), v("zi", 0, 16), 0.0, A.is_equal, float(256 ** f), A.mult)
@@ -383,122 +404,117 @@ def rank_program(g, core, T, topo):
     act(v("su2"), by(v("su"), v("ul")))
 
     def gather_f(r):
-        src = v("mt") if r == 0 else v("pool%d" % (r - 1))
+        src = mt if r == 0 else pool(r - 1, 0, 4 * PW)
         for t in range(4):
-            if t < 2 and r > 0:
-                tt(v("pool%d" % r, t, 4 * P, 4), by(v("rel", P * t, P * t + P), v("rau")), v("fk", P * t, P * t + P), A.add)
-            else:
-                (cp if t < 2 else act)(v("pool%d" % r, t, 4 * P, 4), by(src, v("fu", 20 * t, 20 * t + 20)))
-        quant(v("qf"), v("sf"), v("pool%d" % r, 0, 4 * P))
-
-    def own(x, b):
-        for lo, hi in (((L, P), (0, L)) if x == 0 else ((0, P),)):
-            tt(v("hm", P * x + lo, P * x + hi), v("ps%d" % b, lo, hi), v("ma", lo, hi), A.add)
-            scan(v("hh", P * x + lo, P * x + hi), v("d0", lo, hi), v("hm", P * x + lo, P * x + hi), 0.0, A.min, A.max)
+            (cp if t in F_V[r] else act)(pool(r, t, 4 * P, 4), by(src, v("fu", 20 * t, 20 * t + 20)))
+        quant(v("qf"), v("sf"), pool(r, 0, 4 * P))
 
     def col(x, c):
         return v("hh", P * x + 16 * c + 15, P * x + 16 * c + 16)
 
-    def rank_v(x, b):
-        w = 16 * NV
-        for c in range(NV):
-            e, z = 16 * c + 16, w * (12 * x + c)
-            ts(v("fl", z, z + e), v("ps%d" % b, 0, e), col(x, c), A.is_ge)
-            if e < w:
-                ts(v("fl", z + e, z + w), v("ps%d" % b, e, w), col(x, c), A.is_gt)
-            if c % 3 == 2 or c == NV - 1:
-                n = w * (c % 3 + 1)
-                scan(v("sc", z + w - n, z + w), v("on16", 0, n), v("fl", z + w - n, z + w), 0.0, A.mult, A.add)
-        tt(v("eq", P * x, P * x + P), v("ps%d" % b, 0, P), v("hh", P * x, P * x + P), A.is_equal)
-        scan(v("eqs", P * x, P * x + P), v("rs16"), v("eq", P * x, P * x + P), 0.0, A.mult, A.add)
-        z = 12 * w * x
-        tt(v("rk", 20 * x, 20 * x + NV), v("sc", z + w - 1, z + w * NV, w), v("eqs", P * x + 15, P * x + w, 16), A.subtract)
-        tt(v("ce", 20 * x + NV, 20 * x + 20), v("cc", NV, 20), v("eqs", P * x + w + 15, P * x + P, 16), A.subtract)
+    def rank_of(x, r, bv, bs, ba, bb):
+        fl, qfl, sfl = "fl%d" % (x % NFL), "qfl%d" % x, "sfl%d" % x
+        for lo, hi in (((0, L), (L, P)) if x == 0 else ((0, P),)):
+            tt(v("hm", P * x + lo, P * x + hi), v("ps%d" % bv, lo, hi), v("ma", lo, hi), A.add)
+            scan(v("hh", P * x + lo, P * x + hi), v("d0", lo, hi), v("hm", P * x + lo, P * x + hi), 0.0, A.max, A.min)
+        tt(v(fl, 0, P), v("ps%d" % bv, 0, P), v("hh", P * x, P * x + P), A.is_gt)
 
-    def rank_s(x, b):
-        for c in range(19, NV - 1, -1):
-            e, z = 16 * c + 16, P * (14 * x + c - NV)
-            w = P if c >= MID else e
-            act(v("tt", z, z + w), v("ps%d" % b, 0, w), AF.Sign, bias=col(x, c), scale=-1.0)
-            act(v("st%d" % x, c - NV, e * ns, ns), v("tt", z, z + e), AF.Relu, accum_out=v("acc", 40 * x + c, 40 * x + c + 1))
-            if e < w:
-                act(v("tt", z + e, z + w), v("tt", z + e, z + w), AF.Relu, scale=-1.0, accum_out=v("up", 20 * x + c, 20 * x + c + 1))
+        def later(row, c, a, b, mine):
+            o = v(fl, P * row + a, P * row + b)
+            if mine:
+                ts(o, v("ps%d" % bv, a, b), col(x, c), A.is_gt)
+            else:
+                act(o, v("ps%d" % bs, a, b), AF.Sign, bias=col(x, c), scale=-1.0)
 
-    def rank_end(x):
-        st, w = "st%d" % x, 16 * MID
-        rf, ru = ("ro", "rou") if x == 0 else ("ra", "rau")
-        tt(v("rk", 20 * x + NV, 20 * x + 20), v("ce", 20 * x + NV, 20 * x + 20), v("acc", 40 * x + NV, 40 * x + 20), A.subtract)
-        for k in range(MID - 1, NV - 1, -1):
-            s = ns - (k + 1 - NV)
-            scan(v("cs2", 16 * (k + 1) * ns, 16 * (k + 2) * ns), v("mk", s, s + 16 * ns), v(st, 16 * k * ns, 16 * (k + 1) * ns), 0.0, A.mult, A.add)
-        for k in range(0, NV, 4):
-            n = 16 * min(4, NV - k) * ns
-            scan(v("cs2", 16 * (k + 1) * ns, 16 * (k + 1) * ns + n), v("mk", 0, n), v(st, 16 * k * ns, 16 * k * ns + n), 0.0, A.mult, A.add)
-        op("V", lambda e: e.transpose, [v("tr", 0, w), v("cs2", 17 * ns - 1, (w + 16) * ns, ns)])
-        op("V", lambda e: e.transpose, [v("tr", w, 2 * w + 32), v("cs2", ns - 1, (w + 32) * ns, ns)])
-        scan(v("trs", 0, hw), v("tr", 0, hw), v("half", 0, hw), 0.0, A.add, A.mult)
-        tt(v("up", 20 * x, 20 * x + MID, 2), v("trs", 15, w, 32), v("trs", w + 31, 2 * w, 32), A.add)
-        tt(v("up", 20 * x + 1, 20 * x + MID, 2), v("trs", w + 47, 2 * w + 32, 32), v("trs", 31, w, 32), A.add)
-        tt(v(rf), v("rk", 20 * x, 20 * x + 20), v("up", 20 * x, 20 * x + 20), A.add)
-        cp(v(ru), v(rf))
+        def whole(row, a, b):
+            act(v(fl, P * row + a, P * row + b), v(fl, P * row + a, P * row + b), AF.Relu, scale=-1.0)
 
-    def list4(row, n, out):
-        scan(v("sn", 0, n), v("d4", 0, n), v(row, 0, n), 0.0, A.add, A.max)
-        ts(v(out), v("sn", 3, n, 4), v("cf", 3, 4), A.subtract)
+        for c in range(10):
+            a, b, e = 16 * c + 16, 16 * c + 160, 16 * c + 176
+            lo, up = c in V_LO[x], c in V_UP[x] or c == 9
+            later(c + 1, c, a, b, lo)
+            if c < 9:
+                later(c + 1, c + 10, e, P, up)
+            if not (lo and up):
+                whole(c + 1, e if lo else a, b if up else P)
+            ts(v(fl, P * (c + 2), P * (c + 2) + a), v("ps%d" % bv, 0, a), col(x, c + 10), A.is_ge)
+        for a, b in zip(CHUNKS, CHUNKS[1:]):
+            quant(v(qfl, a, b), v(sfl, a, b), v(fl, 4 * a, 4 * b))
+        for k in range(12):
+            mm(ba, 128, "qk", "sk", 128, qfl, sfl, 80 * k, start=k == 0, stop=k == 11, grp=(x, r))
+        z = FW * x
+        for k, (a, b) in enumerate(zip(PIECES, PIECES[1:])):
+            mm(bb[k % 2], b - a, "qk", "sk", 0, qfl, sfl, a)
+            scan(v("bsc", z + a, z + b), v("db", a, b), v("ps%d" % bb[k % 2], 0, b - a), 0.0, A.min, A.add)
+        scan(v("sel", 80 * x, 80 * x + 80), v("d4", 0, 80), v("ps%d" % ba, 0, 80), 0.0, A.add, A.max)
+        tt(v("tsum", 20 * x, 20 * x + 10), v("bsc", z + 119, z + FW, 84), v("bsc", z + 3, z + 40, 4), A.add)
+        tt(v("tsum", 20 * x + 10, 20 * x + 20), v("bsc", z + 163, z + FW, 84), v("bsc", z + 43, z + 80, 4), A.add)
+        tt(v("rk", 20 * x, 20 * x + 20), v("tsum", 20 * x, 20 * x + 20), v("sel", 80 * x + 3, 80 * x + 80, 4), A.subtract)
+        ts(v("rau" if x else "rou"), v("rk", 20 * x, 20 * x + 20), v("cf", 6, 7), A.add)
+
+    def list4(row, a, n, out):
+        scan(v("sn", a, a + n), v("d4", 0, n), v(row, 0, n), 0.0, A.add, A.max)
+        ts(v(out), v("sn", a + 3, a + n, 4), v("cf", 3, 4), A.subtract)
 
     def list16(row, n, out, k, tmp):
         scan(v(tmp, 0, n), v("d16", 0, n), row, 0.0, A.add, A.max)
         ts(out, v(tmp, 15, n, 16), v("cf", 2, 3), A.subtract, k, A.mult)
 
-    def sources(r):
-        ts(v("smi", 0, 20), v("ro"), float(512 - L), A.add)
+    def sources():
+        ts(v("smi", 0, 20), v("rk", 0, 20), v("cf", 6, 7), A.add, float(512 - L), A.add)
         ts(v("smi", 20, 40), v("smi", 0, 20), 512 + K - 1, A.bitwise_and)
-        tt(v("sm", 20 * r, 20 * r + 20), v("smi", 20, 40), v("jo"), A.max)
-        ts(v("blu"), v("sm", 20 * r, 20 * r + 20), float(-3 * K), A.add)
-        ts(v("sm", 60, 80), v("sm", 20 * r, 20 * r + 20), float(P), A.add)
+        tt(v("sm", 0, 20), v("smi", 20, 40), v("jo"), A.max)
+        cp(v("blu"), v("sm", 0, 20))
 
     def next_lists():
-        ts(v("smi", 40, 60), v("ra"), float(1024 - NA), A.add)
+        ts(v("smi", 40, 60), v("rk", 20, 40), v("cf", 6, 7), A.add, float(1024 - NA), A.add)
         ts(v("smi", 60, 80), v("smi", 40, 60), 1023, A.bitwise_and)
-        tt(v("sm", 80, 100), v("smi", 60, 80), v("sm", 60, 80), A.max)
-        for t in range(2, 4):
-            ts(v("fu", 20 * t, 20 * t + 20), v("sm", 80, 100), 4.0, A.mult, float(t - 2048), A.add)
+        tt(v("sm", 20, 40), v("smi", 60, 80), v("sm", 0, 20), A.max)
+        for t in range(4):
+            ts(v("fu", 20 * t, 20 * t + 20), v("sm", 20, 40), 4.0, A.mult, float(t - 12 * K), A.add)
+        ts(v("tl"), v("sm", 20, 40), float(-3 * K), A.add)
 
-    def tables(r):
+    def free_pages(r):
         end = r == R - 1
-        k = 3 if end else r
-        list16(v("tw", 1024 * r, 1024 * r + P), P, v("twu"), 1.0, "sn3")
+        w = TW * (3 if end else r)
+        list16(v("so", 0, L), L, v("ou"), 0.25, "sno")
+        act(v("to"), by(v("tw", TW * r, TW * r + P), v("ou")))
+        list16(v("to"), L, v("tou"), 1.0, "snt")
         for i in range(8):
             act(v("junk", L * i, L * i + L), by(v("ht", 16 * (7 - i), 16 * (7 - i) + M), v("tou")), accum_out=v("cnt", i, i + 1))
         cp(v("cni"), v("cnt"))
         ts(v("cn", 0, 8), v("cni"), 255, A.bitwise_and)
         ts(v("cn", 8, 16), v("cni"), 8, A.logical_shift_right, 255, A.bitwise_and)
         ts(v("cn", 16, 24), v("cni"), 16, A.logical_shift_right)
-        ts(v("shu"), v("cn", 0, 22), 1.0, A.is_gt)
-        act(v("sh"), by(v("i1"), v("shu")))
-        act(v("shj", 0, P), by(v("sh"), v("twu")))
-        ts(v("fr", 0, 22), v("cn", 0, 22), 0.0, A.is_equal)
-        ts(v("fr", 24, 46), v("cn", 0, 22), 1000.0, A.mult)
-        scan(v("fr", 48, 70), v("ones", 0, 22), v("fr", 0, 22), 0.0, A.mult, A.add)
-        tt(v("fr", 72, 94), v("fr", 24, 46), v("du"), A.min)
-        cp(v("totu", 0, 1), v("fr", 69, 70))
+        ts(v("shu"), v("cn", 0, 22), 1.0, A.not_equal)
+        act(v("sh", 0, M), by(v("i1"), v("shu")))
+        ts(v("fr", 0, 22), v("cn", 0, 22), 0.0, A.is_gt)
+        scan(v("fr", 24, 46), v("ones", 0, 22), v("fr", 0, 22), 0.0, A.add, A.subtract)
+        tt(v("fr", 48, 70), v("fr", 0, 22), v("du"), A.mult)
+        cp(v("totu", 0, 1), v("fr", 45, 46))
         tt(v("bs", 0, 16), by(v("i1"), v("totu", 0, 1)), v("lt"), A.mult)
         op("V", lambda e: e.tensor_reduce, [v("bs", 16, 17), v("bs", 0, 16), AxisListType.X, A.add])
-        ts(v("fr", 96, 118), v("fr", 48, 70), v("bs", 16, 17), A.add, -1.0, A.add)
-        tt(v("fr", 120, 142), v("fr", 96, 118), v("fr", 72, 94), A.max)
-        cp(v("posu"), v("fr", 120, 142))
+        tt(v("fr", 72, 94), v("fr", 24, 46), v("fr", 48, 70), A.max)
+        ts(v("posu"), v("fr", 72, 94), v("bs", 16, 17), A.add, -1.0, A.add)
         if end:
-            act(v("tw", 3072, 3072 + P), by(v("pg"), v("twu")))
-        cp(by(v("tw", 1024 * k + P, 1024 * k + 1024), v("posu")), v("pg" if end else "i1"))
-        list16(v("sa", 0, NA), NA, v("au"), 0.25, "sn4")
-        act(v("more"), by(v("shj"), v("au")))
-        scan(v("cs"), v("ones"), v("more"), float(P + 4 * K - 1), A.mult, A.add)
-        tt(v("ix", 0, NA), v("cs"), v("more"), A.mult)
-        act(v("ixj"), by(v("ix"), v("rau")))
-        list16(v("ixj"), P, v("sm", 100, 120), 1.0, "sn2")
-        tt(v("sm", 120, 140), v("sm", 100, 120), v("sm", 20 * r, 20 * r + 20), A.max)
-        ts(v("tl"), v("sm", 120, 140), float(-3 * K), A.add)
-        act(v("yt", P, 2 * P) if end else v("tw", 1024 * (r + 1), 1024 * (r + 1) + P), by(v("tw", 1024 * k, 1024 * k + 1024), v("tl")))
+            list16(v("tw", TW * r, TW * r + P), P, v("twu"), 1.0, "sn2")
+            act(v("tw", w, w + P), by(v("pg"), v("twu")))
+        cp(by(v("tw", w + P, w + TW), v("posu")), v("pg" if end else "i1"))
+
+    def new_tables(r):
+        end = r == R - 1
+        w = TW * (3 if end else r)
+        list16(v("sa", 0, NA), NA, v("au"), 0.25, "sna")
+        act(v("pa"), by(v("tw", TW * r, TW * r + P + K), v("au")))
+        list16(v("pa"), NA, v("pal"), 1.0, "snp")
+        act(v("more"), by(v("sh"), v("pal")), scale=2.0)
+        scan(v("cs"), v("ones"), v("more"), float(2 * (P + K - 1)), A.mult, A.add)
+        tt(v("ix"), v("cs"), v("more"), A.mult)
+        scan(v("snx"), v("d16", 0, NA), v("ix"), 0.0, A.add, A.max)
+        tt(v("wx"), v("snx", 15, NA, 16), v("sna", 15, NA, 16), A.max)
+        ts(v("wl"), v("wx"), v("cf", 2, 3), A.subtract, 0.25, A.mult)
+        act(v("tw", w + HC, w + PW), by(v("tw", w, w + HC), v("wl")))
+        act(v("yt", P, 2 * P) if end else v("tw", TW * (r + 1), TW * (r + 1) + P), by(v("tw", w, w + PW), v("tl")))
 
     rid, pid, _ = topo.addr(nxt)
     mask = topo.mask(core, nxt)
@@ -506,52 +522,44 @@ def rank_program(g, core, T, topo):
 
     gather_f(0)
     act(v("tw", 0, P), by(v("tc"), v("ptu")))
-    quant(v("qland", 0, 128), v("sland", 0, 128), v("bt"))
-    quant(v("qe"), v("se"), v("et"))
+    quant(v("qk"), v("sk"), v("kt"))
+    for x in range(2):
+        quant(v("qfl%d" % x, CW - 128, CW), v("sfl%d" % x, CW - 128, CW), v("zero"))
+    quant(v("qland", 0, 128), v("sland", 0, 128), v("zero"))
+    for b in range(4):
+        quant(v("qe", 128 * b, 128 * b + 128), v("se", 128 * b, 128 * b + 128), v("et", 3 - b, 515 - b))
     quant(v("qv"), v("sv"), v("vt"))
     for r in range(R):
-        pool = "pool%d" % r
         for b in range(4):
             mm(b, P, "qu2", "su2", 128 * (b // 2), "qf", "sf", 0)
-        own(0, 0)
-        own(1, 2)
-        rank_v(0, 0)
-        rank_s(0, 1)
-        rank_end(0)
-        cp(by(v("so"), v("rou")), v("j4", 0, P))
-        list4("so", K, "bl")
-        act(v("bt", 0, 256), by(v(pool, 0, 4 * P), v("bl")))
+        rank_of(0, r, 0, 1, 4, (5, 6))
+        cp(by(v("so"), v("rou")), v("j4", 3 * K, 3 * K + P))
+        list4("so", 0, K, "bl")
+        act(v("bt", 0, 256), by(pool(r, 0, 4 * P), v("bl")))
         quant(v("qb", 128 * r, 128 * r + 128), v("sb", 128 * r, 128 * r + 128), v("bt"))
-        a, arr = 128 + K * r, T.sem["arr%d" % r]
-        op("G", lambda e: e.remote_dma, [ap(T, cast(v("qland", a, a + K), dt.uint8)), cast(v("qb", 128 * r, 128 * r + K), dt.uint8), arr, T.sem.sent, pid, rid, mask], k="remote")
-        op("G", lambda e: e.remote_dma, [ap(T, v("sland", a, a + K)), v("sb", 128 * r, 128 * r + K), arr, T.sem.sent, pid, rid, mask], k="remote")
-        sources(r)
+        a, arr = 128 + K * r, "arr%d" % r
+        op("G", lambda e: e.remote_dma, [ap(T, cast(v("qland", a, a + K), dt.uint8)), cast(v("qb", 128 * r, 128 * r + K), dt.uint8), T.sem[arr], T.sem.sent, pid, rid, mask], k="remote", arr=arr)
+        op("G", lambda e: e.remote_dma, [ap(T, v("sland", a, a + K)), v("sb", 128 * r, 128 * r + K), T.sem[arr], T.sem.sent, pid, rid, mask], k="remote", arr=arr)
+        sources()
         act(v("vz"), by(v("j4"), v("blu")))
-        for b in range(4):
-            mm(4 + b, 128, "qe", "se", 128 * b, "qland", "sland", a - K, ext=[("arr%d" % r, 2 * neng)])
-            act(v(pool, 4 * P + b, 4 * P + 4 * K, 4), v("ps%d" % (4 + b), K, 128))
-        rank_v(1, 2)
-        rank_s(1, 3)
-        rank_end(1)
-        list16(v("so", 0, L), L, v("ou"), 0.25, "sn4")
-        act(v("to"), by(v("tw", 1024 * r, 1024 * r + P), v("ou")))
-        list16(v("to"), L, v("tou"), 1.0, "sn4")
-        cp(by(v("sa"), v("rau")), v("vz"), after=[v("tou")])
-        list4("sa", NA, "zl")
-        cp(v("zt", 0, 256), by(v(pool, 0, 1536), v("zl", 0, 16)))
-        act(v("zt", 256, 512), by(v(pool, 0, 1536), v("zl", 16, 32)))
+        free_pages(r)
+        rank_of(1, r, 2, 3, 7, (0, 1))
+        for b, bank in enumerate((4, 5, 6, 1)):
+            mm(bank, 128, "qe", "se", 128 * b, "qland", "sland", a - K, ext=[(arr, 2 * neng)])
+            act(pool(r, 4 * P + b, 4 * P + 4 * K, 4), v("ps%d" % bank, K, 128))
+        cp(by(v("sa"), v("rau")), v("vz"))
+        list4("sa", K, NA, "zl")
+        if Z_V:
+            cp(v("zt", 0, 128 * Z_V), by(pool(r, 0, 4 * (P + K)), v("zl", 0, 8 * Z_V)))
+        act(v("zt", 128 * Z_V, 512), by(pool(r, 0, 4 * (P + K)), v("zl", 8 * Z_V, 32)))
         quant(v("qz"), v("sz"), v("zt"))
-        for t in range(2):
-            ts(v("fu", 20 * t, 20 * t + 20), v("sm", 20 * r, 20 * r + 20), 4.0, A.mult, float(t - 12 * K), A.add)
-            act(v("fk", P * t, P * t + P), by(v(pool, 0, 1536), v("fu", 20 * t, 20 * t + 20)))
-        for b in (2, 3, 0, 1):
+        for b in range(4):
             mm(4 + b, 128, "qw", "sw", 128 * b, "qz", "sz", 0)
-            act(v("rel", P * b, P * b + 128), v("ps%d" % (4 + b), 0, 128), AF.Relu, scale=0.03125)
-            if b >= 2:
-                tt(v(pool, 1536 + b, 2048, 4), v("rel", P * b, P * b + 128), v("zt", b, 512, 4), A.add)
+            act(v("rel", 128 * b, 128 * b + 128), v("ps%d" % (4 + b), 0, 128), AF.Relu, scale=0.03125)
+            tt(pool(r, 4 * HC + b, 4 * PW, 4), v("rel", 128 * b, 128 * b + 128), v("zt", b, 512, 4), A.add)
         next_lists()
         gather_f(r + 1)
-        tables(r)
+        new_tables(r)
 
     for h in range(2):
         mm(h, L, "qv", "sv", 0, "qf", "sf", L * h)

@@ -1,3 +1,4 @@
+import math
 import numpy as np
 from concourse.mybir import dt, AluOpType, AxisListType, ActivationFunctionType
 
@@ -6,18 +7,18 @@ AF = ActivationFunctionType
 M, P, K, L, NA, R = 352, 320, 64, 160, 128, 3
 HC = 704
 PW = HC + NA
-FW, CW = 920, 1008
+FW, CW = 880, 928
 TW = 1600
-V_LO = [(7, 8, 9), ()]
-V_UP = [(6, 7, 8), (7, 8)]
-CHUNKS = [0, 252, 504, 756, FW]
-PIECES = [0, 504, 756, FW]
-F_V = [(0, 1), (3,), (3,), (2, 3)]
+LOW = [11, 10]
+CHUNKS = {10: [0, 240, 480, 712, 840], 11: [40, 280, 520, 752, 880]}
+F_V = [(0, 1), (), (), ()]
 Z_V = 1
-NFL = 1
+NFL = 2
+WHO = {"e1": "V", "db": "S", "ht": "S", "ones": "S", "sh": "S", "kt": "S", "d0": "S"}
+H_ADD = (2, 3)
 CASES = [(120, (500, 2000), 1.0, 2.0), (150, (800, 3000), 1.25, 3.15), (130, (1000, 4500), 1.6, 4.6)]
 WEIGHT = [0.3, 0.4, 0.3]
-PASSES, SEED, NOISE = 3000, 2, 800
+PASSES, SEED, NOISE, MOVES, HEAT = 2500, 2, 800, 30000, 25.0
 BIG = float(2 ** 20)
 HUGE = float(2 ** 25)
 FAR = 1e29
@@ -32,22 +33,23 @@ SCRATCH = {
     "pool": _sb(4 * (R * (P + K) + PW), BF), "ut": _sb(512, BF), "vt": _sb(512, BF), "pti": _sb(20, I32),
     "qw": _sb(512, X4), "sw": _sb(512, U8), "qu": _sb(128, X4), "su": _sb(128, U8),
     "qu2": _sb(256, X4), "su2": _sb(256, U8), "qv": _sb(128, X4), "sv": _sb(128, U8),
-    "qf": _sb(P, X4), "sf": _sb(P, U8), "qz": _sb(128, X4), "sz": _sb(128, U8),
-    "qb": _sb(384, X4), "sb": _sb(384, U8), "qland": _sb(320, X4), "sland": _sb(320, U8),
+    "qf": _sb(4 * P, X4), "sf": _sb(4 * P, U8), "qz": _sb(128, X4), "sz": _sb(128, U8),
+    "qland": _sb(R * P, X4), "sland": _sb(R * P, U8), "bland": _sb(16 * R, U16), "dall": _sb(4 * P, BF),
     "qe": _sb(512, X4), "se": _sb(512, U8), "et": _sb(516, BF), "e1": _sb(516, BF), "zero": _sb(512, BF),
     "qk": _sb(256, X4), "sk": _sb(256, U8), "kt": _sb(1024, BF), "k1": _sb(256, BF),
+    "acc": _sb(40, F32), "hb": _sb(2 * L, F32), "hli": _sb(10, I32), "hl": _sb(10, U16),
     "fl0": _sb(4 * FW, BF), "fl1": _sb(4 * FW, BF), "qfl0": _sb(CW, X4), "sfl0": _sb(CW, U8),
-    "qfl1": _sb(CW, X4), "sfl1": _sb(CW, U8), "db": _sb(FW, F32), "bsc": _sb(2 * FW, F32), "sel": _sb(160, F32),
-    "bt": _sb(512, BF), "zt": _sb(512, BF), "rel": _sb(512, F32),
+    "qfl1": _sb(CW, X4), "sfl1": _sb(CW, U8), "db": _sb(128, F32), "bsc": _sb(160, F32), "sel": _sb(160, F32),
+    "zt": _sb(512, BF), "rel": _sb(4 * P, F32), "fk": _sb(4 * P, BF),
     "uli": _sb(16, I32), "ul": _sb(16, U16), "yi": _sb(P, I32), "zi": _sb(P, I32), "nz": _sb(P, F32),
     "ma": _sb(P, F32), "d0": _sb(P, F32), "d16": _sb(P, F32), "d4": _sb(128, F32), "x4": _sb(128, F32),
-    "nz4": _sb(128, F32), "ci": _sb(8, I32), "cf": _sb(8, F32), "x16": _sb(16, F32), "lt": _sb(16, F32),
+    "nz4": _sb(128, F32), "ci": _sb(8, I32), "cf": _sb(10, F32), "x16": _sb(16, F32), "lt": _sb(16, F32),
     "ones": _sb(128, F32), "j4": _sb(3 * K + P + K, F32), "jw": _sb(22, F32), "jo": _sb(20, F32), "du": _sb(22, F32),
     "tc": _sb(M, F32), "pg": _sb(M, F32), "i1": _sb(M, F32), "ht": _sb(464, F32),
     "hm": _sb(2 * P, F32), "hh": _sb(2 * P, F32), "junk": _sb(8 * L, BF), "tsum": _sb(40, F32), "rk": _sb(40, F32),
     "rou": _sb(20, U16), "rau": _sb(20, U16), "vz": _sb(P, F32), "so": _sb(P, F32), "sa": _sb(P, F32),
     "sn": _sb(192, F32), "sn2": _sb(P, F32), "sno": _sb(L, F32), "snt": _sb(L, F32), "sna": _sb(NA, F32),
-    "snp": _sb(NA, F32), "snx": _sb(NA, F32), "bl": _sb(16, U16), "zl": _sb(32, U16), "fu": _sb(80, U16),
+    "snp": _sb(NA, F32), "snx": _sb(NA, F32), "bl": _sb(16 * R, U16), "zl": _sb(32, U16), "fu": _sb(80, U16),
     "ou": _sb(10, U16), "au": _sb(8, U16), "pal": _sb(8, U16), "wl": _sb(8, U16), "wx": _sb(8, F32),
     "ptu": _sb(20, U16), "sm": _sb(40, F32), "smi": _sb(80, I32), "blu": _sb(20, U16), "to": _sb(L, F32),
     "tou": _sb(10, U16), "cnt": _sb(8, F32), "cni": _sb(8, I32), "cn": _sb(24, I32), "twu": _sb(20, U16),
@@ -58,7 +60,7 @@ SCRATCH = {
 for _b in range(8):
     SCRATCH["ps%d" % _b] = ("psum", [128, 512], F32)
 NDMA = 16
-SEMAPHORES = ["sV", "sS", "sP", "sG", "sent", "arr0", "arr1", "arr2"] + ["d%d" % i for i in range(NDMA)]
+SEMAPHORES = ["sV", "sS", "sP", "sG", "sent", "arr0", "arr1", "arr2", "win0", "win1", "win2"] + ["d%d" % i for i in range(NDMA)]
 
 
 def v(name, a=0, b=None, s=1):
@@ -106,7 +108,7 @@ def busy(o, lat, far, pick, put):
     vs = [x for x in o["a"] if is_view(x)]
     n, k = width(vs[0]), o["k"]
     if k == "remote":
-        return far
+        return far[0], far[1] + (12 * n if vs[0][1] == "qf" else 0)
     if o["q"] == "G":
         return 150 + 1.7 * n, lat
     if o["q"] == "P":
@@ -213,6 +215,59 @@ def order(ops):
         else:
             grp = {ops[int(i)]["run"]: NOISE * float(rnd.standard_normal()) for i in rnd.integers(0, n, 4)}
             key = [now[2][i] + grp.get(ops[i]["run"], 0.0) for i in range(n)]
+
+    waits = [[[(j, f * c[j][1]) for j, f in pre[i]] for i in range(n)] for c in cases]
+
+    def longest(seq, k):
+        c, before = cases[k], waits[k]
+        done, free, last, why, end, tip = [0.0] * n, [0.0] * 5, [-1] * 5, [None] * n, 0.0, -1
+        for i in seq:
+            q = qi[i]
+            t, w, held = free[q], last[q], True
+            for j, x in before[i]:
+                if done[j] + x > t:
+                    t, w, held = done[j] + x, j, False
+            why[i] = (w, held)
+            done[i] = free[q] = t + c[i][0]
+            last[q] = i
+            if done[i] + c[i][1] > end:
+                end, tip = done[i] + c[i][1], i
+        path = []
+        while tip >= 0:
+            path.append(tip)
+            tip = why[tip][0]
+        return end, [(i, why[i][1]) for i in path[::-1]]
+
+    def moved(seq, u, w, up):
+        a, b = seq.index(u), seq.index(w)
+        take = {w if up else u}
+        for x in (seq[a:b][::-1] if up else seq[a + 1:b + 1]):
+            if any(y in take for y, f in (post if up else pre)[x]):
+                take.add(x)
+        if u in take and w in take:
+            return None
+        mid = seq[a:b + 1]
+        return seq[:a] + [x for x in mid if (x in take) == up] + [x for x in mid if (x in take) != up] + seq[b + 1:]
+
+    seq = best[1]
+    ways = [longest(seq, k) for k in range(len(cases))]
+    end = sum(w[0] * x for w, x in zip(ways, WEIGHT))
+    for p in range(MOVES):
+        path = ways[int(rnd.integers(len(ways)))][1]
+        held = [k for k in range(1, len(path)) if path[k][1]]
+        k = held[int(rnd.integers(len(held)))]
+        a = k - 1
+        while a > 0 and path[a][1] and rnd.random() < 0.6:
+            a -= 1
+        new = moved(seq, path[a][0], path[k][0], rnd.random() < 0.5)
+        if new is None:
+            continue
+        w2 = [longest(new, k) for k in range(len(cases))]
+        e2 = sum(w[0] * x for w, x in zip(w2, WEIGHT))
+        if e2 <= end - HEAT * (1 - p / MOVES) * math.log(1 - rnd.random()):
+            seq, ways, end = new, w2, e2
+            if end < best[0]:
+                best = (end, seq)
     PLAN["end"] = best[0]
     return best[1]
 
@@ -302,8 +357,8 @@ def rank_program(g, core, T, topo):
     def ms(o, c):
         op("V", lambda e: e.memset, [o, c])
 
-    def act(o, i, f=AF.Copy, **kw):
-        op("S", lambda e: e.activation, [o, i, f], kw=kw)
+    def act(o, i, f=AF.Copy, ext=(), **kw):
+        op("S", lambda e: e.activation, [o, i, f], kw=kw, ext=ext)
 
     def quant(c, s, i):
         op("V", lambda e: e.quantize_mx, [c, s, i], nout=2, k="quant")
@@ -321,10 +376,19 @@ def rank_program(g, core, T, topo):
     def dma(q, o, i, after=()):
         op(q, lambda e: e.dma_start, [o, i], dma=True, after=after)
 
-    def fill(name, a, b, c):
-        for lo in range(a, b, 512):
-            hi = min(b, lo + 512)
-            act(v(name, lo, hi), v("zero", 0, hi - lo), AF.Identity, bias=c)
+    def fill(name, a, b, c, s=1, who=None):
+        who = who or WHO.get(name, "S")
+        if who == "V":
+            ms(v(name, a, b, s), c)
+        elif who == "G":
+            iota(v(name, a, b, s), [[0, len(range(a, b, s))]], int(c))
+        else:
+            for lo in range(a, b, 512 * s):
+                hi = min(b, lo + 512 * s)
+                act(v(name, lo, hi, s), v("zero", 0, len(range(lo, hi, s))), AF.Identity, bias=c)
+
+    def lin(o, i, scale, bias):
+        act(o, i, AF.Identity, scale=scale, bias=bias)
 
     def pool(r, a, b, s=1):
         z = 4 * (P + K) * (R - r)
@@ -339,17 +403,13 @@ def rank_program(g, core, T, topo):
     dma("Y", v("vt"), T.v[:], after=[mt])
 
     ms(v("zero"), 0.0)
-    ms(v("bt", 256, 512), 0.0)
-    ms(v("e1"), 1.0)
-    ms(v("fl0"), 0.0)
-    if NFL > 1:
-        fill("fl1", 0, 4 * FW, 0.0)
+    fill("e1", 0, 516, 1.0)
     iota(v("uli"), [[1, 2], [16, 8]])
     iota(v("yi"), [[0, 20], [1, 16]], 128, -1)
     iota(v("ci", 0, 1), [[0, 1]], 0, 1)
     iota(v("x4"), [[0, 32], [1, 4]])
     iota(v("x16"), [[1, 16]])
-    iota(v("jw"), [[16, 22]])
+    iota(v("jw"), [[16, 22]], 3 * K)
     keep(v("kt", 0, 512), v("e1", 0, 512), [[-1, 128], [0, 4]], A.is_equal, 0, 1)
     keep(v("k1", 0, 128), v("e1", 0, 128), [[-16, 8], [0, 16]], A.is_ge, 0, 1)
     keep(v("k1", 128, 256), v("k1", 0, 128), [[16, 8], [0, 16]], A.is_ge, 15, -1)
@@ -364,16 +424,19 @@ def rank_program(g, core, T, topo):
     for k in (0, 1, 3):
         iota(v("tw", TW * k + P, TW * k + HC), [[0, HC - P]])
     iota(v("tw", 2 * TW + P, 2 * TW + P + K), [[0, K]], M)
+    for b in range(4):
+        if b not in H_ADD:
+            fill("rel", P * b + NA, P * b + P, 0.0, who="G")
     fill("ones", 0, 128, 1.0)
     fill("sh", M, M + 16, 1.0)
     fill("ht", 0, 464, 0.0)
     fill("d0", 0, P, -FAR)
-    ms(v("d0", 0, P, 16), 2 * FAR)
-    fill("db", 0, FW, BIG)
-    ms(v("db", 0, 40, 4), 0.0)
-    ms(v("db", 40, 80, 4), -16.0)
-    ms(v("db", 84, FW, 84), -16.0)
-    ms(v("db", 124, FW, 84), -16.0)
+    fill("d0", 0, P, 2 * FAR, 16)
+    fill("db", 0, 128, BIG)
+    fill("db", 0, 64, 0.0, 4)
+    fill("db", 64, 128, -16.0, 4)
+    iota(v("hli"), [[16, 10]], 15)
+    cp(v("hl"), v("hli"))
     cp(v("ul"), v("uli"))
     ts(v("zi"), v("yi"), 15, A.bitwise_and)
     ts(v("nz"), v("zi"), 0.0, A.not_equal)
@@ -382,20 +445,20 @@ def rank_program(g, core, T, topo):
     ts(v("ci", 1, 2), v("ci", 0, 1), 15, A.bitwise_and)
     ts(v("ci", 2, 3), v("ci", 0, 1), 2, A.logical_shift_right, 3, A.bitwise_and)
     ts(v("ci", 3, 4), v("ci", 0, 1), 3, A.bitwise_and)
-    cp(v("cf", 0, 2), v("ci", 1, 3))
-    cp(v("cf", 4, 5), v("ci", 3, 4))
-    ts(v("cf", 2, 3), v("ci", 1, 2), -BIG, A.mult, 15 * BIG, A.add)
-    ts(v("cf", 5, 6), v("ci", 2, 3), -BIG, A.mult, 3 * BIG, A.add)
-    tt(v("cf", 3, 4), v("cf", 5, 6), v("cf", 4, 5), A.subtract)
-    ts(v("cf", 6, 7), v("cf", 5, 6), v("cf", 0, 1), A.add, 176.0, A.add)
+    cp(v("cf", 0, 3), v("ci", 1, 4))
+    lin(v("cf", 4, 5), v("cf", 0, 1), -BIG, 15 * BIG)
+    lin(v("cf", 5, 6), v("cf", 1, 2), -BIG, 3 * BIG)
+    lin(v("cf", 3, 4), v("cf", 2, 3), -1.0, v("cf", 5, 6))
+    lin(v("cf", 8, 9), v("cf", 5, 6), 1.0, 160.0)
+    lin(v("cf", 6, 7), v("cf", 0, 1), 1.0, v("cf", 8, 9))
     ts(v("nz4"), v("x4"), v("cf", 1, 2), A.subtract, 0.0, A.not_equal)
     act(v("d4"), v("nz4"), AF.Identity, scale=HUGE + BIG, bias=-HUGE)
     ts(v("lt"), v("x16"), v("cf", 0, 1), A.is_lt)
-    ts(v("cf", 7, 8), v("ci", 1, 2), 22.0, A.mult, float(PW - P + 1), A.add)
-    ts(v("du"), v("i1", 0, 22), v("cf", 7, 8), A.add)
-    ts(v("jo"), v("jw", 0, 20), v("cf", 0, 1), A.add, float(3 * K), A.add)
+    lin(v("cf", 7, 8), v("cf", 0, 1), 22.0, float(PW - P + 1))
+    lin(v("du"), v("i1", 0, 22), 1.0, v("cf", 7, 8))
+    lin(v("jo"), v("jw", 0, 20), 1.0, v("cf", 0, 1))
     for f in range(3):
-        ts(v("ht", 128 * f + 112, 128 * f + 128), v("zi", 0, 16), 0.0, A.is_equal, float(256 ** f), A.mult)
+        lin(v("ht", 128 * f + 112, 128 * f + 128), v("nz", 0, 16), -float(256 ** f), float(256 ** f))
     for t in range(4):
         ts(v("fu", 20 * t, 20 * t + 20), v("pti"), 4.0, A.mult, float(t), A.add)
     cp(v("ptu"), v("pti"))
@@ -406,59 +469,63 @@ def rank_program(g, core, T, topo):
     def gather_f(r):
         src = mt if r == 0 else pool(r - 1, 0, 4 * PW)
         for t in range(4):
-            (cp if t in F_V[r] else act)(pool(r, t, 4 * P, 4), by(src, v("fu", 20 * t, 20 * t + 20)))
-        quant(v("qf"), v("sf"), pool(r, 0, 4 * P))
+            if r > 0 and t not in H_ADD:
+                tt(pool(r, t, 4 * P, 4), by(v("rel", P * t, P * t + P), v("rau")), v("fk", P * t, P * t + P), A.add)
+            else:
+                (cp if t in F_V[r] else act)(pool(r, t, 4 * P, 4), by(src, v("fu", 20 * t, 20 * t + 20)))
+        quant(v("qf", P * r, P * r + P), v("sf", P * r, P * r + P), pool(r, 0, 4 * P))
 
     def col(x, c):
         return v("hh", P * x + 16 * c + 15, P * x + 16 * c + 16)
 
     def rank_of(x, r, bv, bs, ba, bb):
-        fl, qfl, sfl = "fl%d" % (x % NFL), "qfl%d" % x, "sfl%d" % x
+        fl, qfl, sfl = "fl%d" % x, "qfl%d" % (x % NFL), "sfl%d" % (x % NFL)
         for lo, hi in (((0, L), (L, P)) if x == 0 else ((0, P),)):
             tt(v("hm", P * x + lo, P * x + hi), v("ps%d" % bv, lo, hi), v("ma", lo, hi), A.add)
             scan(v("hh", P * x + lo, P * x + hi), v("d0", lo, hi), v("hm", P * x + lo, P * x + hi), 0.0, A.max, A.min)
-        tt(v(fl, 0, P), v("ps%d" % bv, 0, P), v("hh", P * x, P * x + P), A.is_gt)
+        m = LOW[x]
+        h, e, z = 20 - m, 16 * m, L * x
 
-        def later(row, c, a, b, mine):
-            o = v(fl, P * row + a, P * row + b)
-            if mine:
-                ts(o, v("ps%d" % bv, a, b), col(x, c), A.is_gt)
-            else:
-                act(o, v("ps%d" % bs, a, b), AF.Sign, bias=col(x, c), scale=-1.0)
+        def flags(row, a, b):
+            return v(fl, P * row + a, P * row + b)
 
-        def whole(row, a, b):
-            act(v(fl, P * row + a, P * row + b), v(fl, P * row + a, P * row + b), AF.Relu, scale=-1.0)
-
-        for c in range(10):
-            a, b, e = 16 * c + 16, 16 * c + 160, 16 * c + 176
-            lo, up = c in V_LO[x], c in V_UP[x] or c == 9
-            later(c + 1, c, a, b, lo)
-            if c < 9:
-                later(c + 1, c + 10, e, P, up)
-            if not (lo and up):
-                whole(c + 1, e if lo else a, b if up else P)
-            ts(v(fl, P * (c + 2), P * (c + 2) + a), v("ps%d" % bv, 0, a), col(x, c + 10), A.is_ge)
-        for a, b in zip(CHUNKS, CHUNKS[1:]):
+        tt(flags(9, e, P), v("ps%d" % bv, e, P), v("hh", P * x + e, P * x + P), A.is_gt)
+        tt(flags(10, 0, e), v("ps%d" % bv, 0, e), v("hh", P * x, P * x + e), A.is_gt)
+        for c in [c for c in range(9, -1, -1)] + [c for c in range(10, m)]:
+            a, b, row = 16 * c + 16, min(16 * c + e, P), 9 - c if c < 10 else c
+            act(flags(row, a, b), v("ps%d" % bs, a, b), AF.Sign, bias=col(x, c), scale=-1.0)
+            act(flags(row, a, b), flags(row, a, b), AF.Relu, scale=-1.0, accum_out=v("acc", 20 * x + c, 20 * x + c + 1))
+        if m > 10:
+            lin(v("acc", 20 * x + 10, 20 * x + 11), v("acc", 20 * x + 10, 20 * x + 11), 1.0, 16.0)
+        act(v("hb", z, z + 16 * h), by(v("hh", P * x + e, P * x + P), v("hl", 0, h)))
+        for d in range(h, 0, -1):
+            if d < h:
+                tt(flags(9 - d, e + 16 * d, P), v("ps%d" % bv, e + 16 * d, P), v("hb", z, z + 16 * (h - d)), A.is_gt)
+            tt(flags(10 - d, 0, 16 * d), v("ps%d" % bv, 0, 16 * d), v("hb", z + 16 * (h - d), z + 16 * h), A.is_ge)
+        cut = CHUNKS[m]
+        for a, b in zip(cut, cut[1:]):
             quant(v(qfl, a, b), v(sfl, a, b), v(fl, 4 * a, 4 * b))
-        for k in range(12):
-            mm(ba, 128, "qk", "sk", 128, qfl, sfl, 80 * k, start=k == 0, stop=k == 11, grp=(x, r))
-        z = FW * x
-        for k, (a, b) in enumerate(zip(PIECES, PIECES[1:])):
-            mm(bb[k % 2], b - a, "qk", "sk", 0, qfl, sfl, a)
-            scan(v("bsc", z + a, z + b), v("db", a, b), v("ps%d" % bb[k % 2], 0, b - a), 0.0, A.min, A.add)
-        scan(v("sel", 80 * x, 80 * x + 80), v("d4", 0, 80), v("ps%d" % ba, 0, 80), 0.0, A.add, A.max)
-        tt(v("tsum", 20 * x, 20 * x + 10), v("bsc", z + 119, z + FW, 84), v("bsc", z + 3, z + 40, 4), A.add)
-        tt(v("tsum", 20 * x + 10, 20 * x + 20), v("bsc", z + 163, z + FW, 84), v("bsc", z + 43, z + 80, 4), A.add)
-        tt(v("rk", 20 * x, 20 * x + 20), v("tsum", 20 * x, 20 * x + 20), v("sel", 80 * x + 3, 80 * x + 80, 4), A.subtract)
+        for k in range(11):
+            mm(ba, 128, "qk", "sk", 128, qfl, sfl, 80 * k, start=k == 0, stop=k == 10, grp=(x, r, 0))
+        for d in range(h, -1, -1):
+            mm(bb[0], 128, "qk", "sk", 0, qfl, sfl, 80 * (9 - d) + 4 * (m + d), start=d == h, stop=d == 0, grp=(x, r, 1))
+        mm(bb[1], 128, "qk", "sk", 0, qfl, sfl, 800)
+        z, lo, hi = 80 * x, 64 * (m - 10), 64 * (11 - m)
+        scan(v("bsc", z, z + 4 * m), v("db", lo, lo + 4 * m), v("ps%d" % bb[1], 0, 4 * m), 0.0, A.min, A.add)
+        scan(v("bsc", z + 4 * m, z + 80), v("db", hi, hi + 4 * h), v("ps%d" % bb[0], 0, 4 * h), 0.0, A.min, A.add)
+        scan(v("sel", z, z + 80), v("d4", 0, 80), v("ps%d" % ba, 0, 80), 0.0, A.add, A.max)
+        tt(v("tsum", 20 * x, 20 * x + m), v("bsc", z + 3, z + 4 * m, 4), v("acc", 20 * x, 20 * x + m), A.add)
+        tt(v("rk", 20 * x, 20 * x + m), v("tsum", 20 * x, 20 * x + m), v("sel", z + 3, z + 4 * m, 4), A.subtract)
+        tt(v("rk", 20 * x + m, 20 * x + 20), v("bsc", z + 4 * m + 3, z + 80, 4), v("sel", z + 4 * m + 3, z + 80, 4), A.subtract)
         ts(v("rau" if x else "rou"), v("rk", 20 * x, 20 * x + 20), v("cf", 6, 7), A.add)
 
     def list4(row, a, n, out):
         scan(v("sn", a, a + n), v("d4", 0, n), v(row, 0, n), 0.0, A.add, A.max)
-        ts(v(out), v("sn", a + 3, a + n, 4), v("cf", 3, 4), A.subtract)
+        ts(out, v("sn", a + 3, a + n, 4), v("cf", 3, 4), A.subtract)
 
     def list16(row, n, out, k, tmp):
         scan(v(tmp, 0, n), v("d16", 0, n), row, 0.0, A.add, A.max)
-        ts(out, v(tmp, 15, n, 16), v("cf", 2, 3), A.subtract, k, A.mult)
+        ts(out, v(tmp, 15, n, 16), v("cf", 4, 5), A.subtract, k, A.mult)
 
     def sources():
         ts(v("smi", 0, 20), v("rk", 0, 20), v("cf", 6, 7), A.add, float(512 - L), A.add)
@@ -470,7 +537,7 @@ def rank_program(g, core, T, topo):
         ts(v("smi", 40, 60), v("rk", 20, 40), v("cf", 6, 7), A.add, float(1024 - NA), A.add)
         ts(v("smi", 60, 80), v("smi", 40, 60), 1023, A.bitwise_and)
         tt(v("sm", 20, 40), v("smi", 60, 80), v("sm", 0, 20), A.max)
-        for t in range(4):
+        for t in H_ADD:
             ts(v("fu", 20 * t, 20 * t + 20), v("sm", 20, 40), 4.0, A.mult, float(t - 12 * K), A.add)
         ts(v("tl"), v("sm", 20, 40), float(-3 * K), A.add)
 
@@ -512,7 +579,7 @@ def rank_program(g, core, T, topo):
         tt(v("ix"), v("cs"), v("more"), A.mult)
         scan(v("snx"), v("d16", 0, NA), v("ix"), 0.0, A.add, A.max)
         tt(v("wx"), v("snx", 15, NA, 16), v("sna", 15, NA, 16), A.max)
-        ts(v("wl"), v("wx"), v("cf", 2, 3), A.subtract, 0.25, A.mult)
+        ts(v("wl"), v("wx"), v("cf", 4, 5), A.subtract, 0.25, A.mult)
         act(v("tw", w + HC, w + PW), by(v("tw", w, w + HC), v("wl")))
         act(v("yt", P, 2 * P) if end else v("tw", TW * (r + 1), TW * (r + 1) + P), by(v("tw", w, w + PW), v("tl")))
 
@@ -520,52 +587,58 @@ def rank_program(g, core, T, topo):
     mask = topo.mask(core, nxt)
     neng = len(topo.engines(core, nxt))
 
+    def send(dst, src, arr):
+        op("G", lambda e: e.remote_dma, [ap(T, dst), src, T.sem[arr], T.sem.sent, pid, rid, mask], k="remote", arr=arr)
+
     gather_f(0)
     act(v("tw", 0, P), by(v("tc"), v("ptu")))
     quant(v("qk"), v("sk"), v("kt"))
-    for x in range(2):
-        quant(v("qfl%d" % x, CW - 128, CW), v("sfl%d" % x, CW - 128, CW), v("zero"))
-    quant(v("qland", 0, 128), v("sland", 0, 128), v("zero"))
+    for x in range(NFL):
+        for a in (CW - 128, 0)[:LOW[x] - 9]:
+            quant(v("qfl%d" % x, a, a + 128), v("sfl%d" % x, a, a + 128), v("zero"))
     for b in range(4):
         quant(v("qe", 128 * b, 128 * b + 128), v("se", 128 * b, 128 * b + 128), v("et", 3 - b, 515 - b))
     quant(v("qv"), v("sv"), v("vt"))
     for r in range(R):
+        send(cast(v("qland", P * r, P * r + P), dt.uint8), cast(v("qf", P * r, P * r + P), dt.uint8), "arr%d" % r)
+        send(v("sland", P * r, P * r + P), v("sf", P * r, P * r + P), "arr%d" % r)
         for b in range(4):
-            mm(b, P, "qu2", "su2", 128 * (b // 2), "qf", "sf", 0)
+            mm(b, P, "qu2", "su2", 128 * (b // 2), "qf", "sf", P * r)
         rank_of(0, r, 0, 1, 4, (5, 6))
         cp(by(v("so"), v("rou")), v("j4", 3 * K, 3 * K + P))
-        list4("so", 0, K, "bl")
-        act(v("bt", 0, 256), by(pool(r, 0, 4 * P), v("bl")))
-        quant(v("qb", 128 * r, 128 * r + 128), v("sb", 128 * r, 128 * r + 128), v("bt"))
-        a, arr = 128 + K * r, "arr%d" % r
-        op("G", lambda e: e.remote_dma, [ap(T, cast(v("qland", a, a + K), dt.uint8)), cast(v("qb", 128 * r, 128 * r + K), dt.uint8), T.sem[arr], T.sem.sent, pid, rid, mask], k="remote", arr=arr)
-        op("G", lambda e: e.remote_dma, [ap(T, v("sland", a, a + K)), v("sb", 128 * r, 128 * r + K), T.sem[arr], T.sem.sent, pid, rid, mask], k="remote", arr=arr)
+        list4("so", 0, K, v("bl", 16 * r, 16 * r + 16))
+        send(v("bland", 16 * r, 16 * r + 16), v("bl", 16 * r, 16 * r + 16), "win%d" % r)
+        for b, bank in enumerate((4, 5, 6, 4)):
+            mm(bank, P, "qe", "se", 128 * b, "qland", "sland", P * r, ext=[("arr%d" % r, 2 * neng)])
+            act(v("dall", b, 4 * P, 4), v("ps%d" % bank, 0, P))
+        act(pool(r, 4 * P, 4 * (P + K)), by(v("dall"), v("bland", 16 * r, 16 * r + 16)), ext=[("win%d" % r, neng)])
         sources()
         act(v("vz"), by(v("j4"), v("blu")))
         free_pages(r)
         rank_of(1, r, 2, 3, 7, (0, 1))
-        for b, bank in enumerate((4, 5, 6, 1)):
-            mm(bank, 128, "qe", "se", 128 * b, "qland", "sland", a - K, ext=[(arr, 2 * neng)])
-            act(pool(r, 4 * P + b, 4 * P + 4 * K, 4), v("ps%d" % bank, K, 128))
         cp(by(v("sa"), v("rau")), v("vz"))
-        list4("sa", K, NA, "zl")
+        list4("sa", K, NA, v("zl"))
         if Z_V:
             cp(v("zt", 0, 128 * Z_V), by(pool(r, 0, 4 * (P + K)), v("zl", 0, 8 * Z_V)))
         act(v("zt", 128 * Z_V, 512), by(pool(r, 0, 4 * (P + K)), v("zl", 8 * Z_V, 32)))
         quant(v("qz"), v("sz"), v("zt"))
         for b in range(4):
             mm(4 + b, 128, "qw", "sw", 128 * b, "qz", "sz", 0)
-            act(v("rel", 128 * b, 128 * b + 128), v("ps%d" % (4 + b), 0, 128), AF.Relu, scale=0.03125)
-            tt(pool(r, 4 * HC + b, 4 * PW, 4), v("rel", 128 * b, 128 * b + 128), v("zt", b, 512, 4), A.add)
+            act(v("rel", P * b, P * b + 128), v("ps%d" % (4 + b), 0, 128), AF.Relu, scale=0.03125)
+            if b in H_ADD:
+                tt(pool(r, 4 * HC + b, 4 * PW, 4), v("rel", P * b, P * b + 128), v("zt", b, 512, 4), A.add)
+            else:
+                ts(v("fu", 20 * b, 20 * b + 20), v("sm", 0, 20), 4.0, A.mult, float(b - 12 * K), A.add)
+                act(v("fk", P * b, P * b + P), by(pool(r, 0, 4 * (P + K)), v("fu", 20 * b, 20 * b + 20)))
         next_lists()
         gather_f(r + 1)
         new_tables(r)
 
     for h in range(2):
-        mm(h, L, "qv", "sv", 0, "qf", "sf", L * h)
-    dma("Y", T.oc[:], cast(v("qf"), dt.uint8))
+        mm(h, L, "qv", "sv", 0, "qf", "sf", P * R + L * h)
+    dma("Y", T.oc[:], cast(v("qf", P * R, P * R + P), dt.uint8))
     for k in range(4):
-        dma("Y", T.osc[4 * k:4 * k + 4, :], T.sf[32 * k:32 * k + 4, :], after=[v("sf")])
+        dma("Y", T.osc[4 * k:4 * k + 4, :], T.sf[32 * k:32 * k + 4, P * R:P * R + P], after=[v("sf", P * R, P * R + P)])
     act(v("yt", L, P), v("ps1", 0, L))
     cp(v("yt", 0, L), v("ps0", 0, L))
     dma("S", T.y[:], v("yt", 0, P))
@@ -574,4 +647,4 @@ def rank_program(g, core, T, topo):
     last = emit(g, T, ops)
     for s in sorted(last):
         g.wait_ge(T.sem[s], last[s])
-    g.wait_ge(T.sem.sent, 2 * neng * R)
+    g.wait_ge(T.sem.sent, 3 * neng * R)

@@ -8,20 +8,30 @@ M, P, K, L, NA, R = 352, 320, 64, 160, 128, 3
 HC = 704
 PW = HC + NA
 FW, CW = 880, 928
-TW = 1600
-LOW = [11, 10]
-CHUNKS = {10: [0, 240, 480, 712, 840], 11: [40, 280, 520, 752, 880]}
+TW = 6400
+LOW = [[10, 10], [10, 10], [10, 10]]
+CHUNKS = {10: list(range(0, 841, 140)), 11: list(range(40, 881, 140))}
 F_V = [(0, 1), (), (), ()]
-Z_V = 1
-NFL = 2
-WHO = {"e1": "V", "db": "S", "ht": "S", "ones": "S", "sh": "S", "kt": "S", "d0": "S"}
+Z_V = [2, 2, 2]
+WHO = {"e1": "V", "db": "G", "ht": "G", "ones": "G", "sh": "G", "kt": "S", "d0": "S"}
 H_ADD = (2, 3)
-CASES = [(120, (500, 2000), 1.0, 2.0), (150, (800, 3000), 1.25, 3.15), (130, (1000, 4500), 1.6, 4.6)]
-WEIGHT = [0.3, 0.4, 0.3]
-PASSES, SEED, NOISE, MOVES, HEAT = 2500, 2, 800, 30000, 25.0
+CASES = [(170, (700, 3000, 16, 1700), 1.2, 2.8, 1.25, 1.2), (215, (900, 3400, 16, 1500), 1.3, 3.15, 1.0, 1.1), (180, (800, 3200, 16, 1700), 1.3, 3.15, 1.0, 1.1),
+         (200, (1100, 4200, 22, 1700), 1.3, 3.3, 1.1, 1.2)]
+WEIGHT = [0.25, 0.35, 0.2, 0.2]
+PASSES, SEED, NOISE, MOVES, HEAT = 60, 6, 650, 34000, 36.0
+KIN, SHAKE, BACK, SLACK = 1.0, 2, 10, 150
+EARLY = [1, 1, 1]
+DEAL = [0, 0, 0]
+D_V = 8
+CNT_V = 1
+TIE, TIE_AT, TIE2 = [("wl",)], 3, [[], [("more",)]]
+KT_V = 1
+JUST = 5
+SPLIT = 1
+HB_V = [0, 0]
 BIG = float(2 ** 20)
 HUGE = float(2 ** 25)
-FAR = 1e29
+FAR = 2.0 ** 96
 F32, BF, I32, U16, X4, U8 = "float32", "bfloat16", "int32", "uint16", "float8_e4m3fn_x4", "uint8"
 
 
@@ -37,29 +47,29 @@ SCRATCH = {
     "qland": _sb(R * P, X4), "sland": _sb(R * P, U8), "bland": _sb(16 * R, U16), "dall": _sb(4 * P, BF),
     "qe": _sb(512, X4), "se": _sb(512, U8), "et": _sb(516, BF), "e1": _sb(516, BF), "zero": _sb(512, BF),
     "qk": _sb(256, X4), "sk": _sb(256, U8), "kt": _sb(1024, BF), "k1": _sb(256, BF),
-    "acc": _sb(40, F32), "hb": _sb(2 * L, F32), "hli": _sb(10, I32), "hl": _sb(10, U16),
+    "acc": _sb(40, F32), "hb": _sb(2 * L + 16, F32), "hli": _sb(10, I32), "hl": _sb(10, U16),
     "fl0": _sb(4 * FW, BF), "fl1": _sb(4 * FW, BF), "qfl0": _sb(CW, X4), "sfl0": _sb(CW, U8),
     "qfl1": _sb(CW, X4), "sfl1": _sb(CW, U8), "db": _sb(128, F32), "bsc": _sb(160, F32), "sel": _sb(160, F32),
-    "zt": _sb(512, BF), "rel": _sb(4 * P, F32), "fk": _sb(4 * P, BF),
-    "uli": _sb(16, I32), "ul": _sb(16, U16), "yi": _sb(P, I32), "zi": _sb(P, I32), "nz": _sb(P, F32),
+    "qb": _sb(384, X4), "sb": _sb(384, U8), "zt": _sb(512, BF), "rel": _sb(4 * P, F32), "fk": _sb(4 * P, BF),
+    "uli": _sb(16, I32), "ul": _sb(16, U16), "yi": _sb(80, I32), "zi": _sb(80, I32), "nz": _sb(16, F32),
     "ma": _sb(P, F32), "d0": _sb(P, F32), "d16": _sb(P, F32), "d4": _sb(128, F32), "x4": _sb(128, F32),
-    "nz4": _sb(128, F32), "ci": _sb(8, I32), "cf": _sb(10, F32), "x16": _sb(16, F32), "lt": _sb(16, F32),
-    "ones": _sb(128, F32), "j4": _sb(3 * K + P + K, F32), "jw": _sb(22, F32), "jo": _sb(20, F32), "du": _sb(22, F32),
-    "tc": _sb(M, F32), "pg": _sb(M, F32), "i1": _sb(M, F32), "ht": _sb(464, F32),
+    "nz4": _sb(128, F32), "ci": _sb(8, I32), "cf": _sb(12, F32),
+    "ones": _sb(150, F32), "jw": _sb(22, F32), "jo": _sb(20, F32), "du": _sb(22, F32),
+    "tc": _sb(4 * M, F32), "pg": _sb(M, F32), "i1": _sb(4 * (P + K), F32), "ht": _sb(464, F32),
     "hm": _sb(2 * P, F32), "hh": _sb(2 * P, F32), "junk": _sb(8 * L, BF), "tsum": _sb(40, F32), "rk": _sb(40, F32),
     "rou": _sb(20, U16), "rau": _sb(20, U16), "vz": _sb(P, F32), "so": _sb(P, F32), "sa": _sb(P, F32),
     "sn": _sb(192, F32), "sn2": _sb(P, F32), "sno": _sb(L, F32), "snt": _sb(L, F32), "sna": _sb(NA, F32),
     "snp": _sb(NA, F32), "snx": _sb(NA, F32), "bl": _sb(16 * R, U16), "zl": _sb(32, U16), "fu": _sb(80, U16),
     "ou": _sb(10, U16), "au": _sb(8, U16), "pal": _sb(8, U16), "wl": _sb(8, U16), "wx": _sb(8, F32),
-    "ptu": _sb(20, U16), "sm": _sb(40, F32), "smi": _sb(80, I32), "blu": _sb(20, U16), "to": _sb(L, F32),
-    "tou": _sb(10, U16), "cnt": _sb(8, F32), "cni": _sb(8, I32), "cn": _sb(24, I32), "twu": _sb(20, U16),
+    "sm": _sb(40, F32), "smi": _sb(80, I32), "fv": _sb(80, U16), "to": _sb(L, F32),
+    "tou": _sb(10, U16), "cnt": _sb(24, F32), "cni": _sb(24, I32), "cn": _sb(24, I32), "twu": _sb(20, U16),
     "fr": _sb(96, F32), "shu": _sb(22, U16), "totu": _sb(2, U16), "bs": _sb(24, F32), "posu": _sb(22, U16),
-    "sh": _sb(M + 16, F32), "tw": _sb(4 * TW, F32), "pa": _sb(NA, F32), "more": _sb(NA, F32),
-    "cs": _sb(NA, F32), "ix": _sb(NA, F32), "tl": _sb(20, U16), "yt": _sb(2 * P, F32),
+    "sh": _sb(M + 16, F32), "tw": _sb(2 * TW, F32), "pa": _sb(NA, F32), "more": _sb(NA, F32),
+    "cs": _sb(NA, F32), "ix": _sb(NA, F32), "yt": _sb(2 * P, F32),
 }
 for _b in range(8):
     SCRATCH["ps%d" % _b] = ("psum", [128, 512], F32)
-NDMA = 16
+NDMA = 20
 SEMAPHORES = ["sV", "sS", "sP", "sG", "sent", "arr0", "arr1", "arr2", "win0", "win1", "win2"] + ["d%d" % i for i in range(NDMA)]
 
 
@@ -102,15 +112,17 @@ def width(x):
     return 16 * len(range(x[5][2], x[5][3])) if x[5] is not None else len(range(x[2], x[3], x[4]))
 
 
-def busy(o, lat, far, pick, put):
+def busy(o, lat, far, pick, put, slow=1.0, pe=1.0):
+    if slow * pe != 1.0 and not o["dma"] and o["k"] != "remote":
+        return busy(o, lat, far, pick, put)[0] * (pe if o["q"] == "P" else slow), lat
     if o["dma"]:
-        return 100, 2500
+        return 100, far[3] + o["dma"] / 300
     vs = [x for x in o["a"] if is_view(x)]
     n, k = width(vs[0]), o["k"]
     if k == "remote":
-        return far[0], far[1] + (12 * n if vs[0][1] == "qf" else 0)
+        return far[0], far[1] + (far[2] * n if vs[0][1] == "qf" else 0) + (500 if o["arr"] == "arr0" else 0)
     if o["q"] == "G":
-        return 150 + 1.7 * n, lat
+        return 170 + 1.75 * n, lat
     if o["q"] == "P":
         return 0.6 * (n + 16), lat
     if k == "quant":
@@ -119,12 +131,12 @@ def busy(o, lat, far, pick, put):
     if vs[0][5] is not None:
         return 50 + put * n, lat
     if any(x[5] is not None for x in vs):
-        return 60 + pick * n + extra, lat
+        return (50 if o["q"] == "V" else 65) + pick * n + extra, lat
     if k == "tt" and not any(x[1].startswith("ps") for x in vs):
         n = 2 * n
     elif k != "tt" and o["q"] == "V" and all(SCRATCH[x[1]][2] in (BF, U16) for x in vs[:3]):
         n = n / 2
-    return 20 + 0.83 * max(64, n) + extra, lat
+    return (20 if o["q"] == "V" else 35) + 0.83 * max(64, n) + extra, lat
 
 
 def needs(ops):
@@ -134,7 +146,7 @@ def needs(ops):
         s = set()
         for name, m, wr in mine:
             for j, m2, wr2 in seen.get(name, []):
-                if m & m2 and (wr or wr2 or (name.startswith("ps") and ops[j]["q"] != o["q"])):
+                if m & m2 and (wr or wr2 or (name.startswith("ps") and ops[j]["q"] != o["q"])) and not adds_to(o, ops[j]):
                     s.add(j)
         pre.append(s)
         for name, m, wr in mine:
@@ -191,15 +203,19 @@ def order(ops):
         return seq, end
 
     def length(seq, c):
-        done, free, end = [0.0] * n, [0.0] * 5, 0.0
+        done, free = [0.0] * n, [0.0] * 5
         for i in seq:
-            t = free[qi[i]]
-            for j, f in pre[i]:
-                if done[j] + f * c[j][1] > t:
-                    t = done[j] + f * c[j][1]
-            done[i] = free[qi[i]] = t + c[i][0]
-            end = max(end, done[i] + c[i][1])
-        return end
+            q = qi[i]
+            t = free[q]
+            for j in first_of[i]:
+                if done[j] > t:
+                    t = done[j]
+            d, w = c[i]
+            free[q] = t = t + d
+            done[i] = t + w
+        return max(done)
+
+    first_of = [[j for j, f in p] for p in pre]
 
     rnd = np.random.default_rng(SEED)
     key, best, now = way, None, None
@@ -208,64 +224,68 @@ def order(ops):
         end = sum(length(seq, c) * w for c, w in zip(cases, WEIGHT))
         if best is None or end < best[0]:
             best = (end, seq)
-        if now is None or end <= now[0] + 150 * float(rnd.random()) ** 3:
+        if now is None or end <= now[0] + SLACK * float(rnd.random()) ** 3:
             now = (end, fw, key)
-        if p < 8 or p % 10 == 0:
+        if p < 8 or p % BACK == 0:
             key = place(now[1], post, behind)[1]
         else:
-            grp = {ops[int(i)]["run"]: NOISE * float(rnd.standard_normal()) for i in rnd.integers(0, n, 4)}
-            key = [now[2][i] + grp.get(ops[i]["run"], 0.0) for i in range(n)]
+            by_what = "kin" if rnd.random() < KIN else "run"
+            grp = {ops[int(i)][by_what]: NOISE * float(rnd.standard_normal()) for i in rnd.integers(0, n, SHAKE)}
+            key = [now[2][i] + grp.get(ops[i][by_what], 0.0) for i in range(n)]
 
-    waits = [[[(j, f * c[j][1]) for j, f in pre[i]] for i in range(n)] for c in cases]
+    def lay(key, before, turn):
+        top = list(key)
+        for i in turn:
+            for j, w in before[i]:
+                if top[j] >= top[i]:
+                    top[i] = top[j] + 1e-3
+        first, last, end = [[] for _ in range(5)], [[] for _ in range(5)], [0.0] * n
+        for i in sorted(turn, key=lambda i: top[i]):
+            t, d = (0.0 if before[i] or before is behind else cost[i][1]), cost[i][0]
+            for j, w in before[i]:
+                if end[j] + w > t:
+                    t = end[j] + w
+            s, e = first[qi[i]], last[qi[i]]
+            k = m = len(s)
+            while k > 0 and e[k - 1] > t:
+                k -= 1
+            while k < m and s[k] < t + d - 1e-6:
+                t = e[k]
+                k += 1
+            s.insert(k, t)
+            e.insert(k, t + d)
+            end[i] = t + d
+        return end
 
-    def longest(seq, k):
-        c, before = cases[k], waits[k]
-        done, free, last, why, end, tip = [0.0] * n, [0.0] * 5, [-1] * 5, [None] * n, 0.0, -1
-        for i in seq:
-            q = qi[i]
-            t, w, held = free[q], last[q], True
-            for j, x in before[i]:
-                if done[j] + x > t:
-                    t, w, held = done[j] + x, j, False
-            why[i] = (w, held)
-            done[i] = free[q] = t + c[i][0]
-            last[q] = i
-            if done[i] + c[i][1] > end:
-                end, tip = done[i] + c[i][1], i
-        path = []
-        while tip >= 0:
-            path.append(tip)
-            tip = why[tip][0]
-        return end, [(i, why[i][1]) for i in path[::-1]]
+    def span_of(end):
+        return max(end[i] + cost[i][1] for i in range(n))
 
-    def moved(seq, u, w, up):
-        a, b = seq.index(u), seq.index(w)
-        take = {w if up else u}
-        for x in (seq[a:b][::-1] if up else seq[a + 1:b + 1]):
-            if any(y in take for y, f in (post if up else pre)[x]):
-                take.add(x)
-        if u in take and w in take:
-            return None
-        mid = seq[a:b + 1]
-        return seq[:a] + [x for x in mid if (x in take) == up] + [x for x in mid if (x in take) != up] + seq[b + 1:]
-
-    seq = best[1]
-    ways = [longest(seq, k) for k in range(len(cases))]
-    end = sum(w[0] * x for w, x in zip(ways, WEIGHT))
+    up, down = list(range(n)), list(range(n - 1, -1, -1))
+    loads = sum(1 << i for i in up if ops[i]["dma"])
+    fixed = [i for i in up if not ops[i]["dma"] and not reach[i] & loads]
+    at = [0.0] * n
+    for p, i in enumerate(best[1]):
+        at[i] = p
+    now = lay(at, behind, up)
+    end, was = best[0] + 1000, span_of(now)
     for p in range(MOVES):
-        path = ways[int(rnd.integers(len(ways)))][1]
-        held = [k for k in range(1, len(path)) if path[k][1]]
-        k = held[int(rnd.integers(len(held)))]
-        a = k - 1
-        while a > 0 and path[a][1] and rnd.random() < 0.6:
-            a -= 1
-        new = moved(seq, path[a][0], path[k][0], rnd.random() < 0.5)
-        if new is None:
+        by_what = "kin" if rnd.random() < 0.5 else "run"
+        grp = {ops[int(i)][by_what]: NOISE * float(rnd.standard_normal()) for i in rnd.integers(0, n, SHAKE)}
+        if p % (5 if 4 * p < MOVES else 25) == 2:
+            i = fixed[int(rnd.integers(len(fixed)))]
+            by_what, grp = "run", {ops[j]["run"]: -3 * NOISE * float(rnd.random()) - 500 for j in fixed if j == i or reach[i] >> j & 1}
+        new = lay([now[i] - cost[i][0] + grp.get(ops[i][by_what], 0.0) for i in up], behind, up)
+        if p % JUST == 0:
+            other = lay([-x for x in lay([-x for x in new], ahead, down)], behind, up)
+            if span_of(other) < span_of(new):
+                new = other
+        room, mid = -HEAT * (1 - p / MOVES) * math.log(1 - rnd.random()), span_of(new)
+        if mid > was + 2 * room + 200:
             continue
-        w2 = [longest(new, k) for k in range(len(cases))]
-        e2 = sum(w[0] * x for w, x in zip(w2, WEIGHT))
-        if e2 <= end - HEAT * (1 - p / MOVES) * math.log(1 - rnd.random()):
-            seq, ways, end = new, w2, e2
+        seq = [i for t, i in sorted((new[i] - cost[i][0], i) for i in up)]
+        e2 = sum(length(seq, c) * w if c is not cost else mid * w for c, w in zip(cases, WEIGHT))
+        if e2 <= end + room:
+            now, end, was = new, e2, mid
             if end < best[0]:
                 best = (end, seq)
     PLAN["end"] = best[0]
@@ -282,11 +302,13 @@ def emit(g, T, ops):
     ops = [ops[i] for i in PLAN["order"]]
     qs = {"V": g.vector, "S": g.scalar, "P": g.tensor, "G": g, "Y": g.sync}
     need = set()
+    for o in ops:
+        if o["grp"] is not None:
+            mates = [p for p in ops if adds_to(o, p)]
+            o["a"][5], o["a"][6] = o is mates[0], o is mates[-1]
     for o, pre in zip(ops, PLAN["needs"]):
         deps = {}
         for j in pre:
-            if adds_to(o, ops[j]):
-                continue
             key = ("dma", j) if ops[j]["dma"] else ops[j]["q"]
             deps[key] = max(deps.get(key, j), j)
         o["deps"] = list(deps.values())
@@ -330,7 +352,7 @@ def rank_program(g, core, T, topo):
         return
     nxt = T.cores[(rank + 1) % len(T.cores)]
     ops = []
-    run = ["", 0]
+    run = ["", 0, {}]
 
     def op(q, f, a, nout=1, kw=None, dma=False, ext=(), after=(), k=None, grp=None, arr=None):
         kw = kw or {}
@@ -340,7 +362,9 @@ def rank_program(g, core, T, topo):
         name = w[0][1] if w else ""
         if name != run[0]:
             run[0], run[1] = name, len(ops)
-        ops.append({"q": q, "f": f, "a": a, "kw": kw, "r": r, "w": w, "dma": dma, "ext": ext, "k": k, "run": run[1], "grp": grp, "arr": arr})
+            run[2][name] = run[2].get(name, 0) + 1
+        ops.append({"q": q, "f": f, "a": a, "kw": kw, "r": r, "w": w, "dma": dma, "ext": ext, "k": k, "run": run[1],
+                    "kin": (name, run[2].get(name, 0)), "grp": grp, "arr": arr})
 
     def ts(o, i, s1, op0, s2=None, op1=None):
         op("V", lambda e: e.tensor_scalar, [o, i, s1, s2, op0] + ([] if op1 is None else [op1]))
@@ -348,11 +372,11 @@ def rank_program(g, core, T, topo):
     def tt(o, a, b, f):
         op("V", lambda e: e.tensor_tensor, [o, a, b, f], k="tt")
 
-    def cp(o, i, after=()):
-        op("V", lambda e: e.tensor_copy, [o, i], after=after)
+    def cp(o, i, ext=()):
+        op("V", lambda e: e.tensor_copy, [o, i], ext=ext)
 
-    def scan(o, a, b, init, op0, op1):
-        op("V", lambda e: e.tensor_tensor_scan, [o, a, b, init, op0, op1])
+    def scan(o, a, b, init, op0, op1, after=()):
+        op("V", lambda e: e.tensor_tensor_scan, [o, a, b, init, op0, op1], after=after)
 
     def ms(o, c):
         op("V", lambda e: e.memset, [o, c])
@@ -360,8 +384,8 @@ def rank_program(g, core, T, topo):
     def act(o, i, f=AF.Copy, ext=(), **kw):
         op("S", lambda e: e.activation, [o, i, f], kw=kw, ext=ext)
 
-    def quant(c, s, i):
-        op("V", lambda e: e.quantize_mx, [c, s, i], nout=2, k="quant")
+    def quant(c, s, i, after=()):
+        op("V", lambda e: e.quantize_mx, [c, s, i], nout=2, k="quant", after=after)
 
     def mm(b, n, wq, wsc, wa, xq, xs, xa, ext=(), start=True, stop=True, grp=None):
         op("P", lambda e: e.matmul_mx, [v("ps%d" % b, 0, n), v(wq, wa, wa + 128), v(wsc, wa, wa + 128), v(xq, xa, xa + n), v(xs, xa, xa + n), start, stop], ext=ext, grp=grp)
@@ -373,8 +397,8 @@ def rank_program(g, core, T, topo):
     def keep(o, i, pat, f, base, cm):
         op("G", lambda e: e.affine_select, [o, i, pat, f, 0.0, base, cm])
 
-    def dma(q, o, i, after=()):
-        op(q, lambda e: e.dma_start, [o, i], dma=True, after=after)
+    def dma(q, o, i, after=(), size=1):
+        op(q, lambda e: e.dma_start, [o, i], dma=size, after=after)
 
     def fill(name, a, b, c, s=1, who=None):
         who = who or WHO.get(name, "S")
@@ -395,9 +419,9 @@ def rank_program(g, core, T, topo):
         return v("pool", z + a, z + b, s)
 
     mt = pool(-1, 0, 4 * M)
-    dma("Y", mt, T.m[:])
+    dma("Y", mt, T.m[:], size=1024 * M)
     dma("S", v("pti"), T.pt[:])
-    dma("S", v("ut"), T.u[:])
+    dma("S", v("ut"), T.u[:], size=1024 * 128)
     dma("Y", cast(v("qw"), dt.uint8), T.wc[:], after=[mt])
     dma("Y", v("sw"), T.ws[:], after=[mt])
     dma("Y", v("vt"), T.v[:], after=[mt])
@@ -405,29 +429,29 @@ def rank_program(g, core, T, topo):
     ms(v("zero"), 0.0)
     fill("e1", 0, 516, 1.0)
     iota(v("uli"), [[1, 2], [16, 8]])
-    iota(v("yi"), [[0, 20], [1, 16]], 128, -1)
+    iota(v("yi"), [[0, 5], [1, 16]], 128, -1)
     iota(v("ci", 0, 1), [[0, 1]], 0, 1)
     iota(v("x4"), [[0, 32], [1, 4]])
-    iota(v("x16"), [[1, 16]])
     iota(v("jw"), [[16, 22]], 3 * K)
-    keep(v("kt", 0, 512), v("e1", 0, 512), [[-1, 128], [0, 4]], A.is_equal, 0, 1)
+    keep(v("et"), v("e1"), [[-1, 516]], A.is_equal, 3, 4)
+    if KT_V == 2:
+        keep(v("kt", 0, 512), v("e1", 0, 512), [[-1, 128], [0, 4]], A.is_equal, 0, 1)
+    for b in range(4 if KT_V < 2 else 0):
+        (cp if KT_V else act)(v("kt", b, 512, 4), v("et", 3, 515, 4))
     keep(v("k1", 0, 128), v("e1", 0, 128), [[-16, 8], [0, 16]], A.is_ge, 0, 1)
     keep(v("k1", 128, 256), v("k1", 0, 128), [[16, 8], [0, 16]], A.is_ge, 15, -1)
     fill("kt", 512, 1024, 0.0)
     for b in range(4):
         act(v("kt", 512 + 5 * b, 1024, 16), v("k1", 128 + b, 256, 4))
-    iota(v("i1"), [[1, M]])
+    iota(v("i1", 0, M), [[1, M]])
+    iota(v("i1", M, 4 * (P + K), 4), [[4, P + K - M // 4]], M)
     iota(v("pg"), [[1, 22], [22, 16]])
-    iota(v("j4"), [[4, 3 * K + P + K]], -12 * K)
-    iota(v("tc"), [[1, 16], [16, 22]])
-    keep(v("et"), v("e1"), [[-1, 516]], A.is_equal, 3, 4)
-    for k in (0, 1, 3):
-        iota(v("tw", TW * k + P, TW * k + HC), [[0, HC - P]])
-    iota(v("tw", 2 * TW + P, 2 * TW + P + K), [[0, K]], M)
+    iota(v("tc", 0, 4 * M, 4), [[1, 16], [16, 22]])
     for b in range(4):
         if b not in H_ADD:
             fill("rel", P * b + NA, P * b + P, 0.0, who="G")
     fill("ones", 0, 128, 1.0)
+    fill("ones", 128, 150, 4.0)
     fill("sh", M, M + 16, 1.0)
     fill("ht", 0, 464, 0.0)
     fill("d0", 0, P, -FAR)
@@ -435,13 +459,15 @@ def rank_program(g, core, T, topo):
     fill("db", 0, 128, BIG)
     fill("db", 0, 64, 0.0, 4)
     fill("db", 64, 128, -16.0, 4)
-    iota(v("hli"), [[16, 10]], 15)
-    cp(v("hl"), v("hli"))
+    if not all(HB_V):
+        iota(v("hli"), [[16, 10]], 15)
+        cp(v("hl"), v("hli"))
     cp(v("ul"), v("uli"))
     ts(v("zi"), v("yi"), 15, A.bitwise_and)
-    ts(v("nz"), v("zi"), 0.0, A.not_equal)
-    act(v("ma"), v("nz"), AF.Identity, scale=FAR)
-    act(v("d16"), v("nz"), AF.Identity, scale=HUGE + BIG, bias=-HUGE)
+    ts(v("nz"), v("zi", 0, 16), 0.0, A.not_equal)
+    for a in range(0, P, 80):
+        ts(v("ma", a, a + 80), v("zi"), 0.0, A.not_equal, FAR, A.mult)
+    lin(v("d16"), v("ma"), (HUGE + BIG) / FAR, -HUGE)
     ts(v("ci", 1, 2), v("ci", 0, 1), 15, A.bitwise_and)
     ts(v("ci", 2, 3), v("ci", 0, 1), 2, A.logical_shift_right, 3, A.bitwise_and)
     ts(v("ci", 3, 4), v("ci", 0, 1), 3, A.bitwise_and)
@@ -453,15 +479,16 @@ def rank_program(g, core, T, topo):
     lin(v("cf", 6, 7), v("cf", 0, 1), 1.0, v("cf", 8, 9))
     ts(v("nz4"), v("x4"), v("cf", 1, 2), A.subtract, 0.0, A.not_equal)
     act(v("d4"), v("nz4"), AF.Identity, scale=HUGE + BIG, bias=-HUGE)
-    ts(v("lt"), v("x16"), v("cf", 0, 1), A.is_lt)
-    lin(v("cf", 7, 8), v("cf", 0, 1), 22.0, float(PW - P + 1))
+    lin(v("cf", 9, 10), v("cf", 0, 1), 96.0, 0.0)
+    lin(v("cf", 10, 11), v("cf", 0, 1), 48.0, 48.0)
+    lin(v("cf", 11, 12), v("cf", 0, 1), v("cf", 10, 11), H_ADD[0] - 4.0)
+    lin(v("cf", 7, 8), v("cf", 0, 1), 22.0, float(PW - P + 2))
     lin(v("du"), v("i1", 0, 22), 1.0, v("cf", 7, 8))
     lin(v("jo"), v("jw", 0, 20), 1.0, v("cf", 0, 1))
     for f in range(3):
         lin(v("ht", 128 * f + 112, 128 * f + 128), v("nz", 0, 16), -float(256 ** f), float(256 ** f))
     for t in range(4):
         ts(v("fu", 20 * t, 20 * t + 20), v("pti"), 4.0, A.mult, float(t), A.add)
-    cp(v("ptu"), v("pti"))
     quant(v("qu"), v("su"), v("ut"))
     cp(cast(v("qu2"), dt.uint32), by(cast(v("qu"), dt.uint32), v("ul")))
     act(v("su2"), by(v("su"), v("ul")))
@@ -479,12 +506,13 @@ def rank_program(g, core, T, topo):
         return v("hh", P * x + 16 * c + 15, P * x + 16 * c + 16)
 
     def rank_of(x, r, bv, bs, ba, bb):
-        fl, qfl, sfl = "fl%d" % x, "qfl%d" % (x % NFL), "sfl%d" % (x % NFL)
-        for lo, hi in (((0, L), (L, P)) if x == 0 else ((0, P),)):
+        fl, qfl, sfl = "fl%d" % x, "qfl%d" % x, "sfl%d" % x
+        for lo, hi in (((0, L), (L, P)) if x == 0 and SPLIT else ((0, P),)):
             tt(v("hm", P * x + lo, P * x + hi), v("ps%d" % bv, lo, hi), v("ma", lo, hi), A.add)
-            scan(v("hh", P * x + lo, P * x + hi), v("d0", lo, hi), v("hm", P * x + lo, P * x + hi), 0.0, A.max, A.min)
-        m = LOW[x]
-        h, e, z = 20 - m, 16 * m, L * x
+            scan(v("hh", P * x + lo, P * x + hi), v("d0", lo, hi), v("hm", P * x + lo, P * x + hi), 0.0, A.max, A.min,
+                 [v(*t) for t in TIE2[x]] if r > 0 else [])
+        m = LOW[r][x]
+        h, e, z = 20 - m, 16 * m, L * x + 16
 
         def flags(row, a, b):
             return v(fl, P * row + a, P * row + b)
@@ -497,14 +525,17 @@ def rank_program(g, core, T, topo):
             act(flags(row, a, b), flags(row, a, b), AF.Relu, scale=-1.0, accum_out=v("acc", 20 * x + c, 20 * x + c + 1))
         if m > 10:
             lin(v("acc", 20 * x + 10, 20 * x + 11), v("acc", 20 * x + 10, 20 * x + 11), 1.0, 16.0)
-        act(v("hb", z, z + 16 * h), by(v("hh", P * x + e, P * x + P), v("hl", 0, h)))
+        if HB_V[x]:
+            scan(v("hb", z + 16 * h - 1, z - 1, -1), v("d0", 0, 16 * h), v("hh", P * x + P - 1, P * x + e - 1, -1), 0.0, A.max, A.min)
+        else:
+            act(v("hb", z, z + 16 * h), by(v("hh", P * x + e, P * x + P), v("hl", 0, h)))
         for d in range(h, 0, -1):
             if d < h:
                 tt(flags(9 - d, e + 16 * d, P), v("ps%d" % bv, e + 16 * d, P), v("hb", z, z + 16 * (h - d)), A.is_gt)
             tt(flags(10 - d, 0, 16 * d), v("ps%d" % bv, 0, 16 * d), v("hb", z + 16 * (h - d), z + 16 * h), A.is_ge)
         cut = CHUNKS[m]
         for a, b in zip(cut, cut[1:]):
-            quant(v(qfl, a, b), v(sfl, a, b), v(fl, 4 * a, 4 * b))
+            quant(v(qfl, a, b), v(sfl, a, b), v(fl, 4 * a, 4 * b), [v(*t) for t in TIE] if r > 0 and x == 0 and a == cut[TIE_AT] else [])
         for k in range(11):
             mm(ba, 128, "qk", "sk", 128, qfl, sfl, 80 * k, start=k == 0, stop=k == 10, grp=(x, r, 0))
         for d in range(h, -1, -1):
@@ -514,9 +545,8 @@ def rank_program(g, core, T, topo):
         scan(v("bsc", z, z + 4 * m), v("db", lo, lo + 4 * m), v("ps%d" % bb[1], 0, 4 * m), 0.0, A.min, A.add)
         scan(v("bsc", z + 4 * m, z + 80), v("db", hi, hi + 4 * h), v("ps%d" % bb[0], 0, 4 * h), 0.0, A.min, A.add)
         scan(v("sel", z, z + 80), v("d4", 0, 80), v("ps%d" % ba, 0, 80), 0.0, A.add, A.max)
-        tt(v("tsum", 20 * x, 20 * x + m), v("bsc", z + 3, z + 4 * m, 4), v("acc", 20 * x, 20 * x + m), A.add)
-        tt(v("rk", 20 * x, 20 * x + m), v("tsum", 20 * x, 20 * x + m), v("sel", z + 3, z + 4 * m, 4), A.subtract)
-        tt(v("rk", 20 * x + m, 20 * x + 20), v("bsc", z + 4 * m + 3, z + 80, 4), v("sel", z + 4 * m + 3, z + 80, 4), A.subtract)
+        tt(v("bsc", z + 3, z + 4 * m, 4), v("bsc", z + 3, z + 4 * m, 4), v("acc", 20 * x, 20 * x + m), A.add)
+        tt(v("rk", 20 * x, 20 * x + 20), v("bsc", z + 3, z + 80, 4), v("sel", z + 3, z + 80, 4), A.subtract)
         ts(v("rau" if x else "rou"), v("rk", 20 * x, 20 * x + 20), v("cf", 6, 7), A.add)
 
     def list4(row, a, n, out):
@@ -525,13 +555,15 @@ def rank_program(g, core, T, topo):
 
     def list16(row, n, out, k, tmp):
         scan(v(tmp, 0, n), v("d16", 0, n), row, 0.0, A.add, A.max)
-        ts(out, v(tmp, 15, n, 16), v("cf", 4, 5), A.subtract, k, A.mult)
+        ts(out, v(tmp, 15, n, 16), v("cf", 4, 5), A.subtract, k, A.add)
 
     def sources():
         ts(v("smi", 0, 20), v("rk", 0, 20), v("cf", 6, 7), A.add, float(512 - L), A.add)
         ts(v("smi", 20, 40), v("smi", 0, 20), 512 + K - 1, A.bitwise_and)
         tt(v("sm", 0, 20), v("smi", 20, 40), v("jo"), A.max)
-        cp(v("blu"), v("sm", 0, 20))
+        for t in range(4):
+            if t == 0 or t not in H_ADD:
+                ts(v("fv", 20 * t, 20 * t + 20), v("sm", 0, 20), 4.0, A.mult, float(t - 12 * K), A.add)
 
     def next_lists():
         ts(v("smi", 40, 60), v("rk", 20, 40), v("cf", 6, 7), A.add, float(1024 - NA), A.add)
@@ -539,49 +571,62 @@ def rank_program(g, core, T, topo):
         tt(v("sm", 20, 40), v("smi", 60, 80), v("sm", 0, 20), A.max)
         for t in H_ADD:
             ts(v("fu", 20 * t, 20 * t + 20), v("sm", 20, 40), 4.0, A.mult, float(t - 12 * K), A.add)
-        ts(v("tl"), v("sm", 20, 40), float(-3 * K), A.add)
+
+    TP = H_ADD[0]
+
+    def tw(k, a, b, one=True):
+        z = TW * (k % 2)
+        return v("tw", z + 4 * a + TP, z + 4 * b, 4) if one else v("tw", z + 4 * a, z + 4 * b)
 
     def free_pages(r):
         end = r == R - 1
-        w = TW * (3 if end else r)
-        list16(v("so", 0, L), L, v("ou"), 0.25, "sno")
-        act(v("to"), by(v("tw", TW * r, TW * r + P), v("ou")))
-        list16(v("to"), L, v("tou"), 1.0, "snt")
+        w = 3 if end else r
+        for row, out, k, tmp, dealt in (("so", "ou", float(TP), "sno", DEAL[r] & 1), ("to", "tou", 0.0, "snt", DEAL[r] & 2)):
+            if dealt:
+                dma("Y", v(tmp, 0, 10), T[row][0:128:16, 0:L], after=[v(row, 0, L)])
+                ts(v(out), v(tmp, 0, 10), k, A.add)
+            else:
+                list16(v(row, 0, L), L, v(out), k, tmp)
+            if row == "so":
+                act(v("to"), by(tw(r, 0, P, False), v("ou")))
         for i in range(8):
             act(v("junk", L * i, L * i + L), by(v("ht", 16 * (7 - i), 16 * (7 - i) + M), v("tou")), accum_out=v("cnt", i, i + 1))
-        cp(v("cni"), v("cnt"))
-        ts(v("cn", 0, 8), v("cni"), 255, A.bitwise_and)
-        ts(v("cn", 8, 16), v("cni"), 8, A.logical_shift_right, 255, A.bitwise_and)
-        ts(v("cn", 16, 24), v("cni"), 16, A.logical_shift_right)
+        for f in (1, 2):
+            if CNT_V:
+                ts(v("cni", 8 * f, 8 * f + 8), v("cnt", 0, 8), 256.0 ** -f, A.mult, -0.3125, A.add)
+            else:
+                lin(v("cnt", 8 * f, 8 * f + 8), v("cnt", 0, 8), 256.0 ** -f, -0.3125)
+        cp(v("cni", 0, 8 if CNT_V else 24), v("cnt", 0, 8 if CNT_V else 24))
+        ts(v("cn"), v("cni"), 255, A.bitwise_and)
         ts(v("shu"), v("cn", 0, 22), 1.0, A.not_equal)
-        act(v("sh", 0, M), by(v("i1"), v("shu")))
-        ts(v("fr", 0, 22), v("cn", 0, 22), 0.0, A.is_gt)
-        scan(v("fr", 24, 46), v("ones", 0, 22), v("fr", 0, 22), 0.0, A.add, A.subtract)
+        act(v("sh", 0, M), by(v("i1", 0, M), v("shu")))
+        ts(v("fr", 0, 22), v("cn", 0, 22), 0.0, A.is_gt, 4.0, A.mult)
+        scan(v("fr", 24, 46), v("ones", 128, 150), v("fr", 0, 22), 0.0, A.add, A.subtract)
         tt(v("fr", 48, 70), v("fr", 0, 22), v("du"), A.mult)
-        cp(v("totu", 0, 1), v("fr", 45, 46))
-        tt(v("bs", 0, 16), by(v("i1"), v("totu", 0, 1)), v("lt"), A.mult)
-        op("V", lambda e: e.tensor_reduce, [v("bs", 16, 17), v("bs", 0, 16), AxisListType.X, A.add])
+        ts(v("totu", 0, 1), v("fr", 45, 46), v("cf", 9, 10), A.add)
+        act(v("bs", 0, 16), by(v("i1"), v("totu", 0, 1)), AF.Relu, scale=-1.0, bias=v("cf", 9, 10), accum_out=v("bs", 16, 17))
         tt(v("fr", 72, 94), v("fr", 24, 46), v("fr", 48, 70), A.max)
-        ts(v("posu"), v("fr", 72, 94), v("bs", 16, 17), A.add, -1.0, A.add)
+        ts(v("posu"), v("fr", 72, 94), v("bs", 16, 17), A.subtract, v("cf", 11, 12), A.add)
         if end:
-            list16(v("tw", TW * r, TW * r + P), P, v("twu"), 1.0, "sn2")
-            act(v("tw", w, w + P), by(v("pg"), v("twu")))
-        cp(by(v("tw", w + P, w + TW), v("posu")), v("pg" if end else "i1"))
+            fill("tw", tw(r, P, P + K)[2], tw(r, P, P + K)[3], float(M), 4, "G")
+            list16(tw(r, 0, P), P, v("twu"), 0.0, "sn2")
+            act(tw(w, 0, P), by(v("pg"), v("twu")))
+        cp(by(tw(w, P, TW // 4, False), v("posu")), v("pg") if end else v("i1", 0, M))
 
     def new_tables(r):
         end = r == R - 1
-        w = TW * (3 if end else r)
-        list16(v("sa", 0, NA), NA, v("au"), 0.25, "sna")
-        act(v("pa"), by(v("tw", TW * r, TW * r + P + K), v("au")))
-        list16(v("pa"), NA, v("pal"), 1.0, "snp")
+        w = 3 if end else r
+        list16(v("sa", 0, NA), NA, v("au"), float(TP), "sna")
+        act(v("pa"), by(tw(r, 0, P + K, False), v("au")))
+        list16(v("pa"), NA, v("pal"), 0.0, "snp")
         act(v("more"), by(v("sh"), v("pal")), scale=2.0)
-        scan(v("cs"), v("ones"), v("more"), float(2 * (P + K - 1)), A.mult, A.add)
+        scan(v("cs"), v("ones", 0, NA), v("more"), float(2 * (P + K - 1)), A.mult, A.add)
         tt(v("ix"), v("cs"), v("more"), A.mult)
         scan(v("snx"), v("d16", 0, NA), v("ix"), 0.0, A.add, A.max)
         tt(v("wx"), v("snx", 15, NA, 16), v("sna", 15, NA, 16), A.max)
-        ts(v("wl"), v("wx"), v("cf", 4, 5), A.subtract, 0.25, A.mult)
-        act(v("tw", w + HC, w + PW), by(v("tw", w, w + HC), v("wl")))
-        act(v("yt", P, 2 * P) if end else v("tw", TW * (r + 1), TW * (r + 1) + P), by(v("tw", w, w + PW), v("tl")))
+        ts(v("wl"), v("wx"), v("cf", 4, 5), A.subtract, float(TP), A.add)
+        act(tw(w, HC, PW), by(tw(w, 0, HC, False), v("wl")))
+        act(v("yt", P, 2 * P) if end else tw(r + 1, 0, P), by(tw(w, 0, PW, False), v("fu", 20 * TP, 20 * TP + 20)))
 
     rid, pid, _ = topo.addr(nxt)
     mask = topo.mask(core, nxt)
@@ -591,36 +636,53 @@ def rank_program(g, core, T, topo):
         op("G", lambda e: e.remote_dma, [ap(T, dst), src, T.sem[arr], T.sem.sent, pid, rid, mask], k="remote", arr=arr)
 
     gather_f(0)
-    act(v("tw", 0, P), by(v("tc"), v("ptu")))
+    act(tw(0, 0, P), by(v("tc"), v("fu", 0, 20)))
     quant(v("qk"), v("sk"), v("kt"))
-    for x in range(NFL):
-        for a in (CW - 128, 0)[:LOW[x] - 9]:
+    for x in range(2):
+        for a in (CW - 128, 0)[:LOW[0][x] - 9]:
             quant(v("qfl%d" % x, a, a + 128), v("sfl%d" % x, a, a + 128), v("zero"))
     for b in range(4):
         quant(v("qe", 128 * b, 128 * b + 128), v("se", 128 * b, 128 * b + 128), v("et", 3 - b, 515 - b))
     quant(v("qv"), v("sv"), v("vt"))
     for r in range(R):
-        send(cast(v("qland", P * r, P * r + P), dt.uint8), cast(v("qf", P * r, P * r + P), dt.uint8), "arr%d" % r)
-        send(v("sland", P * r, P * r + P), v("sf", P * r, P * r + P), "arr%d" % r)
+        run[2] = {}
+        if EARLY[r]:
+            send(cast(v("qland", P * r, P * r + P), dt.uint8), cast(v("qf", P * r, P * r + P), dt.uint8), "arr%d" % r)
+            send(v("sland", P * r, P * r + P), v("sf", P * r, P * r + P), "arr%d" % r)
+        elif r == 0:
+            quant(v("qland", 0, 128), v("sland", 0, 128), v("zero"))
+            fill("dall", 4 * K, 512, 0.0, who="G")
         for b in range(4):
             mm(b, P, "qu2", "su2", 128 * (b // 2), "qf", "sf", P * r)
         rank_of(0, r, 0, 1, 4, (5, 6))
-        cp(by(v("so"), v("rou")), v("j4", 3 * K, 3 * K + P))
+        cp(by(v("so"), v("rou")), v("i1", 0, 4 * P, 4))
         list4("so", 0, K, v("bl", 16 * r, 16 * r + 16))
-        send(v("bland", 16 * r, 16 * r + 16), v("bl", 16 * r, 16 * r + 16), "win%d" % r)
-        for b, bank in enumerate((4, 5, 6, 4)):
-            mm(bank, P, "qe", "se", 128 * b, "qland", "sland", P * r, ext=[("arr%d" % r, 2 * neng)])
-            act(v("dall", b, 4 * P, 4), v("ps%d" % bank, 0, P))
-        act(pool(r, 4 * P, 4 * (P + K)), by(v("dall"), v("bland", 16 * r, 16 * r + 16)), ext=[("win%d" % r, neng)])
+        if EARLY[r]:
+            send(v("bland", 16 * r, 16 * r + 16), v("bl", 16 * r, 16 * r + 16), "win%d" % r)
+            for b, bank in enumerate((4, 5, 6, 4)):
+                mm(bank, P, "qe", "se", 128 * b, "qland", "sland", P * r, ext=[("arr%d" % r, 2 * neng)])
+                act(v("dall", b, 4 * P, 4), v("ps%d" % bank, 0, P))
+            if D_V:
+                cp(pool(r, 4 * P, 4 * P + 16 * D_V), by(v("dall"), v("bland", 16 * r, 16 * r + D_V)), ext=[("win%d" % r, neng)])
+            act(pool(r, 4 * P + 16 * D_V, 4 * (P + K)), by(v("dall"), v("bland", 16 * r + D_V, 16 * r + 16)), ext=[("win%d" % r, neng)])
+        else:
+            a = 128 + K * r
+            act(v("dall", 0, 4 * K), by(pool(r, 0, 4 * P), v("bl", 16 * r, 16 * r + 16)))
+            quant(v("qb", 128 * r, 128 * r + 128), v("sb", 128 * r, 128 * r + 128), v("dall", 0, 512))
+            send(cast(v("qland", a, a + K), dt.uint8), cast(v("qb", 128 * r, 128 * r + K), dt.uint8), "arr%d" % r)
+            send(v("sland", a, a + K), v("sb", 128 * r, 128 * r + K), "arr%d" % r)
+            for b, bank in enumerate((4, 5, 6, 4)):
+                mm(bank, 128, "qe", "se", 128 * b, "qland", "sland", a - K, ext=[("arr%d" % r, 2 * neng)])
+                act(pool(r, 4 * P + b, 4 * P + 4 * K, 4), v("ps%d" % bank, K, 128))
         sources()
-        act(v("vz"), by(v("j4"), v("blu")))
+        act(v("vz"), by(v("i1"), v("fv", 0, 20)))
         free_pages(r)
         rank_of(1, r, 2, 3, 7, (0, 1))
         cp(by(v("sa"), v("rau")), v("vz"))
         list4("sa", K, NA, v("zl"))
-        if Z_V:
-            cp(v("zt", 0, 128 * Z_V), by(pool(r, 0, 4 * (P + K)), v("zl", 0, 8 * Z_V)))
-        act(v("zt", 128 * Z_V, 512), by(pool(r, 0, 4 * (P + K)), v("zl", 8 * Z_V, 32)))
+        if Z_V[r]:
+            cp(v("zt", 0, 128 * Z_V[r]), by(pool(r, 0, 4 * (P + K)), v("zl", 0, 8 * Z_V[r])))
+        act(v("zt", 128 * Z_V[r], 512), by(pool(r, 0, 4 * (P + K)), v("zl", 8 * Z_V[r], 32)))
         quant(v("qz"), v("sz"), v("zt"))
         for b in range(4):
             mm(4 + b, 128, "qw", "sw", 128 * b, "qz", "sz", 0)
@@ -628,23 +690,23 @@ def rank_program(g, core, T, topo):
             if b in H_ADD:
                 tt(pool(r, 4 * HC + b, 4 * PW, 4), v("rel", P * b, P * b + 128), v("zt", b, 512, 4), A.add)
             else:
-                ts(v("fu", 20 * b, 20 * b + 20), v("sm", 0, 20), 4.0, A.mult, float(b - 12 * K), A.add)
-                act(v("fk", P * b, P * b + P), by(pool(r, 0, 4 * (P + K)), v("fu", 20 * b, 20 * b + 20)))
+                act(v("fk", P * b, P * b + P), by(pool(r, 0, 4 * (P + K)), v("fv", 20 * b, 20 * b + 20)))
         next_lists()
         gather_f(r + 1)
         new_tables(r)
 
     for h in range(2):
         mm(h, L, "qv", "sv", 0, "qf", "sf", P * R + L * h)
-    dma("Y", T.oc[:], cast(v("qf", P * R, P * R + P), dt.uint8))
+    dma("Y", T.oc[:], cast(v("qf", P * R, P * R + P), dt.uint8), size=512 * P)
     for k in range(4):
         dma("Y", T.osc[4 * k:4 * k + 4, :], T.sf[32 * k:32 * k + 4, P * R:P * R + P], after=[v("sf", P * R, P * R + P)])
     act(v("yt", L, P), v("ps1", 0, L))
     cp(v("yt", 0, L), v("ps0", 0, L))
-    dma("S", T.y[:], v("yt", 0, P))
+    dma("S", T.y[:, L:P], v("yt", L, P), size=512 * L)
+    dma("Y", T.y[:, 0:L], v("yt", 0, L), size=512 * L)
     dma("S", T.om[:], T.yt[0:128:16, P:2 * P], after=[v("yt", P, 2 * P)])
 
     last = emit(g, T, ops)
     for s in sorted(last):
         g.wait_ge(T.sem[s], last[s])
-    g.wait_ge(T.sem.sent, 3 * neng * R)
+    g.wait_ge(T.sem.sent, neng * sum(2 + e for e in EARLY))

import math
import numpy as np
from concourse.mybir import dt, AluOpType, AxisListType, ActivationFunctionType

A = AluOpType
AF = ActivationFunctionType
M, P, K, L, NA, R = 352, 320, 64, 160, 128, 3
HC = 704
PW = HC + NA
FW, CW = 880, 928
TW = 6400
LOW = [[10, 10], [10, 10], [10, 10]]
CHUNKS = {10: list(range(0, 841, 140)), 11: list(range(40, 881, 140))}
F_V = [(0, 1), (), (), ()]
Z_V = [2, 2, 2]
WHO = {"e1": "V", "db": "G", "ht": "G", "ones": "G", "sh": "G", "kt": "S", "d0": "S"}
H_ADD = (2, 3)
CASES = [(170, (700, 3000, 16, 1700), 1.2, 2.8, 1.25, 1.2), (215, (900, 3400, 16, 1500), 1.3, 3.15, 1.0, 1.1), (180, (800, 3200, 16, 1700), 1.3, 3.15, 1.0, 1.1),
         (200, (1100, 4200, 22, 1700), 1.3, 3.3, 1.1, 1.2)]
WEIGHT = [0.25, 0.35, 0.2, 0.2]
PASSES, SEED, NOISE, MOVES, HEAT = 60, 6, 650, 34000, 36.0
KIN, SHAKE, BACK, SLACK = 1.0, 2, 10, 150
EARLY = [1, 1, 1]
DEAL = [0, 0, 0]
D_V = 8
CNT_V = 1
TIE, TIE_AT, TIE2 = [("wl",)], 3, [[], [("more",)]]
KT_V = 1
JUST = 5
SPLIT = 1
HB_V = [0, 0]
BIG = float(2 ** 20)
HUGE = float(2 ** 25)
FAR = 2.0 ** 96
F32, BF, I32, U16, X4, U8 = "float32", "bfloat16", "int32", "uint16", "float8_e4m3fn_x4", "uint8"


def _sb(n, d):
    return ("sbuf", [128, n], d)


SCRATCH = {
    "pool": _sb(4 * (R * (P + K) + PW), BF), "ut": _sb(512, BF), "vt": _sb(512, BF), "pti": _sb(20, I32),
    "qw": _sb(512, X4), "sw": _sb(512, U8), "qu": _sb(128, X4), "su": _sb(128, U8),
    "qu2": _sb(256, X4), "su2": _sb(256, U8), "qv": _sb(128, X4), "sv": _sb(128, U8),
    "qf": _sb(4 * P, X4), "sf": _sb(4 * P, U8), "qz": _sb(128, X4), "sz": _sb(128, U8),
    "qland": _sb(R * P, X4), "sland": _sb(R * P, U8), "bland": _sb(16 * R, U16), "dall": _sb(4 * P, BF),
    "qe": _sb(512, X4), "se": _sb(512, U8), "et": _sb(516, BF), "e1": _sb(516, BF), "zero": _sb(512, BF),
    "qk": _sb(256, X4), "sk": _sb(256, U8), "kt": _sb(1024, BF), "k1": _sb(256, BF),
    "acc": _sb(40, F32), "hb": _sb(2 * L + 16, F32), "hli": _sb(10, I32), "hl": _sb(10, U16),
    "fl0": _sb(4 * FW, BF), "fl1": _sb(4 * FW, BF), "qfl0": _sb(CW, X4), "sfl0": _sb(CW, U8),
    "qfl1": _sb(CW, X4), "sfl1": _sb(CW, U8), "db": _sb(128, F32), "bsc": _sb(160, F32), "sel": _sb(160, F32),
    "qb": _sb(384, X4), "sb": _sb(384, U8), "zt": _sb(512, BF), "rel": _sb(4 * P, F32), "fk": _sb(4 * P, BF),
    "uli": _sb(16, I32), "ul": _sb(16, U16), "yi": _sb(80, I32), "zi": _sb(80, I32), "nz": _sb(16, F32),
    "ma": _sb(P, F32), "d0": _sb(P, F32), "d16": _sb(P, F32), "d4": _sb(128, F32), "x4": _sb(128, F32),
    "nz4": _sb(128, F32), "ci": _sb(8, I32), "cf": _sb(12, F32),
    "ones": _sb(150, F32), "jw": _sb(22, F32), "jo": _sb(20, F32), "du": _sb(22, F32),
    "tc": _sb(4 * M, F32), "pg": _sb(M, F32), "i1": _sb(4 * (P + K), F32), "ht": _sb(464, F32),
    "hm": _sb(2 * P, F32), "hh": _sb(2 * P, F32), "junk": _sb(8 * L, BF), "tsum": _sb(40, F32), "rk": _sb(40, F32),
    "rou": _sb(20, U16), "rau": _sb(20, U16), "vz": _sb(P, F32), "so": _sb(P, F32), "sa": _sb(P, F32),
    "sn": _sb(192, F32), "sn2": _sb(P, F32), "sno": _sb(L, F32), "snt": _sb(L, F32), "sna": _sb(NA, F32),
    "snp": _sb(NA, F32), "snx": _sb(NA, F32), "bl": _sb(16 * R, U16), "zl": _sb(32, U16), "fu": _sb(80, U16),
    "ou": _sb(10, U16), "au": _sb(8, U16), "pal": _sb(8, U16), "wl": _sb(8, U16), "wx": _sb(8, F32),
    "sm": _sb(40, F32), "smi": _sb(80, I32), "fv": _sb(80, U16), "to": _sb(L, F32),
    "tou": _sb(10, U16), "cnt": _sb(24, F32), "cni": _sb(24, I32), "cn": _sb(24, I32), "twu": _sb(20, U16),
    "fr": _sb(96, F32), "shu": _sb(22, U16), "totu": _sb(2, U16), "bs": _sb(24, F32), "posu": _sb(22, U16),
    "sh": _sb(M + 16, F32), "tw": _sb(2 * TW, F32), "pa": _sb(NA, F32), "more": _sb(NA, F32),
    "cs": _sb(NA, F32), "ix": _sb(NA, F32), "yt": _sb(2 * P, F32),
}
for _b in range(8):
    SCRATCH["ps%d" % _b] = ("psum", [128, 512], F32)
NDMA = 20
SEMAPHORES = ["sV", "sS", "sP", "sG", "sent", "arr0", "arr1", "arr2", "win0", "win1", "win2"] + ["d%d" % i for i in range(NDMA)]


def v(name, a=0, b=None, s=1):
    return ("view", name, a, SCRATCH[name][1][1] if b is None else b, s, None, None)


def by(w, off):
    return w[:5] + (off, w[6])


def cast(w, d):
    return w[:6] + (d,)


def is_view(x):
    return isinstance(x, tuple) and len(x) == 7 and x[0] == "view"


def ap(T, x):
    if not is_view(x):
        return x
    r = T[x[1]][:, x[2]:x[3]] if x[4] == 1 else T[x[1]][:, x[2]:x[3]:x[4]]
    if x[6] is not None:
        r = r.bitcast(x[6])
    if x[5] is not None:
        r = r.indirect(ap(T, x[5]))
    return r


def span(x):
    if x[1].startswith("ps"):
        return 1
    if x[4] == 1:
        return ((1 << (x[3] - x[2])) - 1) << x[2]
    return sum(1 << c for c in range(x[2], x[3], x[4]))


def width(x):
    return 16 * len(range(x[5][2], x[5][3])) if x[5] is not None else len(range(x[2], x[3], x[4]))


def busy(o, lat, far, pick, put, slow=1.0, pe=1.0):
    if slow * pe != 1.0 and not o["dma"] and o["k"] != "remote":
        return busy(o, lat, far, pick, put)[0] * (pe if o["q"] == "P" else slow), lat
    if o["dma"]:
        return 100, far[3] + o["dma"] / 300
    vs = [x for x in o["a"] if is_view(x)]
    n, k = width(vs[0]), o["k"]
    if k == "remote":
        return far[0], far[1] + (far[2] * n if vs[0][1] == "qf" else 0) + (500 if o["arr"] == "arr0" else 0)
    if o["q"] == "G":
        return 170 + 1.75 * n, lat
    if o["q"] == "P":
        return 0.6 * (n + 16), lat
    if k == "quant":
        return 12 + 0.88 * n, lat
    extra = 20 if "accum_out" in o["kw"] else 0
    if vs[0][5] is not None:
        return 50 + put * n, lat
    if any(x[5] is not None for x in vs):
        return (50 if o["q"] == "V" else 65) + pick * n + extra, lat
    if k == "tt" and not any(x[1].startswith("ps") for x in vs):
        n = 2 * n
    elif k != "tt" and o["q"] == "V" and all(SCRATCH[x[1]][2] in (BF, U16) for x in vs[:3]):
        n = n / 2
    return (20 if o["q"] == "V" else 35) + 0.83 * max(64, n) + extra, lat


def needs(ops):
    seen, pre = {}, []
    for i, o in enumerate(ops):
        mine = [(x[1], span(x), False) for x in o["r"]] + [(x[1], span(x), True) for x in o["w"]]
        s = set()
        for name, m, wr in mine:
            for j, m2, wr2 in seen.get(name, []):
                if m & m2 and (wr or wr2 or (name.startswith("ps") and ops[j]["q"] != o["q"])) and not adds_to(o, ops[j]):
                    s.add(j)
        pre.append(s)
        for name, m, wr in mine:
            seen.setdefault(name, []).append((i, m, wr))
    return pre


def adds_to(o, p):
    return o["grp"] is not None and o["grp"] == p["grp"]


def order(ops):
    n, pre = len(ops), needs(ops)
    reach = [0] * n
    for i in range(n):
        if ops[i]["ext"]:
            pre[i] |= set(j for j in range(i) if ops[j]["k"] == "remote" and ops[j]["arr"] == ops[i]["ext"][0][0])
        far = 0
        for j in pre[i]:
            far |= reach[j]
        reach[i] = far | sum(1 << j for j in pre[i])
        pre[i] = [j for j in sorted(pre[i]) if not far >> j & 1]
    cases = [[busy(o, *c) for o in ops] for c in CASES]
    cost = cases[1]
    pre = [[(j, 0.0 if adds_to(ops[i], ops[j]) else 1.0) for j in pre[i]] for i in range(n)]
    post = [[] for _ in ops]
    for i in range(n):
        for j, f in pre[i]:
            post[j].append((i, f))
    way = [0.0] * n
    for i in range(n - 1, -1, -1):
        way[i] = cost[i][0] + max([way[j] + f * cost[i][1] for j, f in post[i]] + [cost[i][1]])

    qi = ["VSPGY".index(o["q"]) for o in ops]
    ahead = [[(j, f * cost[i][1]) for j, f in post[i]] for i in range(n)]
    behind = [[(j, f * cost[j][1]) for j, f in pre[i]] for i in range(n)]

    def place(key, before, after):
        left, ready, free = [len(p) for p in before], [0.0] * n, [0.0] * 5
        wait = [[i for i in range(n) if not left[i] and qi[i] == q] for q in range(5)]
        seq, end = [], [0.0] * n
        for _ in range(n):
            t, q = min((max(free[q], min([ready[i] for i in wait[q]])), q) for q in range(5) if wait[q])
            i = max([(key[i], i) for i in wait[q] if ready[i] <= t])[1]
            wait[q].remove(i)
            end[i] = free[q] = t + cost[i][0]
            seq.append(i)
            for j, w in after[i]:
                if end[i] + w > ready[j]:
                    ready[j] = end[i] + w
                left[j] -= 1
                if not left[j]:
                    wait[qi[j]].append(j)
        return seq, end

    def length(seq, c):
        done, free = [0.0] * n, [0.0] * 5
        for i in seq:
            q = qi[i]
            t = free[q]
            for j in first_of[i]:
                if done[j] > t:
                    t = done[j]
            d, w = c[i]
            free[q] = t = t + d
            done[i] = t + w
        return max(done)

    first_of = [[j for j, f in p] for p in pre]

    rnd = np.random.default_rng(SEED)
    key, best, now = way, None, None
    for p in range(PASSES):
        seq, fw = place(key, pre, ahead)
        end = sum(length(seq, c) * w for c, w in zip(cases, WEIGHT))
        if best is None or end < best[0]:
            best = (end, seq)
        if now is None or end <= now[0] + SLACK * float(rnd.random()) ** 3:
            now = (end, fw, key)
        if p < 8 or p % BACK == 0:
            key = place(now[1], post, behind)[1]
        else:
            by_what = "kin" if rnd.random() < KIN else "run"
            grp = {ops[int(i)][by_what]: NOISE * float(rnd.standard_normal()) for i in rnd.integers(0, n, SHAKE)}
            key = [now[2][i] + grp.get(ops[i][by_what], 0.0) for i in range(n)]

    def lay(key, before, turn):
        top = list(key)
        for i in turn:
            for j, w in before[i]:
                if top[j] >= top[i]:
                    top[i] = top[j] + 1e-3
        first, last, end = [[] for _ in range(5)], [[] for _ in range(5)], [0.0] * n
        for i in sorted(turn, key=lambda i: top[i]):
            t, d = (0.0 if before[i] or before is behind else cost[i][1]), cost[i][0]
            for j, w in before[i]:
                if end[j] + w > t:
                    t = end[j] + w
            s, e = first[qi[i]], last[qi[i]]
            k = m = len(s)
            while k > 0 and e[k - 1] > t:
                k -= 1
            while k < m and s[k] < t + d - 1e-6:
                t = e[k]
                k += 1
            s.insert(k, t)
            e.insert(k, t + d)
            end[i] = t + d
        return end

    def span_of(end):
        return max(end[i] + cost[i][1] for i in range(n))

    up, down = list(range(n)), list(range(n - 1, -1, -1))
    loads = sum(1 << i for i in up if ops[i]["dma"])
    fixed = [i for i in up if not ops[i]["dma"] and not reach[i] & loads]
    at = [0.0] * n
    for p, i in enumerate(best[1]):
        at[i] = p
    now = lay(at, behind, up)
    end, was = best[0] + 1000, span_of(now)
    for p in range(MOVES):
        by_what = "kin" if rnd.random() < 0.5 else "run"
        grp = {ops[int(i)][by_what]: NOISE * float(rnd.standard_normal()) for i in rnd.integers(0, n, SHAKE)}
        if p % (5 if 4 * p < MOVES else 25) == 2:
            i = fixed[int(rnd.integers(len(fixed)))]
            by_what, grp = "run", {ops[j]["run"]: -3 * NOISE * float(rnd.random()) - 500 for j in fixed if j == i or reach[i] >> j & 1}
        new = lay([now[i] - cost[i][0] + grp.get(ops[i][by_what], 0.0) for i in up], behind, up)
        if p % JUST == 0:
            other = lay([-x for x in lay([-x for x in new], ahead, down)], behind, up)
            if span_of(other) < span_of(new):
                new = other
        room, mid = -HEAT * (1 - p / MOVES) * math.log(1 - rnd.random()), span_of(new)
        if mid > was + 2 * room + 200:
            continue
        seq = [i for t, i in sorted((new[i] - cost[i][0], i) for i in up)]
        e2 = sum(length(seq, c) * w if c is not cost else mid * w for c, w in zip(cases, WEIGHT))
        if e2 <= end + room:
            now, end, was = new, e2, mid
            if end < best[0]:
                best = (end, seq)
    PLAN["end"] = best[0]
    return best[1]


PLAN = {}


def emit(g, T, ops):
    if "order" not in PLAN:
        PLAN["order"] = order(ops)
        PLAN["needs"] = needs([ops[i] for i in PLAN["order"]])
    ops = [ops[i] for i in PLAN["order"]]
    qs = {"V": g.vector, "S": g.scalar, "P": g.tensor, "G": g, "Y": g.sync}
    need = set()
    for o in ops:
        if o["grp"] is not None:
            mates = [p for p in ops if adds_to(o, p)]
            o["a"][5], o["a"][6] = o is mates[0], o is mates[-1]
    for o, pre in zip(ops, PLAN["needs"]):
        deps = {}
        for j in pre:
            key = ("dma", j) if ops[j]["dma"] else ops[j]["q"]
            deps[key] = max(deps.get(key, j), j)
        o["deps"] = list(deps.values())
        need |= set(o["deps"])
    count = {q: 0 for q in qs}
    known = {q: {} for q in qs}
    nd = 0
    last = {}
    for i, o in enumerate(ops):
        q, kn = o["q"], known[o["q"]]
        for j in sorted(o["deps"], reverse=True):
            s, n = ops[j]["sig"]
            if kn.get(s, 0) < n:
                qs[q].wait_ge(T.sem[s], n)
                kn[s] = n
                for s2, n2 in ops[j]["kn"].items():
                    if kn.get(s2, 0) < n2:
                        kn[s2] = n2
        for s, n in o["ext"]:
            if kn.get(s, 0) < n:
                qs[q].wait_ge(T.sem[s], n)
                kn[s] = n
        o["kn"] = dict(kn)
        ins = o["f"](qs[q])(*[ap(T, x) for x in o["a"]], **{k: ap(T, x) for k, x in o["kw"].items()})
        if o["dma"]:
            o["sig"] = ("d%d" % nd, 16)
            nd += 1
            ins.then_inc(T.sem[o["sig"][0]], 16)
            last[o["sig"][0]] = 16
        elif i in need:
            count[q] += 1
            o["sig"] = ("s" + q, count[q])
            ins.then_inc(T.sem["s" + q], 1)
            last["s" + q] = count[q]
    return last


def rank_program(g, core, T, topo):
    rank = T.rank_of(core)
    if rank is None:
        return
    nxt = T.cores[(rank + 1) % len(T.cores)]
    ops = []
    run = ["", 0, {}]

    def op(q, f, a, nout=1, kw=None, dma=False, ext=(), after=(), k=None, grp=None, arr=None):
        kw = kw or {}
        w = [x for x in a[:nout] if is_view(x)] + [x for n, x in kw.items() if n == "accum_out"]
        r = [x for x in a[nout:] if is_view(x)] + [x for n, x in kw.items() if n != "accum_out" and is_view(x)] + list(after)
        r += [x[5] for x in r + w if x[5] is not None]
        name = w[0][1] if w else ""
        if name != run[0]:
            run[0], run[1] = name, len(ops)
            run[2][name] = run[2].get(name, 0) + 1
        ops.append({"q": q, "f": f, "a": a, "kw": kw, "r": r, "w": w, "dma": dma, "ext": ext, "k": k, "run": run[1],
                    "kin": (name, run[2].get(name, 0)), "grp": grp, "arr": arr})

    def ts(o, i, s1, op0, s2=None, op1=None):
        op("V", lambda e: e.tensor_scalar, [o, i, s1, s2, op0] + ([] if op1 is None else [op1]))

    def tt(o, a, b, f):
        op("V", lambda e: e.tensor_tensor, [o, a, b, f], k="tt")

    def cp(o, i, ext=()):
        op("V", lambda e: e.tensor_copy, [o, i], ext=ext)

    def scan(o, a, b, init, op0, op1, after=()):
        op("V", lambda e: e.tensor_tensor_scan, [o, a, b, init, op0, op1], after=after)

    def ms(o, c):
        op("V", lambda e: e.memset, [o, c])

    def act(o, i, f=AF.Copy, ext=(), **kw):
        op("S", lambda e: e.activation, [o, i, f], kw=kw, ext=ext)

    def quant(c, s, i, after=()):
        op("V", lambda e: e.quantize_mx, [c, s, i], nout=2, k="quant", after=after)

    def mm(b, n, wq, wsc, wa, xq, xs, xa, ext=(), start=True, stop=True, grp=None):
        op("P", lambda e: e.matmul_mx, [v("ps%d" % b, 0, n), v(wq, wa, wa + 128), v(wsc, wa, wa + 128), v(xq, xa, xa + n), v(xs, xa, xa + n), start, stop], ext=ext, grp=grp)

    def iota(o, pat, base=0, cm=0):
        kw = {} if SCRATCH[o[1]][2] == I32 else {"allow_small_or_imprecise_dtypes": True}
        op("G", lambda e: e.iota, [o, pat, base, cm], kw=kw)

    def keep(o, i, pat, f, base, cm):
        op("G", lambda e: e.affine_select, [o, i, pat, f, 0.0, base, cm])

    def dma(q, o, i, after=(), size=1):
        op(q, lambda e: e.dma_start, [o, i], dma=size, after=after)

    def fill(name, a, b, c, s=1, who=None):
        who = who or WHO.get(name, "S")
        if who == "V":
            ms(v(name, a, b, s), c)
        elif who == "G":
            iota(v(name, a, b, s), [[0, len(range(a, b, s))]], int(c))
        else:
            for lo in range(a, b, 512 * s):
                hi = min(b, lo + 512 * s)
                act(v(name, lo, hi, s), v("zero", 0, len(range(lo, hi, s))), AF.Identity, bias=c)

    def lin(o, i, scale, bias):
        act(o, i, AF.Identity, scale=scale, bias=bias)

    def pool(r, a, b, s=1):
        z = 4 * (P + K) * (R - r)
        return v("pool", z + a, z + b, s)

    mt = pool(-1, 0, 4 * M)
    dma("Y", mt, T.m[:], size=1024 * M)
    dma("S", v("pti"), T.pt[:])
    dma("S", v("ut"), T.u[:], size=1024 * 128)
    dma("Y", cast(v("qw"), dt.uint8), T.wc[:], after=[mt])
    dma("Y", v("sw"), T.ws[:], after=[mt])
    dma("Y", v("vt"), T.v[:], after=[mt])

    ms(v("zero"), 0.0)
    fill("e1", 0, 516, 1.0)
    iota(v("uli"), [[1, 2], [16, 8]])
    iota(v("yi"), [[0, 5], [1, 16]], 128, -1)
    iota(v("ci", 0, 1), [[0, 1]], 0, 1)
    iota(v("x4"), [[0, 32], [1, 4]])
    iota(v("jw"), [[16, 22]], 3 * K)
    keep(v("et"), v("e1"), [[-1, 516]], A.is_equal, 3, 4)
    if KT_V == 2:
        keep(v("kt", 0, 512), v("e1", 0, 512), [[-1, 128], [0, 4]], A.is_equal, 0, 1)
    for b in range(4 if KT_V < 2 else 0):
        (cp if KT_V else act)(v("kt", b, 512, 4), v("et", 3, 515, 4))
    keep(v("k1", 0, 128), v("e1", 0, 128), [[-16, 8], [0, 16]], A.is_ge, 0, 1)
    keep(v("k1", 128, 256), v("k1", 0, 128), [[16, 8], [0, 16]], A.is_ge, 15, -1)
    fill("kt", 512, 1024, 0.0)
    for b in range(4):
        act(v("kt", 512 + 5 * b, 1024, 16), v("k1", 128 + b, 256, 4))
    iota(v("i1", 0, M), [[1, M]])
    iota(v("i1", M, 4 * (P + K), 4), [[4, P + K - M // 4]], M)
    iota(v("pg"), [[1, 22], [22, 16]])
    iota(v("tc", 0, 4 * M, 4), [[1, 16], [16, 22]])
    for b in range(4):
        if b not in H_ADD:
            fill("rel", P * b + NA, P * b + P, 0.0, who="G")
    fill("ones", 0, 128, 1.0)
    fill("ones", 128, 150, 4.0)
    fill("sh", M, M + 16, 1.0)
    fill("ht", 0, 464, 0.0)
    fill("d0", 0, P, -FAR)
    fill("d0", 0, P, 2 * FAR, 16)
    fill("db", 0, 128, BIG)
    fill("db", 0, 64, 0.0, 4)
    fill("db", 64, 128, -16.0, 4)
    if not all(HB_V):
        iota(v("hli"), [[16, 10]], 15)
        cp(v("hl"), v("hli"))
    cp(v("ul"), v("uli"))
    ts(v("zi"), v("yi"), 15, A.bitwise_and)
    ts(v("nz"), v("zi", 0, 16), 0.0, A.not_equal)
    for a in range(0, P, 80):
        ts(v("ma", a, a + 80), v("zi"), 0.0, A.not_equal, FAR, A.mult)
    lin(v("d16"), v("ma"), (HUGE + BIG) / FAR, -HUGE)
    ts(v("ci", 1, 2), v("ci", 0, 1), 15, A.bitwise_and)
    ts(v("ci", 2, 3), v("ci", 0, 1), 2, A.logical_shift_right, 3, A.bitwise_and)
    ts(v("ci", 3, 4), v("ci", 0, 1), 3, A.bitwise_and)
    cp(v("cf", 0, 3), v("ci", 1, 4))
    lin(v("cf", 4, 5), v("cf", 0, 1), -BIG, 15 * BIG)
    lin(v("cf", 5, 6), v("cf", 1, 2), -BIG, 3 * BIG)
    lin(v("cf", 3, 4), v("cf", 2, 3), -1.0, v("cf", 5, 6))
    lin(v("cf", 8, 9), v("cf", 5, 6), 1.0, 160.0)
    lin(v("cf", 6, 7), v("cf", 0, 1), 1.0, v("cf", 8, 9))
    ts(v("nz4"), v("x4"), v("cf", 1, 2), A.subtract, 0.0, A.not_equal)
    act(v("d4"), v("nz4"), AF.Identity, scale=HUGE + BIG, bias=-HUGE)
    lin(v("cf", 9, 10), v("cf", 0, 1), 96.0, 0.0)
    lin(v("cf", 10, 11), v("cf", 0, 1), 48.0, 48.0)
    lin(v("cf", 11, 12), v("cf", 0, 1), v("cf", 10, 11), H_ADD[0] - 4.0)
    lin(v("cf", 7, 8), v("cf", 0, 1), 22.0, float(PW - P + 2))
    lin(v("du"), v("i1", 0, 22), 1.0, v("cf", 7, 8))
    lin(v("jo"), v("jw", 0, 20), 1.0, v("cf", 0, 1))
    for f in range(3):
        lin(v("ht", 128 * f + 112, 128 * f + 128), v("nz", 0, 16), -float(256 ** f), float(256 ** f))
    for t in range(4):
        ts(v("fu", 20 * t, 20 * t + 20), v("pti"), 4.0, A.mult, float(t), A.add)
    quant(v("qu"), v("su"), v("ut"))
    cp(cast(v("qu2"), dt.uint32), by(cast(v("qu"), dt.uint32), v("ul")))
    act(v("su2"), by(v("su"), v("ul")))

    def gather_f(r):
        src = mt if r == 0 else pool(r - 1, 0, 4 * PW)
        for t in range(4):
            if r > 0 and t not in H_ADD:
                tt(pool(r, t, 4 * P, 4), by(v("rel", P * t, P * t + P), v("rau")), v("fk", P * t, P * t + P), A.add)
            else:
                (cp if t in F_V[r] else act)(pool(r, t, 4 * P, 4), by(src, v("fu", 20 * t, 20 * t + 20)))
        quant(v("qf", P * r, P * r + P), v("sf", P * r, P * r + P), pool(r, 0, 4 * P))

    def col(x, c):
        return v("hh", P * x + 16 * c + 15, P * x + 16 * c + 16)

    def rank_of(x, r, bv, bs, ba, bb):
        fl, qfl, sfl = "fl%d" % x, "qfl%d" % x, "sfl%d" % x
        for lo, hi in (((0, L), (L, P)) if x == 0 and SPLIT else ((0, P),)):
            tt(v("hm", P * x + lo, P * x + hi), v("ps%d" % bv, lo, hi), v("ma", lo, hi), A.add)
            scan(v("hh", P * x + lo, P * x + hi), v("d0", lo, hi), v("hm", P * x + lo, P * x + hi), 0.0, A.max, A.min,
                 [v(*t) for t in TIE2[x]] if r > 0 else [])
        m = LOW[r][x]
        h, e, z = 20 - m, 16 * m, L * x + 16

        def flags(row, a, b):
            return v(fl, P * row + a, P * row + b)

        tt(flags(9, e, P), v("ps%d" % bv, e, P), v("hh", P * x + e, P * x + P), A.is_gt)
        tt(flags(10, 0, e), v("ps%d" % bv, 0, e), v("hh", P * x, P * x + e), A.is_gt)
        for c in [c for c in range(9, -1, -1)] + [c for c in range(10, m)]:
            a, b, row = 16 * c + 16, min(16 * c + e, P), 9 - c if c < 10 else c
            act(flags(row, a, b), v("ps%d" % bs, a, b), AF.Sign, bias=col(x, c), scale=-1.0)
            act(flags(row, a, b), flags(row, a, b), AF.Relu, scale=-1.0, accum_out=v("acc", 20 * x + c, 20 * x + c + 1))
        if m > 10:
            lin(v("acc", 20 * x + 10, 20 * x + 11), v("acc", 20 * x + 10, 20 * x + 11), 1.0, 16.0)
        if HB_V[x]:
            scan(v("hb", z + 16 * h - 1, z - 1, -1), v("d0", 0, 16 * h), v("hh", P * x + P - 1, P * x + e - 1, -1), 0.0, A.max, A.min)
        else:
            act(v("hb", z, z + 16 * h), by(v("hh", P * x + e, P * x + P), v("hl", 0, h)))
        for d in range(h, 0, -1):
            if d < h:
                tt(flags(9 - d, e + 16 * d, P), v("ps%d" % bv, e + 16 * d, P), v("hb", z, z + 16 * (h - d)), A.is_gt)
            tt(flags(10 - d, 0, 16 * d), v("ps%d" % bv, 0, 16 * d), v("hb", z + 16 * (h - d), z + 16 * h), A.is_ge)
        cut = CHUNKS[m]
        for a, b in zip(cut, cut[1:]):
            quant(v(qfl, a, b), v(sfl, a, b), v(fl, 4 * a, 4 * b), [v(*t) for t in TIE] if r > 0 and x == 0 and a == cut[TIE_AT] else [])
        for k in range(11):
            mm(ba, 128, "qk", "sk", 128, qfl, sfl, 80 * k, start=k == 0, stop=k == 10, grp=(x, r, 0))
        for d in range(h, -1, -1):
            mm(bb[0], 128, "qk", "sk", 0, qfl, sfl, 80 * (9 - d) + 4 * (m + d), start=d == h, stop=d == 0, grp=(x, r, 1))
        mm(bb[1], 128, "qk", "sk", 0, qfl, sfl, 800)
        z, lo, hi = 80 * x, 64 * (m - 10), 64 * (11 - m)
        scan(v("bsc", z, z + 4 * m), v("db", lo, lo + 4 * m), v("ps%d" % bb[1], 0, 4 * m), 0.0, A.min, A.add)
        scan(v("bsc", z + 4 * m, z + 80), v("db", hi, hi + 4 * h), v("ps%d" % bb[0], 0, 4 * h), 0.0, A.min, A.add)
        scan(v("sel", z, z + 80), v("d4", 0, 80), v("ps%d" % ba, 0, 80), 0.0, A.add, A.max)
        tt(v("bsc", z + 3, z + 4 * m, 4), v("bsc", z + 3, z + 4 * m, 4), v("acc", 20 * x, 20 * x + m), A.add)
        tt(v("rk", 20 * x, 20 * x + 20), v("bsc", z + 3, z + 80, 4), v("sel", z + 3, z + 80, 4), A.subtract)
        ts(v("rau" if x else "rou"), v("rk", 20 * x, 20 * x + 20), v("cf", 6, 7), A.add)

    def list4(row, a, n, out):
        scan(v("sn", a, a + n), v("d4", 0, n), v(row, 0, n), 0.0, A.add, A.max)
        ts(out, v("sn", a + 3, a + n, 4), v("cf", 3, 4), A.subtract)

    def list16(row, n, out, k, tmp):
        scan(v(tmp, 0, n), v("d16", 0, n), row, 0.0, A.add, A.max)
        ts(out, v(tmp, 15, n, 16), v("cf", 4, 5), A.subtract, k, A.add)

    def sources():
        ts(v("smi", 0, 20), v("rk", 0, 20), v("cf", 6, 7), A.add, float(512 - L), A.add)
        ts(v("smi", 20, 40), v("smi", 0, 20), 512 + K - 1, A.bitwise_and)
        tt(v("sm", 0, 20), v("smi", 20, 40), v("jo"), A.max)
        for t in range(4):
            if t == 0 or t not in H_ADD:
                ts(v("fv", 20 * t, 20 * t + 20), v("sm", 0, 20), 4.0, A.mult, float(t - 12 * K), A.add)

    def next_lists():
        ts(v("smi", 40, 60), v("rk", 20, 40), v("cf", 6, 7), A.add, float(1024 - NA), A.add)
        ts(v("smi", 60, 80), v("smi", 40, 60), 1023, A.bitwise_and)
        tt(v("sm", 20, 40), v("smi", 60, 80), v("sm", 0, 20), A.max)
        for t in H_ADD:
            ts(v("fu", 20 * t, 20 * t + 20), v("sm", 20, 40), 4.0, A.mult, float(t - 12 * K), A.add)

    TP = H_ADD[0]

    def tw(k, a, b, one=True):
        z = TW * (k % 2)
        return v("tw", z + 4 * a + TP, z + 4 * b, 4) if one else v("tw", z + 4 * a, z + 4 * b)

    def free_pages(r):
        end = r == R - 1
        w = 3 if end else r
        for row, out, k, tmp, dealt in (("so", "ou", float(TP), "sno", DEAL[r] & 1), ("to", "tou", 0.0, "snt", DEAL[r] & 2)):
            if dealt:
                dma("Y", v(tmp, 0, 10), T[row][0:128:16, 0:L], after=[v(row, 0, L)])
                ts(v(out), v(tmp, 0, 10), k, A.add)
            else:
                list16(v(row, 0, L), L, v(out), k, tmp)
            if row == "so":
                act(v("to"), by(tw(r, 0, P, False), v("ou")))
        for i in range(8):
            act(v("junk", L * i, L * i + L), by(v("ht", 16 * (7 - i), 16 * (7 - i) + M), v("tou")), accum_out=v("cnt", i, i + 1))
        for f in (1, 2):
            if CNT_V:
                ts(v("cni", 8 * f, 8 * f + 8), v("cnt", 0, 8), 256.0 ** -f, A.mult, -0.3125, A.add)
            else:
                lin(v("cnt", 8 * f, 8 * f + 8), v("cnt", 0, 8), 256.0 ** -f, -0.3125)
        cp(v("cni", 0, 8 if CNT_V else 24), v("cnt", 0, 8 if CNT_V else 24))
        ts(v("cn"), v("cni"), 255, A.bitwise_and)
        ts(v("shu"), v("cn", 0, 22), 1.0, A.not_equal)
        act(v("sh", 0, M), by(v("i1", 0, M), v("shu")))
        ts(v("fr", 0, 22), v("cn", 0, 22), 0.0, A.is_gt, 4.0, A.mult)
        scan(v("fr", 24, 46), v("ones", 128, 150), v("fr", 0, 22), 0.0, A.add, A.subtract)
        tt(v("fr", 48, 70), v("fr", 0, 22), v("du"), A.mult)
        ts(v("totu", 0, 1), v("fr", 45, 46), v("cf", 9, 10), A.add)
        act(v("bs", 0, 16), by(v("i1"), v("totu", 0, 1)), AF.Relu, scale=-1.0, bias=v("cf", 9, 10), accum_out=v("bs", 16, 17))
        tt(v("fr", 72, 94), v("fr", 24, 46), v("fr", 48, 70), A.max)
        ts(v("posu"), v("fr", 72, 94), v("bs", 16, 17), A.subtract, v("cf", 11, 12), A.add)
        if end:
            fill("tw", tw(r, P, P + K)[2], tw(r, P, P + K)[3], float(M), 4, "G")
            list16(tw(r, 0, P), P, v("twu"), 0.0, "sn2")
            act(tw(w, 0, P), by(v("pg"), v("twu")))
        cp(by(tw(w, P, TW // 4, False), v("posu")), v("pg") if end else v("i1", 0, M))

    def new_tables(r):
        end = r == R - 1
        w = 3 if end else r
        list16(v("sa", 0, NA), NA, v("au"), float(TP), "sna")
        act(v("pa"), by(tw(r, 0, P + K, False), v("au")))
        list16(v("pa"), NA, v("pal"), 0.0, "snp")
        act(v("more"), by(v("sh"), v("pal")), scale=2.0)
        scan(v("cs"), v("ones", 0, NA), v("more"), float(2 * (P + K - 1)), A.mult, A.add)
        tt(v("ix"), v("cs"), v("more"), A.mult)
        scan(v("snx"), v("d16", 0, NA), v("ix"), 0.0, A.add, A.max)
        tt(v("wx"), v("snx", 15, NA, 16), v("sna", 15, NA, 16), A.max)
        ts(v("wl"), v("wx"), v("cf", 4, 5), A.subtract, float(TP), A.add)
        act(tw(w, HC, PW), by(tw(w, 0, HC, False), v("wl")))
        act(v("yt", P, 2 * P) if end else tw(r + 1, 0, P), by(tw(w, 0, PW, False), v("fu", 20 * TP, 20 * TP + 20)))

    rid, pid, _ = topo.addr(nxt)
    mask = topo.mask(core, nxt)
    neng = len(topo.engines(core, nxt))

    def send(dst, src, arr):
        op("G", lambda e: e.remote_dma, [ap(T, dst), src, T.sem[arr], T.sem.sent, pid, rid, mask], k="remote", arr=arr)

    gather_f(0)
    act(tw(0, 0, P), by(v("tc"), v("fu", 0, 20)))
    quant(v("qk"), v("sk"), v("kt"))
    for x in range(2):
        for a in (CW - 128, 0)[:LOW[0][x] - 9]:
            quant(v("qfl%d" % x, a, a + 128), v("sfl%d" % x, a, a + 128), v("zero"))
    for b in range(4):
        quant(v("qe", 128 * b, 128 * b + 128), v("se", 128 * b, 128 * b + 128), v("et", 3 - b, 515 - b))
    quant(v("qv"), v("sv"), v("vt"))
    for r in range(R):
        run[2] = {}
        if EARLY[r]:
            send(cast(v("qland", P * r, P * r + P), dt.uint8), cast(v("qf", P * r, P * r + P), dt.uint8), "arr%d" % r)
            send(v("sland", P * r, P * r + P), v("sf", P * r, P * r + P), "arr%d" % r)
        elif r == 0:
            quant(v("qland", 0, 128), v("sland", 0, 128), v("zero"))
            fill("dall", 4 * K, 512, 0.0, who="G")
        for b in range(4):
            mm(b, P, "qu2", "su2", 128 * (b // 2), "qf", "sf", P * r)
        rank_of(0, r, 0, 1, 4, (5, 6))
        cp(by(v("so"), v("rou")), v("i1", 0, 4 * P, 4))
        list4("so", 0, K, v("bl", 16 * r, 16 * r + 16))
        if EARLY[r]:
            send(v("bland", 16 * r, 16 * r + 16), v("bl", 16 * r, 16 * r + 16), "win%d" % r)
            for b, bank in enumerate((4, 5, 6, 4)):
                mm(bank, P, "qe", "se", 128 * b, "qland", "sland", P * r, ext=[("arr%d" % r, 2 * neng)])
                act(v("dall", b, 4 * P, 4), v("ps%d" % bank, 0, P))
            if D_V:
                cp(pool(r, 4 * P, 4 * P + 16 * D_V), by(v("dall"), v("bland", 16 * r, 16 * r + D_V)), ext=[("win%d" % r, neng)])
            act(pool(r, 4 * P + 16 * D_V, 4 * (P + K)), by(v("dall"), v("bland", 16 * r + D_V, 16 * r + 16)), ext=[("win%d" % r, neng)])
        else:
            a = 128 + K * r
            act(v("dall", 0, 4 * K), by(pool(r, 0, 4 * P), v("bl", 16 * r, 16 * r + 16)))
            quant(v("qb", 128 * r, 128 * r + 128), v("sb", 128 * r, 128 * r + 128), v("dall", 0, 512))
            send(cast(v("qland", a, a + K), dt.uint8), cast(v("qb", 128 * r, 128 * r + K), dt.uint8), "arr%d" % r)
            send(v("sland", a, a + K), v("sb", 128 * r, 128 * r + K), "arr%d" % r)
            for b, bank in enumerate((4, 5, 6, 4)):
                mm(bank, 128, "qe", "se", 128 * b, "qland", "sland", a - K, ext=[("arr%d" % r, 2 * neng)])
                act(pool(r, 4 * P + b, 4 * P + 4 * K, 4), v("ps%d" % bank, K, 128))
        sources()
        act(v("vz"), by(v("i1"), v("fv", 0, 20)))
        free_pages(r)
        rank_of(1, r, 2, 3, 7, (0, 1))
        cp(by(v("sa"), v("rau")), v("vz"))
        list4("sa", K, NA, v("zl"))
        if Z_V[r]:
            cp(v("zt", 0, 128 * Z_V[r]), by(pool(r, 0, 4 * (P + K)), v("zl", 0, 8 * Z_V[r])))
        act(v("zt", 128 * Z_V[r], 512), by(pool(r, 0, 4 * (P + K)), v("zl", 8 * Z_V[r], 32)))
        quant(v("qz"), v("sz"), v("zt"))
        for b in range(4):
            mm(4 + b, 128, "qw", "sw", 128 * b, "qz", "sz", 0)
            act(v("rel", P * b, P * b + 128), v("ps%d" % (4 + b), 0, 128), AF.Relu, scale=0.03125)
            if b in H_ADD:
                tt(pool(r, 4 * HC + b, 4 * PW, 4), v("rel", P * b, P * b + 128), v("zt", b, 512, 4), A.add)
            else:
                act(v("fk", P * b, P * b + P), by(pool(r, 0, 4 * (P + K)), v("fv", 20 * b, 20 * b + 20)))
        next_lists()
        gather_f(r + 1)
        new_tables(r)

    for h in range(2):
        mm(h, L, "qv", "sv", 0, "qf", "sf", P * R + L * h)
    dma("Y", T.oc[:], cast(v("qf", P * R, P * R + P), dt.uint8), size=512 * P)
    for k in range(4):
        dma("Y", T.osc[4 * k:4 * k + 4, :], T.sf[32 * k:32 * k + 4, P * R:P * R + P], after=[v("sf", P * R, P * R + P)])
    act(v("yt", L, P), v("ps1", 0, L))
    cp(v("yt", 0, L), v("ps0", 0, L))
    dma("S", T.y[:, L:P], v("yt", L, P), size=512 * L)
    dma("Y", T.y[:, 0:L], v("yt", 0, L), size=512 * L)
    dma("S", T.om[:], T.yt[0:128:16, P:2 * P], after=[v("yt", P, 2 * P)])

    last = emit(g, T, ops)
    for s in sorted(last):
        g.wait_ge(T.sem[s], last[s])
    g.wait_ge(T.sem.sent, neng * sum(2 + e for e in EARLY))
